import numpy as np
import ml_dtypes


def mxq(x, axis, fmt="e4m3"):
    dtype, down = {"e4m3": (ml_dtypes.float8_e4m3fn, 7), "e5m2": (ml_dtypes.float8_e5m2, 14)}[fmt]
    v = np.moveaxis(np.asarray(x, np.float32).astype(ml_dtypes.bfloat16).astype(np.float64), axis, -1)
    blocks = v.reshape(v.shape[:-1] + (-1, 32))
    amax = np.abs(blocks).max(-1, keepdims=True)
    byte = np.maximum(np.where(amax > 0, np.frexp(amax)[1] - 1 + 127, 0) - down, 1)
    scale = np.exp2(byte - 127.0)
    codes = (blocks / scale).astype(np.float32).astype(dtype).astype(np.float64)
    return np.moveaxis((codes * scale).reshape(v.shape), -1, axis)


WIDE = False


def mx_kscale(k):
    if not WIDE:
        return np.ones(k)
    levels = np.array([10, -10, 5, -5, 0])
    if k % 512:
        return np.exp2(np.random.permutation(np.resize(levels, k // 32))).repeat(32)
    a = np.empty((k // 512, 16))
    for p in range(k // 512):
        a[p, :8] = np.random.permutation(np.resize(levels, 8))
        for g in range(8):
            far = levels[np.abs(levels - a[p, g]) >= 10]
            a[p, g + 8] = far[np.random.randint(len(far))]
    return np.exp2(a.ravel()).repeat(32)


def f64(x):
    return np.asarray(x).astype(np.float64)


def striped(idx):
    return np.tile(np.asarray(idx).reshape(-1, 16).T, (8, 1)).astype(np.uint16)


def unstriped(offs):
    return offs[:16].T.reshape(-1).astype(np.int64)


O, G, K, T, D, M = 3, 256, 8, 2048, 1024, 128


def setup_inputs():
    n = np.random.standard_normal
    s = mx_kscale(D)[:, None]
    grid = lambda x: np.round(x * 32) / 32
    part = np.random.randint(1, 128 // K, (O, G, K)) / 64.0
    return {
        "xT": (grid(n((D, T))) * s).astype(np.float32),
        "w": (n((O, D, M)) / np.sqrt(O * D) / s).astype(np.float32),
        "part": np.tile(part.reshape(-1), (128, 1)).astype(np.float32),
        "offs": striped(np.random.randint(0, T, O * G * K)),
    }


def reference(xT, w, part, offs):
    x = f64(xT)[:, unstriped(offs)] * f64(part)[:1]
    e = mxq(x.reshape(D, O, G, K).sum(-1), 0, "e4m3")
    wq = mxq(f64(w), 1, "e4m3")
    y = sum(wq[o].T @ e[:, o] for o in range(O))
    return y

@@ -1,0 +1,198 @@
+from contextlib import ExitStack
+
+import concourse.mybir as mybir
+from concourse.masks import make_identity
+
+TAPS, POINTS, CORNERS, COLUMNS, FEATURES, CHANNELS = 3, 256, 8, 2048, 1024, 128
+
+FLOPS = 2 * TAPS * FEATURES * POINTS * CHANNELS
+BYTES = 4 * FEATURES * COLUMNS + 4 * TAPS * FEATURES * CHANNELS + 4 * TAPS * POINTS * CORNERS + 2 * 128 * 384 + 4 * CHANNELS * POINTS
+
+F32 = mybir.dt.float32
+BF16 = mybir.dt.bfloat16
+U32 = mybir.dt.uint32
+U16 = mybir.dt.uint16
+U8 = mybir.dt.uint8
+FP8X4 = mybir.dt.float8_e4m3fn_x4
+COPY = mybir.ActivationFunctionType.Copy
+MULT = mybir.AluOpType.mult
+ADD = mybir.AluOpType.add
+
+P = 128
+HALVES = 2
+UNITS = TAPS * POINTS // P
+ENTRIES = P * CORNERS
+CHUNK = 512
+
+
+def tile_attend_deform_kernel(tc, xT, w, part, offs, out):
+    nc = tc.nc
+    with ExitStack() as ctx:
+        lists = ctx.enter_context(tc.tile_pool(name="lists", bufs=1))
+        keep = ctx.enter_context(tc.tile_pool(name="keep", bufs=1))
+        words_pool = ctx.enter_context(tc.tile_pool(name="words", bufs=3))
+        prod_pool = ctx.enter_context(tc.tile_pool(name="prod", bufs=5))
+        e_pool = ctx.enter_context(tc.tile_pool(name="epool", bufs=8))
+        code_pool = ctx.enter_context(tc.tile_pool(name="codes", bufs=4))
+        lift_psum = ctx.enter_context(tc.psum_pool(name="lift", bufs=4))
+        turn_psum = ctx.enter_context(tc.psum_pool(name="turn", bufs=2))
+        acc_psum = ctx.enter_context(tc.psum_pool(name="accs", bufs=1))
+
+        offsets = lists.tile([P, TAPS * POINTS * CORNERS // 16], U16, name="offsets")
+
+        x_view = xT.rearrange("(s p u e) c -> s u p e c", s=HALVES, p=P, u=2, e=2)
+        raws = {}
+        tables = {}
+
+        def load_window(s, u):
+            for c in range(COLUMNS // CHUNK):
+                raw = keep.tile([P, 2, CHUNK], F32, name=f"raw{s}{u}{c}")
+                nc.sync.dma_start(raw[:], x_view[s, u, :, :, c * CHUNK : (c + 1) * CHUNK])
+                raws[s, u, c] = raw
+
+        def cast_chunk(s, u, c, engine):
+            if c == 0:
+                tables[s, u] = keep.tile([P, COLUMNS, 2], BF16, name=f"table{s}{u}", align_bytes=64)
+            dst = tables[s, u][:, c * CHUNK : (c + 1) * CHUNK, :]
+            src = raws[s, u, c][:].rearrange("p e c -> p c e")
+            if engine == "v":
+                nc.vector.tensor_copy(dst, src)
+            else:
+                nc.scalar.activation(dst, src, COPY)
+
+        load_window(0, 0)
+        nc.sync.dma_start(offsets[:], offs)
+        weights = keep.tile([P, UNITS, CORNERS], F32, name="weights")
+        nc.scalar.dma_start(weights[:], part[0:1, :].rearrange("one (k g j) -> g (one k) j", g=P, j=CORNERS))
+        load_window(0, 1)
+        load_window(1, 0)
+        w_raw = keep.tile([P, TAPS, HALVES, 4, CHANNELS], F32, name="w_raw")
+        w_view = w.rearrange("o (s p t) m -> o s p t m", s=HALVES, t=4)
+        for o in range(TAPS):
+            for s in range(HALVES):
+                nc.sync.dma_start(w_raw[:, o, s, :, :], w_view[o, s])
+        load_window(1, 1)
+
+        identity = keep.tile([P, P], F32, name="identity")
+        make_identity(nc, identity[:])
+
+        units = [(s, u, k) for s in range(HALVES) for u in range(2) for k in range(UNITS)]
+        count = len(units)
+        words = {}
+        addends = {}
+        e_tiles = {}
+
+        def gather(i):
+            s, u, k = units[i]
+            got = words_pool.tile([P, ENTRIES], U32, name="got")
+            nc.vector.tensor_copy(
+                got[:].rearrange("p (q g h) -> p g q h", q=4, h=2),
+                tables[s, u][:].rearrange("p c e -> p (c e)").bitcast(U32).indirect(offsets[:, k * 64 : (k + 1) * 64]),
+            )
+            words[i] = got
+
+        def corners(i):
+            k = units[i][2]
+            late = i >= count - 2
+            prod = prod_pool.tile([P, CORNERS, 256], F32, name="prod")
+            pair = prod_pool.tile([P, 4, 256], F32, name="pair")
+            for b in range(2):
+                bank = lift_psum.tile([P, 4, P], F32, name="bank")
+                for jj in range(4):
+                    src = words[i][:].bitcast(F32).rearrange("p (q g h) -> p q g h", q=4, h=2)[:, 2 * b + jj // 2, :, jj % 2]
+                    nc.tensor.transpose(bank[:, jj, :], src, identity[:])
+                for jj in range(4):
+                    j = 4 * b + jj
+                    src = bank[:, jj, :].bitcast(BF16).rearrange("p (m e) -> p e m", e=2)
+                    scale = weights[:, k, j : j + 1]
+                    if late and b == 1:
+                        nc.vector.scalar_tensor_tensor(
+                            pair[:, jj, :].rearrange("p (e m) -> p e m", e=2),
+                            src,
+                            scale,
+                            prod[:, jj, :].rearrange("p (e m) -> p e m", e=2),
+                            op0=MULT,
+                            op1=ADD,
+                        )
+                    else:
+                        nc.scalar.activation(prod[:, j, :].rearrange("p (e m) -> p e m", e=2), src, COPY, scale=scale)
+            if not late:
+                nc.gpsimd.tensor_tensor(pair[:], prod[:, 0:4, :], prod[:, 4:8, :], ADD)
+            addends[i] = [pair[:, n, :] for n in range(4)]
+            if i % 3 == 1 and i < 20:
+                both = prod_pool.tile([P, 2, 256], F32, name="both")
+                nc.gpsimd.tensor_tensor(both[:], pair[:, 0:2, :], pair[:, 2:4, :], ADD)
+                addends[i] = [both[:, n, :] for n in range(2)]
+
+        w_codes = keep.tile([P, TAPS, HALVES, CHANNELS], U32, name="w_codes", align_bytes=64)
+        w_scales = keep.tile([P, TAPS, HALVES, CHANNELS], U8, name="w_scales", align_bytes=64)
+        w_bf = keep.tile([P, TAPS, HALVES, CHANNELS, 4], BF16, name="w_bf", align_bytes=64)
+
+        def quantize_w(o):
+            for s in range(HALVES):
+                nc.gpsimd.tensor_copy(w_bf[:, o, s, :, :], w_raw[:, o, s, :, :].rearrange("p t m -> p m t"))
+            nc.vector.quantize_mx(
+                out=w_codes[:, o, :, :].rearrange("p s m -> p (s m)").bitcast(FP8X4),
+                scales=w_scales[:, o, :, :].rearrange("p s m -> p (s m)"),
+                in_=w_bf[:, o, :, :, :].rearrange("p s m t -> p (s m t)"),
+            )
+
+        accs = [acc_psum.tile([P, P], F32, name=f"acc{b}") for b in range(2)]
+
+        def finish(i):
+            s, u, k = units[i]
+            o, b = k // 2, k % 2
+            turned = turn_psum.tile([P, 2, P], F32, name="turned")
+            for e in range(2):
+                for n, addend in enumerate(addends[i]):
+                    nc.tensor.matmul(
+                        turned[:, e, :],
+                        addend[:, e * P : (e + 1) * P],
+                        identity[:],
+                        start=(n == 0),
+                        stop=(n == len(addends[i]) - 1),
+                        is_transpose=True,
+                    )
+            if u == 0:
+                e_tiles[s, k] = e_pool.tile([P, P, 4], BF16, name="e_bf", align_bytes=64)
+            e_bf = e_tiles[s, k]
+            dst = e_bf[:, :, 2 * u : 2 * u + 2]
+            src = turned[:].rearrange("p e g -> p g e")
+            if i >= count - 2:
+                nc.vector.tensor_copy(dst, src)
+            else:
+                nc.scalar.activation(dst, src, COPY)
+            if u == 0:
+                return
+            codes = code_pool.tile([P, P], U32, name="codes", align_bytes=64)
+            scales = code_pool.tile([P, P], U8, name="scales", align_bytes=64)
+            nc.vector.quantize_mx(out=codes[:].bitcast(FP8X4), scales=scales[:], in_=e_bf[:].rearrange("p g t -> p (g t)"))
+            nc.tensor.matmul_mx(
+                out=accs[b][:],
+                lhsT=w_codes[:, o, s, :].bitcast(FP8X4),
+                lhsT_scale=w_scales[:, o, s, :],
+                rhs=codes[:].bitcast(FP8X4),
+                rhs_scale=scales[:],
+                start=(s == 0 and o == 0),
+                stop=(s == HALVES - 1 and o == TAPS - 1),
+            )
+            if s == HALVES - 1 and o == TAPS - 1:
+                result = code_pool.tile([P, P], F32, name="result")
+                nc.vector.tensor_copy(result[:], accs[b][:])
+                nc.sync.dma_start(out[:, b * P : (b + 1) * P], result[:])
+
+        for c in range(4):
+            cast_chunk(0, 0, c, "v")
+        gather(0)
+        for i in range(count + 3):
+            if i + 1 < count:
+                gather(i + 1)
+            if i < count:
+                corners(i)
+            for first, s, u, engines in ((0, 0, 1, "svsv"), (1, 1, 0, "sssv"), (5, 1, 1, "ssss")):
+                if first <= i < first + 4:
+                    cast_chunk(s, u, i - first, engines[i - first])
+            if 5 <= i < 5 + TAPS:
+                quantize_w(i - 5)
+            if i >= 3:
+                finish(i - 3)

@@ -23,6 +23,7 @@ HALVES = 2
 UNITS = TAPS * POINTS // P
 ENTRIES = P * CORNERS
 CHUNK = 512
+LATE = 9
 
 
 def tile_attend_deform_kernel(tc, xT, w, part, offs, out):
@@ -30,11 +31,12 @@ def tile_attend_deform_kernel(tc, xT, w, part, offs, out):
     with ExitStack() as ctx:
         lists = ctx.enter_context(tc.tile_pool(name="lists", bufs=1))
         keep = ctx.enter_context(tc.tile_pool(name="keep", bufs=1))
-        words_pool = ctx.enter_context(tc.tile_pool(name="words", bufs=3))
-        prod_pool = ctx.enter_context(tc.tile_pool(name="prod", bufs=5))
-        e_pool = ctx.enter_context(tc.tile_pool(name="epool", bufs=8))
-        code_pool = ctx.enter_context(tc.tile_pool(name="codes", bufs=4))
-        lift_psum = ctx.enter_context(tc.psum_pool(name="lift", bufs=4))
+        words_pool = ctx.enter_context(tc.tile_pool(name="words", bufs=8))
+        prod_pool = ctx.enter_context(tc.tile_pool(name="prod", bufs=4))
+        pair_pool = ctx.enter_context(tc.tile_pool(name="pairs", bufs=3))
+        e_pool = ctx.enter_context(tc.tile_pool(name="epool", bufs=1))
+        code_pool = ctx.enter_context(tc.tile_pool(name="codes", bufs=1))
+        lift_psum = ctx.enter_context(tc.psum_pool(name="lift", bufs=5))
         turn_psum = ctx.enter_context(tc.psum_pool(name="turn", bufs=2))
         acc_psum = ctx.enter_context(tc.psum_pool(name="accs", bufs=1))
 
@@ -66,12 +68,12 @@ def tile_attend_deform_kernel(tc, xT, w, part, offs, out):
         nc.scalar.dma_start(weights[:], part[0:1, :].rearrange("one (k g j) -> g (one k) j", g=P, j=CORNERS))
         load_window(0, 1)
         load_window(1, 0)
+        load_window(1, 1)
         w_raw = keep.tile([P, TAPS, HALVES, 4, CHANNELS], F32, name="w_raw")
         w_view = w.rearrange("o (s p t) m -> o s p t m", s=HALVES, t=4)
         for o in range(TAPS):
             for s in range(HALVES):
                 nc.sync.dma_start(w_raw[:, o, s, :, :], w_view[o, s])
-        load_window(1, 1)
 
         identity = keep.tile([P, P], F32, name="identity")
         make_identity(nc, identity[:])
@@ -93,9 +95,10 @@ def tile_attend_deform_kernel(tc, xT, w, part, offs, out):
 
         def corners(i):
             k = units[i][2]
-            late = i >= count - 2
+            late = i >= count - LATE
             prod = prod_pool.tile([P, CORNERS, 256], F32, name="prod")
-            pair = prod_pool.tile([P, 4, 256], F32, name="pair")
+            if late:
+                pair = pair_pool.tile([P, 4, 256], F32, name="pair")
             for b in range(2):
                 bank = lift_psum.tile([P, 4, P], F32, name="bank")
                 for jj in range(4):
@@ -116,13 +119,10 @@ def tile_attend_deform_kernel(tc, xT, w, part, offs, out):
                         )
                     else:
                         nc.scalar.activation(prod[:, j, :].rearrange("p (e m) -> p e m", e=2), src, COPY, scale=scale)
-            if not late:
-                nc.gpsimd.tensor_tensor(pair[:], prod[:, 0:4, :], prod[:, 4:8, :], ADD)
-            addends[i] = [pair[:, n, :] for n in range(4)]
-            if i % 3 == 1 and i < 20:
-                both = prod_pool.tile([P, 2, 256], F32, name="both")
-                nc.gpsimd.tensor_tensor(both[:], pair[:, 0:2, :], pair[:, 2:4, :], ADD)
-                addends[i] = [both[:, n, :] for n in range(2)]
+            if late:
+                addends[i] = [pair[:, n, :] for n in range(4)]
+            else:
+                addends[i] = [prod[:, n, :] for n in range(CORNERS)]
 
         w_codes = keep.tile([P, TAPS, HALVES, CHANNELS], U32, name="w_codes", align_bytes=64)
         w_scales = keep.tile([P, TAPS, HALVES, CHANNELS], U8, name="w_scales", align_bytes=64)
@@ -130,14 +130,28 @@ def tile_attend_deform_kernel(tc, xT, w, part, offs, out):
 
         def quantize_w(o):
             for s in range(HALVES):
-                nc.gpsimd.tensor_copy(w_bf[:, o, s, :, :], w_raw[:, o, s, :, :].rearrange("p t m -> p m t"))
+                nc.vector.tensor_copy(w_bf[:, o, s, :, :], w_raw[:, o, s, :, :].rearrange("p t m -> p m t"))
             nc.vector.quantize_mx(
                 out=w_codes[:, o, :, :].rearrange("p s m -> p (s m)").bitcast(FP8X4),
                 scales=w_scales[:, o, :, :].rearrange("p s m -> p (s m)"),
                 in_=w_bf[:, o, :, :, :].rearrange("p s m t -> p (s m t)"),
             )
 
-        accs = [acc_psum.tile([P, P], F32, name=f"acc{b}") for b in range(2)]
+        acc = acc_psum.tile([P, POINTS], F32, name="acc")
+        e_codes = {}
+        passes = [(1, 0), (0, 0), (0, 1), (0, 2), (1, 1), (1, 2)]
+
+        def multiply(s, o):
+            codes, scales = e_codes[s, o]
+            nc.tensor.matmul_mx(
+                out=acc[:],
+                lhsT=w_codes[:, o, s, :].bitcast(FP8X4),
+                lhsT_scale=w_scales[:, o, s, :],
+                rhs=codes[:].bitcast(FP8X4),
+                rhs_scale=scales[:],
+                start=((s, o) == passes[0]),
+                stop=((s, o) == passes[-1]),
+            )
 
         def finish(i):
             s, u, k = units[i]
@@ -153,46 +167,43 @@ def tile_attend_deform_kernel(tc, xT, w, part, offs, out):
                         stop=(n == len(addends[i]) - 1),
                         is_transpose=True,
                     )
-            if u == 0:
-                e_tiles[s, k] = e_pool.tile([P, P, 4], BF16, name="e_bf", align_bytes=64)
-            e_bf = e_tiles[s, k]
-            dst = e_bf[:, :, 2 * u : 2 * u + 2]
+            if u == 0 and b == 0:
+                e_tiles[s, o] = e_pool.tile([P, POINTS, 4], BF16, name=f"e_bf{s}{o}", align_bytes=64)
+            e_bf = e_tiles[s, o]
+            dst = e_bf[:, b * P : (b + 1) * P, 2 * u : 2 * u + 2]
             src = turned[:].rearrange("p e g -> p g e")
             if i >= count - 2:
                 nc.vector.tensor_copy(dst, src)
             else:
                 nc.scalar.activation(dst, src, COPY)
-            if u == 0:
+            if u == 0 or b == 0:
                 return
-            codes = code_pool.tile([P, P], U32, name="codes", align_bytes=64)
-            scales = code_pool.tile([P, P], U8, name="scales", align_bytes=64)
+            codes = code_pool.tile([P, POINTS], U32, name=f"codes{s}{o}", align_bytes=64)
+            scales = code_pool.tile([P, POINTS], U8, name=f"scales{s}{o}", align_bytes=64)
             nc.vector.quantize_mx(out=codes[:].bitcast(FP8X4), scales=scales[:], in_=e_bf[:].rearrange("p g t -> p (g t)"))
-            nc.tensor.matmul_mx(
-                out=accs[b][:],
-                lhsT=w_codes[:, o, s, :].bitcast(FP8X4),
-                lhsT_scale=w_scales[:, o, s, :],
-                rhs=codes[:].bitcast(FP8X4),
-                rhs_scale=scales[:],
-                start=(s == 0 and o == 0),
-                stop=(s == HALVES - 1 and o == TAPS - 1),
-            )
-            if s == HALVES - 1 and o == TAPS - 1:
-                result = code_pool.tile([P, P], F32, name="result")
-                nc.vector.tensor_copy(result[:], accs[b][:])
-                nc.sync.dma_start(out[:, b * P : (b + 1) * P], result[:])
+            e_codes[s, o] = (codes, scales)
+            if (s, o) == passes[0]:
+                for done in passes[:4]:
+                    multiply(*done)
+            elif s == 1:
+                multiply(s, o)
+            if (s, o) == passes[-1]:
+                result = code_pool.tile([P, POINTS], F32, name="result")
+                nc.vector.tensor_copy(result[:], acc[:])
+                nc.sync.dma_start(out, result[:])
 
         for c in range(4):
             cast_chunk(0, 0, c, "v")
         gather(0)
-        for i in range(count + 3):
+        for i in range(count + 2):
             if i + 1 < count:
                 gather(i + 1)
             if i < count:
                 corners(i)
-            for first, s, u, engines in ((0, 0, 1, "svsv"), (1, 1, 0, "sssv"), (5, 1, 1, "ssss")):
+            for first, s, u, engines in ((0, 0, 1, "ssss"), (3, 1, 0, "ssss"), (7, 1, 1, "ssss")):
                 if first <= i < first + 4:
                     cast_chunk(s, u, i - first, engines[i - first])
-            if 5 <= i < 5 + TAPS:
-                quantize_w(i - 5)
-            if i >= 3:
-                finish(i - 3)
+            if 12 <= i < 12 + TAPS:
+                quantize_w(i - 12)
+            if i >= 2:
+                finish(i - 2)

@@ -23,7 +23,18 @@ HALVES = 2
 UNITS = TAPS * POINTS // P
 ENTRIES = P * CORNERS
 CHUNK = 512
-LATE = 9
+DW = 2048
+SLOTS = ["got0","got1","got2","got3","raw013","raw012"]
+PRODS = 3
+DAT = 0
+DENG = "vvvv"
+WFIRST = 1
+LAGS = (2,)*12
+TAIL = "ffwab01234c5"
+WAT = 0
+VBANKS = (0,)*10+(2,)*2
+GADDS = (0,)+(2,)*9+(0,0)
+VCOPY = 0
 
 
 def tile_attend_deform_kernel(tc, xT, w, part, offs, out):
@@ -31,14 +42,9 @@ def tile_attend_deform_kernel(tc, xT, w, part, offs, out):
     with ExitStack() as ctx:
         lists = ctx.enter_context(tc.tile_pool(name="lists", bufs=1))
         keep = ctx.enter_context(tc.tile_pool(name="keep", bufs=1))
-        words_pool = ctx.enter_context(tc.tile_pool(name="words", bufs=8))
-        prod_pool = ctx.enter_context(tc.tile_pool(name="prod", bufs=4))
-        pair_pool = ctx.enter_context(tc.tile_pool(name="pairs", bufs=3))
-        e_pool = ctx.enter_context(tc.tile_pool(name="epool", bufs=1))
+        prod_pool = ctx.enter_context(tc.tile_pool(name="prod", bufs=PRODS))
         code_pool = ctx.enter_context(tc.tile_pool(name="codes", bufs=1))
-        lift_psum = ctx.enter_context(tc.psum_pool(name="lift", bufs=5))
-        turn_psum = ctx.enter_context(tc.psum_pool(name="turn", bufs=2))
-        acc_psum = ctx.enter_context(tc.psum_pool(name="accs", bufs=1))
+        psum = ctx.enter_context(tc.psum_pool(name="banks", bufs=1))
 
         offsets = lists.tile([P, TAPS * POINTS * CORNERS // 16], U16, name="offsets")
 
@@ -46,16 +52,19 @@ def tile_attend_deform_kernel(tc, xT, w, part, offs, out):
         raws = {}
         tables = {}
 
+        widths = {(0, 0): CHUNK, (0, 1): CHUNK, (1, 0): CHUNK, (1, 1): DW}
+
         def load_window(s, u):
-            for c in range(COLUMNS // CHUNK):
-                raw = keep.tile([P, 2, CHUNK], F32, name=f"raw{s}{u}{c}")
-                nc.sync.dma_start(raw[:], x_view[s, u, :, :, c * CHUNK : (c + 1) * CHUNK])
+            width = widths[s, u]
+            for c in range(COLUMNS // width):
+                raw = keep.tile([P, 2, width], F32, name=f"raw{s}{u}{c}", align_bytes=64)
+                nc.sync.dma_start(raw[:], x_view[s, u, :, :, c * width : (c + 1) * width])
                 raws[s, u, c] = raw
 
         def cast_chunk(s, u, c, engine):
             if c == 0:
                 tables[s, u] = keep.tile([P, COLUMNS, 2], BF16, name=f"table{s}{u}", align_bytes=64)
-            dst = tables[s, u][:, c * CHUNK : (c + 1) * CHUNK, :]
+            dst = tables[s, u][:, c * widths[s, u] : (c + 1) * widths[s, u], :]
             src = raws[s, u, c][:].rearrange("p e c -> p c e")
             if engine == "v":
                 nc.vector.tensor_copy(dst, src)
@@ -67,143 +76,191 @@ def tile_attend_deform_kernel(tc, xT, w, part, offs, out):
         weights = keep.tile([P, UNITS, CORNERS], F32, name="weights")
         nc.scalar.dma_start(weights[:], part[0:1, :].rearrange("one (k g j) -> g (one k) j", g=P, j=CORNERS))
         load_window(0, 1)
-        load_window(1, 0)
-        load_window(1, 1)
+        if WFIRST < 2:
+            load_window(1, 0)
+        if WFIRST < 1:
+            load_window(1, 1)
         w_raw = keep.tile([P, TAPS, HALVES, 4, CHANNELS], F32, name="w_raw")
         w_view = w.rearrange("o (s p t) m -> o s p t m", s=HALVES, t=4)
         for o in range(TAPS):
             for s in range(HALVES):
                 nc.sync.dma_start(w_raw[:, o, s, :, :], w_view[o, s])
+        if WFIRST >= 2:
+            load_window(1, 0)
+        if WFIRST >= 1:
+            load_window(1, 1)
 
         identity = keep.tile([P, P], F32, name="identity")
         make_identity(nc, identity[:])
 
-        units = [(s, u, k) for s in range(HALVES) for u in range(2) for k in range(UNITS)]
+        units = [(s, k) for s in range(HALVES) for k in range(UNITS)]
         count = len(units)
+        lookups = [(0, 0), (1, 0), (0, 1), (1, 1)] + [(i, u) for i in range(2, count) for u in range(2)]
         words = {}
         addends = {}
-        e_tiles = {}
 
-        def gather(i):
-            s, u, k = units[i]
-            got = words_pool.tile([P, ENTRIES], U32, name="got")
+        slots = SLOTS
+        taken = []
+
+        def next_slot():
+            taken.append(slots[len(taken) % len(slots)])
+            return taken[-1]
+
+        banks = [f"bank{n}" for n in range(8)]
+
+        def next_bank():
+            name = banks[0]
+            banks.remove(name)
+            banks.append(name)
+            return name
+
+        def gather(i, u):
+            s, k = units[i]
+            got = keep.tile([P, ENTRIES], U32, name=next_slot(), align_bytes=64)
             nc.vector.tensor_copy(
                 got[:].rearrange("p (q g h) -> p g q h", q=4, h=2),
                 tables[s, u][:].rearrange("p c e -> p (c e)").bitcast(U32).indirect(offsets[:, k * 64 : (k + 1) * 64]),
             )
-            words[i] = got
+            words[i, u] = got
 
         def corners(i):
-            k = units[i][2]
-            late = i >= count - LATE
-            prod = prod_pool.tile([P, CORNERS, 256], F32, name="prod")
-            if late:
-                pair = pair_pool.tile([P, 4, 256], F32, name="pair")
-            for b in range(2):
-                bank = lift_psum.tile([P, 4, P], F32, name="bank")
-                for jj in range(4):
-                    src = words[i][:].bitcast(F32).rearrange("p (q g h) -> p q g h", q=4, h=2)[:, 2 * b + jj // 2, :, jj % 2]
-                    nc.tensor.transpose(bank[:, jj, :], src, identity[:])
-                for jj in range(4):
-                    j = 4 * b + jj
-                    src = bank[:, jj, :].bitcast(BF16).rearrange("p (m e) -> p e m", e=2)
+            k = units[i][1]
+            prod = prod_pool.tile([P, CORNERS, 2, 2, P], F32, name="prod", align_bytes=64)
+            on_vector = VBANKS[i]
+            order = {0: (0, 1, 2, 3), 1: (0, 1, 2, 3), 2: (0, 2, 1, 3)}[on_vector]
+            for q in order:
+                bank = psum.tile([P, 2, 2, P], F32, name=next_bank())
+                for u in (1, 0):
+                    planes = words[i, u][:].bitcast(F32).rearrange("p (q g h) -> p q g h", q=4, h=2)
+                    for h in range(2):
+                        nc.tensor.transpose(bank[:, h, u, :], planes[:, q, :, h], identity[:])
+                for h in range(2):
+                    j = 2 * q + h
+                    src = bank[:, h, :, :].bitcast(BF16).rearrange("p u (m e) -> p u e m", e=2)
                     scale = weights[:, k, j : j + 1]
-                    if late and b == 1:
-                        nc.vector.scalar_tensor_tensor(
-                            pair[:, jj, :].rearrange("p (e m) -> p e m", e=2),
-                            src,
-                            scale,
-                            prod[:, jj, :].rearrange("p (e m) -> p e m", e=2),
-                            op0=MULT,
-                            op1=ADD,
-                        )
+                    if q >= 4 - on_vector:
+                        onto = j - 2 * (4 - on_vector)
+                        for u in range(2):
+                            nc.vector.scalar_tensor_tensor(
+                                prod[:, onto, u, :, :], src[:, u, :, :], scale, prod[:, onto, u, :, :], op0=MULT, op1=ADD
+                            )
                     else:
-                        nc.scalar.activation(prod[:, j, :].rearrange("p (e m) -> p e m", e=2), src, COPY, scale=scale)
-            if late:
-                addends[i] = [pair[:, n, :] for n in range(4)]
-            else:
-                addends[i] = [prod[:, n, :] for n in range(CORNERS)]
+                        nc.scalar.activation(prod[:, j, :, :, :], src, COPY, scale=scale)
+            flat = prod[:].rearrange("p (q h) u e m -> p q (h u e m)", h=2)
+            left = list(range(4 - on_vector))
+            for n in range(GADDS[i]):
+                first = len(left) - 2 if on_vector else n
+                a, b = left[first], left[first + 1]
+                nc.gpsimd.tensor_tensor(flat[:, a, :], flat[:, a, :], flat[:, b, :], ADD)
+                left.remove(b)
+            addends[i] = [prod[:, 2 * q + h] for q in left for h in range(2)]
 
-        w_codes = keep.tile([P, TAPS, HALVES, CHANNELS], U32, name="w_codes", align_bytes=64)
         w_scales = keep.tile([P, TAPS, HALVES, CHANNELS], U8, name="w_scales", align_bytes=64)
         w_bf = keep.tile([P, TAPS, HALVES, CHANNELS, 4], BF16, name="w_bf", align_bytes=64)
 
-        def quantize_w(o):
+        def cast_w(o):
             for s in range(HALVES):
-                nc.vector.tensor_copy(w_bf[:, o, s, :, :], w_raw[:, o, s, :, :].rearrange("p t m -> p m t"))
+                nc.gpsimd.tensor_copy(w_bf[:, o, s, :, :], w_raw[:, o, s, :, :].rearrange("p t m -> p m t"))
+
+        quantized = {}
+
+        def quantize_w():
+            w_codes = prod_pool.tile([P, TAPS, HALVES, CHANNELS], U32, name="prod", align_bytes=64)
+            for taps in (slice(0, 2), slice(2, 3)):
+                nc.vector.quantize_mx(
+                    out=w_codes[:, taps, :, :].rearrange("p o s m -> p (o s m)").bitcast(FP8X4),
+                    scales=w_scales[:, taps, :, :].rearrange("p o s m -> p (o s m)"),
+                    in_=w_bf[:, taps, :, :, :].rearrange("p o s m t -> p (o s m t)"),
+                )
+            quantized["w"] = w_codes
+
+        passes = [(s, o) for s in range(HALVES) for o in range(TAPS)]
+        e_bf = keep.tile([P, len(passes), POINTS, 4], BF16, name="e_bf", align_bytes=64)
+        e_scales = keep.tile([P, len(passes), POINTS], U8, name="e_scales", align_bytes=64)
+
+
+        def quantize_e(first, last, pool, tag):
+            codes = pool.tile([P, last - first, POINTS], U32, name=tag, align_bytes=64)
+            for n in range(first, last):
+                quantized[n] = codes[:, n - first, :]
             nc.vector.quantize_mx(
-                out=w_codes[:, o, :, :].rearrange("p s m -> p (s m)").bitcast(FP8X4),
-                scales=w_scales[:, o, :, :].rearrange("p s m -> p (s m)"),
-                in_=w_bf[:, o, :, :, :].rearrange("p s m t -> p (s m t)"),
+                out=codes[:].rearrange("p n g -> p (n g)").bitcast(FP8X4),
+                scales=e_scales[:, first:last, :].rearrange("p n g -> p (n g)"),
+                in_=e_bf[:, first:last, :, :].rearrange("p n g t -> p (n g t)"),
             )
 
-        acc = acc_psum.tile([P, POINTS], F32, name="acc")
-        e_codes = {}
-        passes = [(1, 0), (0, 0), (0, 1), (0, 2), (1, 1), (1, 2)]
-
-        def multiply(s, o):
-            codes, scales = e_codes[s, o]
+        def multiply(n):
+            s, o = passes[n]
+            if n == 0:
+                name = next_bank()
+                banks.remove(name)
+                quantized["acc"] = psum.tile([P, POINTS], F32, name=name)
+            acc = quantized["acc"]
             nc.tensor.matmul_mx(
                 out=acc[:],
-                lhsT=w_codes[:, o, s, :].bitcast(FP8X4),
+                lhsT=quantized["w"][:, o, s, :].bitcast(FP8X4),
                 lhsT_scale=w_scales[:, o, s, :],
-                rhs=codes[:].bitcast(FP8X4),
-                rhs_scale=scales[:],
-                start=((s, o) == passes[0]),
-                stop=((s, o) == passes[-1]),
+                rhs=quantized[n].bitcast(FP8X4),
+                rhs_scale=e_scales[:, n, :],
+                start=(n == 0),
+                stop=(n == len(passes) - 1),
             )
 
         def finish(i):
-            s, u, k = units[i]
+            s, k = units[i]
             o, b = k // 2, k % 2
-            turned = turn_psum.tile([P, 2, P], F32, name="turned")
-            for e in range(2):
+            turned = psum.tile([P, 4, P], F32, name=next_bank())
+            for t in range(4):
                 for n, addend in enumerate(addends[i]):
                     nc.tensor.matmul(
-                        turned[:, e, :],
-                        addend[:, e * P : (e + 1) * P],
+                        turned[:, t, :],
+                        addend[:, t // 2, t % 2, :],
                         identity[:],
                         start=(n == 0),
                         stop=(n == len(addends[i]) - 1),
                         is_transpose=True,
                     )
-            if u == 0 and b == 0:
-                e_tiles[s, o] = e_pool.tile([P, POINTS, 4], BF16, name=f"e_bf{s}{o}", align_bytes=64)
-            e_bf = e_tiles[s, o]
-            dst = e_bf[:, b * P : (b + 1) * P, 2 * u : 2 * u + 2]
-            src = turned[:].rearrange("p e g -> p g e")
-            if i >= count - 2:
+            dst = e_bf[:, i // 2, b * P : (b + 1) * P, :]
+            src = turned[:].rearrange("p t g -> p g t")
+            if i >= count - VCOPY:
                 nc.vector.tensor_copy(dst, src)
             else:
                 nc.scalar.activation(dst, src, COPY)
-            if u == 0 or b == 0:
-                return
-            codes = code_pool.tile([P, POINTS], U32, name=f"codes{s}{o}", align_bytes=64)
-            scales = code_pool.tile([P, POINTS], U8, name=f"scales{s}{o}", align_bytes=64)
-            nc.vector.quantize_mx(out=codes[:].bitcast(FP8X4), scales=scales[:], in_=e_bf[:].rearrange("p g t -> p (g t)"))
-            e_codes[s, o] = (codes, scales)
-            if (s, o) == passes[0]:
-                for done in passes[:4]:
-                    multiply(*done)
-            elif s == 1:
-                multiply(s, o)
-            if (s, o) == passes[-1]:
-                result = code_pool.tile([P, POINTS], F32, name="result")
-                nc.vector.tensor_copy(result[:], acc[:])
-                nc.sync.dma_start(out, result[:])
 
         for c in range(4):
             cast_chunk(0, 0, c, "v")
-        gather(0)
-        for i in range(count + 2):
-            if i + 1 < count:
-                gather(i + 1)
-            if i < count:
-                corners(i)
-            for first, s, u, engines in ((0, 0, 1, "ssss"), (3, 1, 0, "ssss"), (7, 1, 1, "ssss")):
-                if first <= i < first + 4:
-                    cast_chunk(s, u, i - first, engines[i - first])
-            if 12 <= i < 12 + TAPS:
-                quantize_w(i - 12)
-            if i >= 2:
-                finish(i - 2)
+        for c in range(4):
+            cast_chunk(0, 1, c, "s")
+        for i, u in lookups[:4]:
+            gather(i, u)
+        for c in range(4):
+            cast_chunk(1, 0, c, "s")
+        finished = 0
+        for i in range(count):
+            corners(i)
+            if DAT <= i < DAT + COLUMNS // DW:
+                cast_chunk(1, 1, i - DAT, DENG[i - DAT])
+            for i2, u in lookups[2 * i + 4 : 2 * i + 6]:
+                gather(i2, u)
+            if WAT <= i < WAT + TAPS:
+                cast_w(i - WAT)
+            while finished <= i - LAGS[i]:
+                finish(finished)
+                finished = finished + 1
+        for step in TAIL:
+            if step == "w":
+                quantize_w()
+            elif step == "a":
+                quantize_e(0, 4, prod_pool, "prod")
+            elif step == "b":
+                quantize_e(4, 5, code_pool, "codes4")
+            elif step == "c":
+                quantize_e(5, 6, code_pool, "codes5")
+            elif step == "f":
+                finish(finished)
+                finished = finished + 1
+            else:
+                multiply(int(step))
+        result = code_pool.tile([P, POINTS], F32, name="result")
+        nc.vector.tensor_copy(result[:], quantized["acc"][:])
+        nc.sync.dma_start(out, result[:])

@@ -23,18 +23,23 @@ HALVES = 2
 UNITS = TAPS * POINTS // P
 ENTRIES = P * CORNERS
 CHUNK = 512
-DW = 2048
-SLOTS = ["got0","got1","got2","got3","raw013","raw012"]
+DW = 512
+SLOTS = ["got0","got1","got2","got3","raw013","raw012","got1","got3","raw013","raw012","got1","got3","raw111"]
 PRODS = 3
 DAT = 0
-DENG = "vvvv"
-WFIRST = 1
-LAGS = (2,)*12
-TAIL = "ffwab01234c5"
+RING = 5
+JMAJOR = 1
+FIRST = {1: "raw103", 2: "raw110"}
+UNTURNED = (0,)
+SPLIT = 1
+DENG = "ssss"
+WFIRST = 0
+LAGS = (2,) * 12
+TAIL = "f f w a b c y x d z"
 WAT = 0
-VBANKS = (0,)*10+(2,)*2
-GADDS = (0,)+(2,)*9+(0,0)
-VCOPY = 0
+VBANKS = (0,) * 8 + (2,) * 4
+GADDS = (0, 0, 3) + (4,) * 5 + (1, 1, 1, 0)
+VCOPY = ()
 
 
 def tile_attend_deform_kernel(tc, xT, w, part, offs, out):
@@ -103,7 +108,8 @@ def tile_attend_deform_kernel(tc, xT, w, part, offs, out):
         taken = []
 
         def next_slot():
-            taken.append(slots[len(taken) % len(slots)])
+            n = len(taken)
+            taken.append(slots[n] if n < len(slots) else taken[n - RING])
             return taken[-1]
 
         banks = [f"bank{n}" for n in range(8)]
@@ -123,37 +129,109 @@ def tile_attend_deform_kernel(tc, xT, w, part, offs, out):
             )
             words[i, u] = got
 
+        def lift(bank_part, i, u, j):
+            planes = words[i, u][:].bitcast(F32).rearrange("p (q g h) -> p q g h", q=4, h=2)
+            nc.tensor.transpose(bank_part, planes[:, j // 2, :, j % 2], identity[:])
+
+        def weigh_and_add(dst, src, scale):
+            nc.vector.scalar_tensor_tensor(dst, src, scale, dst, op0=MULT, op1=ADD)
+
+        spread = {}
+        held = {}
+
+        def spread_weights(k):
+            spread[k] = keep.tile([P, CORNERS, P], F32, name=f"spread{k}")
+            for half in range(2):
+                bank = psum.tile([P, 4, P], F32, name=next_bank())
+                for jj in range(4):
+                    j = 4 * half + jj
+                    nc.tensor.transpose(bank[:, jj, :], weights[:, k, j : j + 1].to_broadcast([P, P]), identity[:])
+                nc.scalar.copy(spread[k][:, 4 * half : 4 * half + 4, :], bank[:])
+
+        def weigh_unturned(i, u):
+            k = units[i][1]
+            if u == 0:
+                held[i] = next_bank()
+                banks.remove(held[i])
+                addends[i] = psum.tile([P, 2, 2, P], F32, name=held[i])
+            values = words[i, u][:].bitcast(BF16).rearrange("p (q g h e) -> p e q h g", q=4, h=2, e=2)
+            for e in range(2):
+                products = keep.tile([P, CORNERS, P], F32, name=f"unturned{e}")
+                nc.gpsimd.tensor_tensor(
+                    products[:].rearrange("p (q h) g -> p q h g", h=2),
+                    values[:, e],
+                    spread[k][:].rearrange("p (q h) g -> p q h g", h=2),
+                    MULT,
+                )
+                for j in range(CORNERS):
+                    nc.tensor.matmul(
+                        addends[i][:, u, e, :], products[:, j, :], identity[:], start=(j == 0), stop=(j == CORNERS - 1), is_transpose=True
+                    )
+
+        def finish_unturned(i):
+            sums = addends[i]
+            rounded = keep.tile([P, 2, P, 2], BF16, name=FIRST[i + 1], align_bytes=64)
+            nc.scalar.activation(rounded[:], sums[:].rearrange("p u e m -> p u m e"), COPY)
+            back = psum.tile([P, 2, P], F32, name=held[i])
+            pairs = rounded[:].rearrange("p u m e -> p u (m e)").bitcast(F32)
+            for u in range(2):
+                nc.tensor.transpose(back[:, u, :], pairs[:, u, :], identity[:])
+            nc.scalar.copy(
+                e_bf[:, i, :, :].rearrange("p g t -> p (g t)").bitcast(F32).rearrange("p (g u) -> p g u", u=2),
+                back[:].rearrange("p u g -> p g u"),
+            )
+            banks.append(held[i])
+
         def corners(i):
             k = units[i][1]
-            prod = prod_pool.tile([P, CORNERS, 2, 2, P], F32, name="prod", align_bytes=64)
+            if i in UNTURNED:
+                for u in range(2):
+                    weigh_unturned(i, u)
+                return
+            if i in FIRST:
+                prod = keep.tile([P, CORNERS, 2, 2, P], F32, name=FIRST[i], align_bytes=64)
+            else:
+                prod = prod_pool.tile([P, CORNERS, 2, 2, P], F32, name="prod", align_bytes=64)
             on_vector = VBANKS[i]
-            order = {0: (0, 1, 2, 3), 1: (0, 1, 2, 3), 2: (0, 2, 1, 3)}[on_vector]
+            left = list(range(CORNERS - 2 * on_vector))
+            addends[i] = (prod, left)
+            if i >= count - SPLIT:
+                for u in range(2):
+                    for half in range(2):
+                        bank = psum.tile([P, 4, P], F32, name=next_bank())
+                        for jj in range(4):
+                            lift(bank[:, jj, :], i, u, 4 * half + jj)
+                        for jj in range(4):
+                            src = bank[:, jj, :].bitcast(BF16).rearrange("p (m e) -> p e m", e=2)
+                            scale = weights[:, k, 4 * half + jj : 4 * half + jj + 1]
+                            if half == 0:
+                                nc.scalar.activation(prod[:, jj, u, :, :], src, COPY, scale=scale)
+                            else:
+                                weigh_and_add(prod[:, jj, u, :, :], src, scale)
+                return
+            order = (0, 2, 1, 3) if on_vector == 2 else (0, 1, 2, 3)
+            added = 0
             for q in order:
                 bank = psum.tile([P, 2, 2, P], F32, name=next_bank())
                 for u in (1, 0):
-                    planes = words[i, u][:].bitcast(F32).rearrange("p (q g h) -> p q g h", q=4, h=2)
                     for h in range(2):
-                        nc.tensor.transpose(bank[:, h, u, :], planes[:, q, :, h], identity[:])
+                        lift(bank[:, h, u, :], i, u, 2 * q + h)
                 for h in range(2):
                     j = 2 * q + h
                     src = bank[:, h, :, :].bitcast(BF16).rearrange("p u (m e) -> p u e m", e=2)
                     scale = weights[:, k, j : j + 1]
                     if q >= 4 - on_vector:
-                        onto = j - 2 * (4 - on_vector)
+                        onto = j % (2 * (4 - on_vector))
                         for u in range(2):
-                            nc.vector.scalar_tensor_tensor(
-                                prod[:, onto, u, :, :], src[:, u, :, :], scale, prod[:, onto, u, :, :], op0=MULT, op1=ADD
-                            )
+                            weigh_and_add(prod[:, onto, u, :, :], src[:, u, :, :], scale)
                     else:
                         nc.scalar.activation(prod[:, j, :, :, :], src, COPY, scale=scale)
-            flat = prod[:].rearrange("p (q h) u e m -> p q (h u e m)", h=2)
-            left = list(range(4 - on_vector))
-            for n in range(GADDS[i]):
-                first = len(left) - 2 if on_vector else n
-                a, b = left[first], left[first + 1]
-                nc.gpsimd.tensor_tensor(flat[:, a, :], flat[:, a, :], flat[:, b, :], ADD)
-                left.remove(b)
-            addends[i] = [prod[:, 2 * q + h] for q in left for h in range(2)]
+                done = q - (4 - on_vector) if q >= 4 - on_vector else q
+                if on_vector < 3 and (q >= 4 - on_vector or q >= on_vector) and added < GADDS[i]:
+                    flat = prod[:].rearrange("p j u e m -> p j (u e m)")
+                    nc.gpsimd.tensor_tensor(flat[:, 2 * done, :], flat[:, 2 * done, :], flat[:, 2 * done + 1, :], ADD)
+                    left.remove(2 * done + 1)
+                    added = added + 1
 
         w_scales = keep.tile([P, TAPS, HALVES, CHANNELS], U8, name="w_scales", align_bytes=64)
         w_bf = keep.tile([P, TAPS, HALVES, CHANNELS, 4], BF16, name="w_bf", align_bytes=64)
@@ -175,12 +253,12 @@ def tile_attend_deform_kernel(tc, xT, w, part, offs, out):
             quantized["w"] = w_codes
 
         passes = [(s, o) for s in range(HALVES) for o in range(TAPS)]
-        e_bf = keep.tile([P, len(passes), POINTS, 4], BF16, name="e_bf", align_bytes=64)
-        e_scales = keep.tile([P, len(passes), POINTS], U8, name="e_scales", align_bytes=64)
+        e_bf = keep.tile([P, count, P, 4], BF16, name="e_bf", align_bytes=64)
+        e_scales = keep.tile([P, count, P], U8, name="e_scales", align_bytes=64)
 
 
         def quantize_e(first, last, pool, tag):
-            codes = pool.tile([P, last - first, POINTS], U32, name=tag, align_bytes=64)
+            codes = pool.tile([P, last - first, P], U32, name=tag, align_bytes=64)
             for n in range(first, last):
                 quantized[n] = codes[:, n - first, :]
             nc.vector.quantize_mx(
@@ -189,44 +267,54 @@ def tile_attend_deform_kernel(tc, xT, w, part, offs, out):
                 in_=e_bf[:, first:last, :, :].rearrange("p n g t -> p (n g t)"),
             )
 
-        def multiply(n):
+        def multiply(n, b):
             s, o = passes[n]
             if n == 0:
                 name = next_bank()
                 banks.remove(name)
-                quantized["acc"] = psum.tile([P, POINTS], F32, name=name)
-            acc = quantized["acc"]
+                quantized["acc", b] = psum.tile([P, P], F32, name=name)
+            acc = quantized["acc", b]
             nc.tensor.matmul_mx(
                 out=acc[:],
                 lhsT=quantized["w"][:, o, s, :].bitcast(FP8X4),
                 lhsT_scale=w_scales[:, o, s, :],
-                rhs=quantized[n].bitcast(FP8X4),
-                rhs_scale=e_scales[:, n, :],
+                rhs=quantized[2 * n + b].bitcast(FP8X4),
+                rhs_scale=e_scales[:, 2 * n + b, :],
                 start=(n == 0),
                 stop=(n == len(passes) - 1),
             )
 
         def finish(i):
+            if i in UNTURNED:
+                return
             s, k = units[i]
             o, b = k // 2, k % 2
+            prod, left = addends[i]
             turned = psum.tile([P, 4, P], F32, name=next_bank())
-            for t in range(4):
-                for n, addend in enumerate(addends[i]):
-                    nc.tensor.matmul(
-                        turned[:, t, :],
-                        addend[:, t // 2, t % 2, :],
-                        identity[:],
-                        start=(n == 0),
-                        stop=(n == len(addends[i]) - 1),
-                        is_transpose=True,
-                    )
-            dst = e_bf[:, i // 2, b * P : (b + 1) * P, :]
+            if i >= count - JMAJOR:
+                if i >= count - SPLIT:
+                    steps = [(2 * u + e, j) for u in range(2) for j in left for e in range(2)]
+                else:
+                    steps = [(t, j) for j in left for t in range(4)]
+                flags = [(n == 0, n == len(steps) - 1) for n in range(len(steps))]
+            else:
+                steps = [(t, j) for t in range(4) for j in left]
+                flags = [(j == left[0], j == left[-1]) for t, j in steps]
+            for (t, j), (start, stop) in zip(steps, flags):
+                nc.tensor.matmul(
+                    turned[:, t, :], prod[:, j, t // 2, t % 2, :], identity[:], start=start, stop=stop, is_transpose=True
+                )
+            dst = e_bf[:, i, :, :]
             src = turned[:].rearrange("p t g -> p g t")
-            if i >= count - VCOPY:
+            if i in VCOPY:
                 nc.vector.tensor_copy(dst, src)
             else:
                 nc.scalar.activation(dst, src, COPY)
+            if i - 1 in UNTURNED:
+                finish_unturned(i - 1)
 
+        for i in UNTURNED:
+            spread_weights(units[i][1])
         for c in range(4):
             cast_chunk(0, 0, c, "v")
         for c in range(4):
@@ -247,20 +335,33 @@ def tile_attend_deform_kernel(tc, xT, w, part, offs, out):
             while finished <= i - LAGS[i]:
                 finish(finished)
                 finished = finished + 1
-        for step in TAIL:
+
+        def store(b):
+            result = code_pool.tile([P, P], F32, name=f"result{b}")
+            nc.vector.tensor_copy(result[:], quantized["acc", b][:])
+            nc.sync.dma_start(out[:, b * P : (b + 1) * P], result[:])
+
+        for step in TAIL.split():
             if step == "w":
                 quantize_w()
             elif step == "a":
-                quantize_e(0, 4, prod_pool, "prod")
+                quantize_e(0, 8, prod_pool, "prod")
             elif step == "b":
-                quantize_e(4, 5, code_pool, "codes4")
+                quantize_e(8, 10, code_pool, "codes4")
             elif step == "c":
-                quantize_e(5, 6, code_pool, "codes5")
+                quantize_e(10, 11, code_pool, "codes5")
+            elif step == "d":
+                quantize_e(11, 12, code_pool, "codes6")
             elif step == "f":
                 finish(finished)
                 finished = finished + 1
+            elif step == "x":
+                for n in range(6):
+                    multiply(n, 0)
+                store(0)
+            elif step == "y":
+                for n in range(5):
+                    multiply(n, 1)
             else:
-                multiply(int(step))
-        result = code_pool.tile([P, POINTS], F32, name="result")
-        nc.vector.tensor_copy(result[:], quantized["acc"][:])
-        nc.sync.dma_start(out, result[:])
+                multiply(5, 1)
+                store(1)

@@ -24,10 +24,12 @@ UNITS = TAPS * POINTS // P
 ENTRIES = P * CORNERS
 CHUNK = 512
 DW = 512
-SLOTS = ["got0","got1","got2","got3","raw013","raw012","got1","got3","raw013","raw012","got1","got3","raw111"]
+SLOTS = ["got0","got1","got2","got3","raw013","raw012","got1","got3","raw013","raw012","got1","got3","raw111","raw112"]
 PRODS = 3
 DAT = 0
-RING = 5
+PLACE = 4
+TB = 2
+RING = 6
 JMAJOR = 1
 FIRST = {1: "raw103", 2: "raw110"}
 UNTURNED = (0,)
@@ -37,9 +39,9 @@ WFIRST = 0
 LAGS = (2,) * 12
 TAIL = "f f w a b c y x d z"
 WAT = 0
-VBANKS = (0,) * 8 + (2,) * 4
-GADDS = (0, 0, 3) + (4,) * 5 + (1, 1, 1, 0)
-VCOPY = ()
+VBANKS = (0,) * 9 + (3, 2, 2)
+GADDS = ("", "", "a") + ("ab",) * 5 + ("ad", "", "", "")
+VCOPY = range(1, 4)
 
 
 def tile_attend_deform_kernel(tc, xT, w, part, offs, out):
@@ -112,7 +114,7 @@ def tile_attend_deform_kernel(tc, xT, w, part, offs, out):
             taken.append(slots[n] if n < len(slots) else taken[n - RING])
             return taken[-1]
 
-        banks = [f"bank{n}" for n in range(8)]
+        banks = [f"bank{n}" for n in range(8 - TB)]
 
         def next_bank():
             name = banks[0]
@@ -176,6 +178,10 @@ def tile_attend_deform_kernel(tc, xT, w, part, offs, out):
             pairs = rounded[:].rearrange("p u m e -> p u (m e)").bitcast(F32)
             for u in range(2):
                 nc.tensor.transpose(back[:, u, :], pairs[:, u, :], identity[:])
+            addends[i] = back
+
+        def place_unturned(i):
+            back = addends[i]
             nc.scalar.copy(
                 e_bf[:, i, :, :].rearrange("p g t -> p (g t)").bitcast(F32).rearrange("p (g u) -> p g u", u=2),
                 back[:].rearrange("p u g -> p g u"),
@@ -210,7 +216,6 @@ def tile_attend_deform_kernel(tc, xT, w, part, offs, out):
                                 weigh_and_add(prod[:, jj, u, :, :], src, scale)
                 return
             order = (0, 2, 1, 3) if on_vector == 2 else (0, 1, 2, 3)
-            added = 0
             for q in order:
                 bank = psum.tile([P, 2, 2, P], F32, name=next_bank())
                 for u in (1, 0):
@@ -226,19 +231,19 @@ def tile_attend_deform_kernel(tc, xT, w, part, offs, out):
                             weigh_and_add(prod[:, onto, u, :, :], src[:, u, :, :], scale)
                     else:
                         nc.scalar.activation(prod[:, j, :, :, :], src, COPY, scale=scale)
-                done = q - (4 - on_vector) if q >= 4 - on_vector else q
-                if on_vector < 3 and (q >= 4 - on_vector or q >= on_vector) and added < GADDS[i]:
-                    flat = prod[:].rearrange("p j u e m -> p j (u e m)")
-                    nc.gpsimd.tensor_tensor(flat[:, 2 * done, :], flat[:, 2 * done, :], flat[:, 2 * done + 1, :], ADD)
-                    left.remove(2 * done + 1)
-                    added = added + 1
+                flat = prod[:].rearrange("p j u e m -> p (j u e m)")
+                for name, after, first, second, n in (("a", 1, 0, 2, 2), ("b", 3, 4, 6, 2), ("c", 0, 0, 1, 1), ("d", 2, 4, 5, 1), ("e", 3, 6, 7, 1), ("f", 1, 2, 3, 1)):
+                    if name in GADDS[i] and q == after:
+                        dst = flat[:, 512 * first : 512 * (first + n)]
+                        nc.gpsimd.tensor_tensor(dst, dst, flat[:, 512 * second : 512 * (second + n)], ADD)
+                        for j in range(second, second + n):
+                            left.remove(j)
 
         w_scales = keep.tile([P, TAPS, HALVES, CHANNELS], U8, name="w_scales", align_bytes=64)
         w_bf = keep.tile([P, TAPS, HALVES, CHANNELS, 4], BF16, name="w_bf", align_bytes=64)
 
         def cast_w(o):
-            for s in range(HALVES):
-                nc.gpsimd.tensor_copy(w_bf[:, o, s, :, :], w_raw[:, o, s, :, :].rearrange("p t m -> p m t"))
+            nc.gpsimd.tensor_copy(w_bf[:, o, :, :, :], w_raw[:, o, :, :, :].rearrange("p s t m -> p s m t"))
 
         quantized = {}
 
@@ -290,7 +295,7 @@ def tile_attend_deform_kernel(tc, xT, w, part, offs, out):
             s, k = units[i]
             o, b = k // 2, k % 2
             prod, left = addends[i]
-            turned = psum.tile([P, 4, P], F32, name=next_bank())
+            turned = psum.tile([P, 4, P], F32, name=(f"turn{i % TB}" if TB else next_bank()))
             if i >= count - JMAJOR:
                 if i >= count - SPLIT:
                     steps = [(2 * u + e, j) for u in range(2) for j in left for e in range(2)]
@@ -328,6 +333,8 @@ def tile_attend_deform_kernel(tc, xT, w, part, offs, out):
             corners(i)
             if DAT <= i < DAT + COLUMNS // DW:
                 cast_chunk(1, 1, i - DAT, DENG[i - DAT])
+            if i - PLACE in UNTURNED:
+                place_unturned(i - PLACE)
             for i2, u in lookups[2 * i + 4 : 2 * i + 6]:
                 gather(i2, u)
             if WAT <= i < WAT + TAPS:

@@ -19,29 +19,18 @@ MULT = mybir.AluOpType.mult
 ADD = mybir.AluOpType.add
 
 P = 128
-HALVES = 2
-UNITS = TAPS * POINTS // P
+PASSES = FEATURES // 512
+BLOCKS = TAPS * POINTS // P
+UNITS = PASSES * BLOCKS
+LAST = UNITS - 1
 ENTRIES = P * CORNERS
-CHUNK = 512
-DW = 512
-SLOTS = ["got0","got1","got2","got3","raw013","raw012","got1","got3","raw013","raw012","got1","got3","raw111","raw112"]
-PRODS = 3
-DAT = 0
-PLACE = 4
-TB = 2
-RING = 6
-JMAJOR = 1
-FIRST = {1: "raw103", 2: "raw110"}
-UNTURNED = (0,)
-SPLIT = 1
-DENG = "ssss"
-WFIRST = 0
-LAGS = (2,) * 12
-TAIL = "f f w a b c y x d z"
-WAT = 0
-VBANKS = (0,) * 9 + (3, 2, 2)
-GADDS = ("", "", "a") + ("ab",) * 5 + ("ad", "", "", "")
-VCOPY = range(1, 4)
+LIST_COLUMNS = ENTRIES // 16
+CHUNKS = 4
+CHUNK = COLUMNS // CHUNKS
+CORNER = 4 * P
+HELPED = 3
+SUM_LAG = 2
+SUM_BANKS = 2
 
 
 def tile_attend_deform_kernel(tc, xT, w, part, offs, out):
@@ -49,72 +38,73 @@ def tile_attend_deform_kernel(tc, xT, w, part, offs, out):
     with ExitStack() as ctx:
         lists = ctx.enter_context(tc.tile_pool(name="lists", bufs=1))
         keep = ctx.enter_context(tc.tile_pool(name="keep", bufs=1))
-        prod_pool = ctx.enter_context(tc.tile_pool(name="prod", bufs=PRODS))
+        prod_pool = ctx.enter_context(tc.tile_pool(name="prod", bufs=SUM_LAG + 1))
         code_pool = ctx.enter_context(tc.tile_pool(name="codes", bufs=1))
         psum = ctx.enter_context(tc.psum_pool(name="banks", bufs=1))
 
-        offsets = lists.tile([P, TAPS * POINTS * CORNERS // 16], U16, name="offsets")
-
-        x_view = xT.rearrange("(s p u e) c -> s u p e c", s=HALVES, p=P, u=2, e=2)
-        raws = {}
+        offsets = lists.tile([P, BLOCKS * LIST_COLUMNS], U16, name="offsets")
+        x_view = xT.rearrange("(s p u e) c -> s u p e c", s=PASSES, p=P, u=2, e=2)
+        staged = {}
         tables = {}
 
-        widths = {(0, 0): CHUNK, (0, 1): CHUNK, (1, 0): CHUNK, (1, 1): DW}
+        def staging_name(s, u, c):
+            return f"staged{s}{u}{c}"
 
         def load_window(s, u):
-            width = widths[s, u]
-            for c in range(COLUMNS // width):
-                raw = keep.tile([P, 2, width], F32, name=f"raw{s}{u}{c}", align_bytes=64)
-                nc.sync.dma_start(raw[:], x_view[s, u, :, :, c * width : (c + 1) * width])
-                raws[s, u, c] = raw
+            for c in range(CHUNKS):
+                raw = keep.tile([P, 2, CHUNK], F32, name=staging_name(s, u, c), align_bytes=64)
+                nc.sync.dma_start(raw[:], x_view[s, u, :, :, c * CHUNK : (c + 1) * CHUNK])
+                staged[s, u, c] = raw
 
-        def cast_chunk(s, u, c, engine):
+        def cast_chunk(s, u, c):
             if c == 0:
                 tables[s, u] = keep.tile([P, COLUMNS, 2], BF16, name=f"table{s}{u}", align_bytes=64)
-            dst = tables[s, u][:, c * widths[s, u] : (c + 1) * widths[s, u], :]
-            src = raws[s, u, c][:].rearrange("p e c -> p c e")
-            if engine == "v":
+            dst = tables[s, u][:, c * CHUNK : (c + 1) * CHUNK, :]
+            src = staged[s, u, c][:].rearrange("p e c -> p c e")
+            if (s, u) == (0, 0):
                 nc.vector.tensor_copy(dst, src)
             else:
                 nc.scalar.activation(dst, src, COPY)
 
         load_window(0, 0)
         nc.sync.dma_start(offsets[:], offs)
-        weights = keep.tile([P, UNITS, CORNERS], F32, name="weights")
+        weights = keep.tile([P, BLOCKS, CORNERS], F32, name="weights")
         nc.scalar.dma_start(weights[:], part[0:1, :].rearrange("one (k g j) -> g (one k) j", g=P, j=CORNERS))
         load_window(0, 1)
-        if WFIRST < 2:
-            load_window(1, 0)
-        if WFIRST < 1:
-            load_window(1, 1)
-        w_raw = keep.tile([P, TAPS, HALVES, 4, CHANNELS], F32, name="w_raw")
-        w_view = w.rearrange("o (s p t) m -> o s p t m", s=HALVES, t=4)
+        load_window(1, 0)
+        load_window(1, 1)
+        w_raw = keep.tile([P, TAPS, PASSES, 4, CHANNELS], F32, name="w_raw")
+        w_view = w.rearrange("o (s p t) m -> o s p t m", s=PASSES, t=4)
         for o in range(TAPS):
-            for s in range(HALVES):
+            for s in range(PASSES):
                 nc.sync.dma_start(w_raw[:, o, s, :, :], w_view[o, s])
-        if WFIRST >= 2:
-            load_window(1, 0)
-        if WFIRST >= 1:
-            load_window(1, 1)
 
         identity = keep.tile([P, P], F32, name="identity")
         make_identity(nc, identity[:])
 
-        units = [(s, k) for s in range(HALVES) for k in range(UNITS)]
-        count = len(units)
-        lookups = [(0, 0), (1, 0), (0, 1), (1, 1)] + [(i, u) for i in range(2, count) for u in range(2)]
         words = {}
-        addends = {}
+        word_names = {}
 
-        slots = SLOTS
-        taken = []
+        def gather(i, u):
+            if i < 2:
+                name = f"words{i}{u}"
+            elif i == 2:
+                name = staging_name(0, 1, CHUNKS - 1 - u)
+            elif i == BLOCKS:
+                name = staging_name(1, 1, CHUNKS - 2 + u)
+            else:
+                name = word_names[i - (2 if i < BLOCKS else 3), u]
+            word_names[i, u] = name
+            s, k = divmod(i, BLOCKS)
+            got = keep.tile([P, ENTRIES], U32, name=name, align_bytes=64)
+            window = tables[s, u][:].rearrange("p c e -> p (c e)").bitcast(U32)
+            nc.vector.tensor_copy(
+                got[:].rearrange("p (q g h) -> p g q h", q=4, h=2),
+                window.indirect(offsets[:, k * LIST_COLUMNS : (k + 1) * LIST_COLUMNS]),
+            )
+            words[i, u] = got
 
-        def next_slot():
-            n = len(taken)
-            taken.append(slots[n] if n < len(slots) else taken[n - RING])
-            return taken[-1]
-
-        banks = [f"bank{n}" for n in range(8 - TB)]
+        banks = [f"bank{n}" for n in range(8 - SUM_BANKS)]
 
         def next_bank():
             name = banks[0]
@@ -122,253 +112,221 @@ def tile_attend_deform_kernel(tc, xT, w, part, offs, out):
             banks.append(name)
             return name
 
-        def gather(i, u):
-            s, k = units[i]
-            got = keep.tile([P, ENTRIES], U32, name=next_slot(), align_bytes=64)
-            nc.vector.tensor_copy(
-                got[:].rearrange("p (q g h) -> p g q h", q=4, h=2),
-                tables[s, u][:].rearrange("p c e -> p (c e)").bitcast(U32).indirect(offsets[:, k * 64 : (k + 1) * 64]),
-            )
-            words[i, u] = got
+        def held_bank():
+            name = next_bank()
+            banks.remove(name)
+            return name
 
-        def lift(bank_part, i, u, j):
-            planes = words[i, u][:].bitcast(F32).rearrange("p (q g h) -> p q g h", q=4, h=2)
-            nc.tensor.transpose(bank_part, planes[:, j // 2, :, j % 2], identity[:])
+        def add_turned(dst, src, start, stop):
+            nc.tensor.matmul(dst, src, identity[:], start=start, stop=stop, is_transpose=True)
 
-        def weigh_and_add(dst, src, scale):
-            nc.vector.scalar_tensor_tensor(dst, src, scale, dst, op0=MULT, op1=ADD)
+        e_bf = keep.tile([P, UNITS, P, 4], BF16, name="e_bf", align_bytes=64)
+        e_scales = keep.tile([P, UNITS, P], U8, name="e_scales", align_bytes=64)
 
-        spread = {}
-        held = {}
+        first = {}
 
-        def spread_weights(k):
-            spread[k] = keep.tile([P, CORNERS, P], F32, name=f"spread{k}")
+        def spread_weights():
+            first["spread"] = keep.tile([P, CORNERS, P], F32, name="spread")
             for half in range(2):
                 bank = psum.tile([P, 4, P], F32, name=next_bank())
                 for jj in range(4):
                     j = 4 * half + jj
-                    nc.tensor.transpose(bank[:, jj, :], weights[:, k, j : j + 1].to_broadcast([P, P]), identity[:])
-                nc.scalar.copy(spread[k][:, 4 * half : 4 * half + 4, :], bank[:])
+                    nc.tensor.transpose(bank[:, jj, :], weights[:, 0, j : j + 1].to_broadcast([P, P]), identity[:])
+                nc.scalar.copy(first["spread"][:, 4 * half : 4 * half + 4, :], bank[:])
 
-        def weigh_unturned(i, u):
-            k = units[i][1]
-            if u == 0:
-                held[i] = next_bank()
-                banks.remove(held[i])
-                addends[i] = psum.tile([P, 2, 2, P], F32, name=held[i])
-            values = words[i, u][:].bitcast(BF16).rearrange("p (q g h e) -> p e q h g", q=4, h=2, e=2)
-            for e in range(2):
-                products = keep.tile([P, CORNERS, P], F32, name=f"unturned{e}")
-                nc.gpsimd.tensor_tensor(
-                    products[:].rearrange("p (q h) g -> p q h g", h=2),
-                    values[:, e],
-                    spread[k][:].rearrange("p (q h) g -> p q h g", h=2),
-                    MULT,
-                )
-                for j in range(CORNERS):
-                    nc.tensor.matmul(
-                        addends[i][:, u, e, :], products[:, j, :], identity[:], start=(j == 0), stop=(j == CORNERS - 1), is_transpose=True
-                    )
-
-        def finish_unturned(i):
-            sums = addends[i]
-            rounded = keep.tile([P, 2, P, 2], BF16, name=FIRST[i + 1], align_bytes=64)
-            nc.scalar.activation(rounded[:], sums[:].rearrange("p u e m -> p u m e"), COPY)
-            back = psum.tile([P, 2, P], F32, name=held[i])
-            pairs = rounded[:].rearrange("p u m e -> p u (m e)").bitcast(F32)
+        def weigh_first():
+            first["bank"] = held_bank()
+            first["sums"] = psum.tile([P, 2, 2, P], F32, name=first["bank"])
             for u in range(2):
-                nc.tensor.transpose(back[:, u, :], pairs[:, u, :], identity[:])
-            addends[i] = back
+                values = words[0, u][:].bitcast(BF16).rearrange("p (q g h e) -> p e q h g", q=4, h=2, e=2)
+                for e in range(2):
+                    products = keep.tile([P, CORNERS, P], F32, name=f"first_products{e}")
+                    nc.gpsimd.tensor_tensor(
+                        products[:].rearrange("p (q h) g -> p q h g", h=2),
+                        values[:, e],
+                        first["spread"][:].rearrange("p (q h) g -> p q h g", h=2),
+                        MULT,
+                    )
+                    for j in range(CORNERS):
+                        add_turned(first["sums"][:, u, e, :], products[:, j, :], j == 0, j == CORNERS - 1)
 
-        def place_unturned(i):
-            back = addends[i]
+        def round_first():
+            rounded = keep.tile([P, 2, P, 2], BF16, name=staging_name(1, 1, 0), align_bytes=64)
+            nc.scalar.activation(rounded[:], first["sums"][:].rearrange("g u e p -> g u p e"), COPY)
+            first["back"] = psum.tile([P, 2, P], F32, name=first["bank"])
+            pairs = rounded[:].rearrange("g u p e -> g u (p e)").bitcast(F32)
+            for u in range(2):
+                nc.tensor.transpose(first["back"][:, u, :], pairs[:, u, :], identity[:])
+
+        def place_first():
             nc.scalar.copy(
-                e_bf[:, i, :, :].rearrange("p g t -> p (g t)").bitcast(F32).rearrange("p (g u) -> p g u", u=2),
-                back[:].rearrange("p u g -> p g u"),
+                e_bf[:, 0, :, :].rearrange("p g t -> p (g t)").bitcast(F32).rearrange("p (g u) -> p g u", u=2),
+                first["back"][:].rearrange("p u g -> p g u"),
             )
-            banks.append(held[i])
+            banks.append(first["bank"])
 
-        def corners(i):
-            k = units[i][1]
-            if i in UNTURNED:
-                for u in range(2):
-                    weigh_unturned(i, u)
-                return
-            if i in FIRST:
-                prod = keep.tile([P, CORNERS, 2, 2, P], F32, name=FIRST[i], align_bytes=64)
+        addends = {}
+
+        def lift(dst, i, u, j):
+            planes = words[i, u][:].bitcast(F32).rearrange("p (q g h) -> p q g h", q=4, h=2)
+            nc.tensor.transpose(dst, planes[:, j // 2, :, j % 2], identity[:])
+
+        def weigh_and_add(dst, src, scale):
+            nc.vector.scalar_tensor_tensor(dst, src, scale, dst, op0=MULT, op1=ADD)
+
+        def weigh(i):
+            k = i % BLOCKS
+            helped = i >= UNITS - HELPED
+            if i <= 2:
+                prod = keep.tile([P, CORNERS, 2, 2, P], F32, name=staging_name(1, 1, i - 1), align_bytes=64)
             else:
                 prod = prod_pool.tile([P, CORNERS, 2, 2, P], F32, name="prod", align_bytes=64)
-            on_vector = VBANKS[i]
-            left = list(range(CORNERS - 2 * on_vector))
+            flat = prod[:].rearrange("g j u e p -> g (j u e p)")
+            left = list(range(4 if helped else CORNERS))
             addends[i] = (prod, left)
-            if i >= count - SPLIT:
+
+            def add_corners(onto, taken, n):
+                dst = flat[:, CORNER * onto : CORNER * (onto + n)]
+                nc.gpsimd.tensor_tensor(dst, dst, flat[:, CORNER * taken : CORNER * (taken + n)], ADD)
+                for j in range(taken, taken + n):
+                    left.remove(j)
+
+            if i == LAST:
                 for u in range(2):
                     for half in range(2):
                         bank = psum.tile([P, 4, P], F32, name=next_bank())
                         for jj in range(4):
                             lift(bank[:, jj, :], i, u, 4 * half + jj)
                         for jj in range(4):
-                            src = bank[:, jj, :].bitcast(BF16).rearrange("p (m e) -> p e m", e=2)
+                            src = bank[:, jj, :].bitcast(BF16).rearrange("g (p e) -> g e p", e=2)
                             scale = weights[:, k, 4 * half + jj : 4 * half + jj + 1]
                             if half == 0:
                                 nc.scalar.activation(prod[:, jj, u, :, :], src, COPY, scale=scale)
                             else:
                                 weigh_and_add(prod[:, jj, u, :, :], src, scale)
                 return
-            order = (0, 2, 1, 3) if on_vector == 2 else (0, 1, 2, 3)
-            for q in order:
+            for q in (0, 2, 1, 3) if helped else range(4):
                 bank = psum.tile([P, 2, 2, P], F32, name=next_bank())
                 for u in (1, 0):
                     for h in range(2):
                         lift(bank[:, h, u, :], i, u, 2 * q + h)
                 for h in range(2):
                     j = 2 * q + h
-                    src = bank[:, h, :, :].bitcast(BF16).rearrange("p u (m e) -> p u e m", e=2)
+                    src = bank[:, h, :, :].bitcast(BF16).rearrange("g u (p e) -> g u e p", e=2)
                     scale = weights[:, k, j : j + 1]
-                    if q >= 4 - on_vector:
-                        onto = j % (2 * (4 - on_vector))
+                    if helped and q >= 2:
                         for u in range(2):
-                            weigh_and_add(prod[:, onto, u, :, :], src[:, u, :, :], scale)
+                            weigh_and_add(prod[:, j - 4, u, :, :], src[:, u, :, :], scale)
                     else:
                         nc.scalar.activation(prod[:, j, :, :, :], src, COPY, scale=scale)
-                flat = prod[:].rearrange("p j u e m -> p (j u e m)")
-                for name, after, first, second, n in (("a", 1, 0, 2, 2), ("b", 3, 4, 6, 2), ("c", 0, 0, 1, 1), ("d", 2, 4, 5, 1), ("e", 3, 6, 7, 1), ("f", 1, 2, 3, 1)):
-                    if name in GADDS[i] and q == after:
-                        dst = flat[:, 512 * first : 512 * (first + n)]
-                        nc.gpsimd.tensor_tensor(dst, dst, flat[:, 512 * second : 512 * (second + n)], ADD)
-                        for j in range(second, second + n):
-                            left.remove(j)
+                if helped:
+                    if q == 2:
+                        add_corners(0, 1, 1)
+                elif q == 1 and i >= 2:
+                    add_corners(0, 2, 2)
+                elif q == 2 and i >= 3:
+                    add_corners(4, 5, 1)
 
-        w_scales = keep.tile([P, TAPS, HALVES, CHANNELS], U8, name="w_scales", align_bytes=64)
-        w_bf = keep.tile([P, TAPS, HALVES, CHANNELS, 4], BF16, name="w_bf", align_bytes=64)
-
-        def cast_w(o):
-            nc.gpsimd.tensor_copy(w_bf[:, o, :, :, :], w_raw[:, o, :, :, :].rearrange("p s t m -> p s m t"))
-
-        quantized = {}
-
-        def quantize_w():
-            w_codes = prod_pool.tile([P, TAPS, HALVES, CHANNELS], U32, name="prod", align_bytes=64)
-            for taps in (slice(0, 2), slice(2, 3)):
-                nc.vector.quantize_mx(
-                    out=w_codes[:, taps, :, :].rearrange("p o s m -> p (o s m)").bitcast(FP8X4),
-                    scales=w_scales[:, taps, :, :].rearrange("p o s m -> p (o s m)"),
-                    in_=w_bf[:, taps, :, :, :].rearrange("p o s m t -> p (o s m t)"),
-                )
-            quantized["w"] = w_codes
-
-        passes = [(s, o) for s in range(HALVES) for o in range(TAPS)]
-        e_bf = keep.tile([P, count, P, 4], BF16, name="e_bf", align_bytes=64)
-        e_scales = keep.tile([P, count, P], U8, name="e_scales", align_bytes=64)
-
-
-        def quantize_e(first, last, pool, tag):
-            codes = pool.tile([P, last - first, P], U32, name=tag, align_bytes=64)
-            for n in range(first, last):
-                quantized[n] = codes[:, n - first, :]
-            nc.vector.quantize_mx(
-                out=codes[:].rearrange("p n g -> p (n g)").bitcast(FP8X4),
-                scales=e_scales[:, first:last, :].rearrange("p n g -> p (n g)"),
-                in_=e_bf[:, first:last, :, :].rearrange("p n g t -> p (n g t)"),
-            )
-
-        def multiply(n, b):
-            s, o = passes[n]
-            if n == 0:
-                name = next_bank()
-                banks.remove(name)
-                quantized["acc", b] = psum.tile([P, P], F32, name=name)
-            acc = quantized["acc", b]
-            nc.tensor.matmul_mx(
-                out=acc[:],
-                lhsT=quantized["w"][:, o, s, :].bitcast(FP8X4),
-                lhsT_scale=w_scales[:, o, s, :],
-                rhs=quantized[2 * n + b].bitcast(FP8X4),
-                rhs_scale=e_scales[:, 2 * n + b, :],
-                start=(n == 0),
-                stop=(n == len(passes) - 1),
-            )
-
-        def finish(i):
-            if i in UNTURNED:
-                return
-            s, k = units[i]
-            o, b = k // 2, k % 2
+        def sum_unit(i):
             prod, left = addends[i]
-            turned = psum.tile([P, 4, P], F32, name=(f"turn{i % TB}" if TB else next_bank()))
-            if i >= count - JMAJOR:
-                if i >= count - SPLIT:
-                    steps = [(2 * u + e, j) for u in range(2) for j in left for e in range(2)]
-                else:
-                    steps = [(t, j) for j in left for t in range(4)]
+            turned = psum.tile([P, 4, P], F32, name=f"sum{i % SUM_BANKS}")
+            if i == LAST:
+                steps = [(2 * u + e, j) for u in range(2) for j in left for e in range(2)]
                 flags = [(n == 0, n == len(steps) - 1) for n in range(len(steps))]
             else:
                 steps = [(t, j) for t in range(4) for j in left]
                 flags = [(j == left[0], j == left[-1]) for t, j in steps]
             for (t, j), (start, stop) in zip(steps, flags):
-                nc.tensor.matmul(
-                    turned[:, t, :], prod[:, j, t // 2, t % 2, :], identity[:], start=start, stop=stop, is_transpose=True
-                )
-            dst = e_bf[:, i, :, :]
-            src = turned[:].rearrange("p t g -> p g t")
-            if i in VCOPY:
-                nc.vector.tensor_copy(dst, src)
-            else:
-                nc.scalar.activation(dst, src, COPY)
-            if i - 1 in UNTURNED:
-                finish_unturned(i - 1)
+                add_turned(turned[:, t, :], prod[:, j, t // 2, t % 2, :], start, stop)
+            nc.scalar.activation(e_bf[:, i, :, :], turned[:].rearrange("p t g -> p g t"), COPY)
 
-        for i in UNTURNED:
-            spread_weights(units[i][1])
-        for c in range(4):
-            cast_chunk(0, 0, c, "v")
-        for c in range(4):
-            cast_chunk(0, 1, c, "s")
-        for i, u in lookups[:4]:
-            gather(i, u)
-        for c in range(4):
-            cast_chunk(1, 0, c, "s")
-        finished = 0
-        for i in range(count):
-            corners(i)
-            if DAT <= i < DAT + COLUMNS // DW:
-                cast_chunk(1, 1, i - DAT, DENG[i - DAT])
-            if i - PLACE in UNTURNED:
-                place_unturned(i - PLACE)
-            for i2, u in lookups[2 * i + 4 : 2 * i + 6]:
-                gather(i2, u)
-            if WAT <= i < WAT + TAPS:
-                cast_w(i - WAT)
-            while finished <= i - LAGS[i]:
-                finish(finished)
-                finished = finished + 1
+        w_scales = keep.tile([P, TAPS, PASSES, CHANNELS], U8, name="w_scales", align_bytes=64)
+        w_bf = keep.tile([P, TAPS, PASSES, CHANNELS, 4], BF16, name="w_bf", align_bytes=64)
+
+        def cast_w(o):
+            nc.gpsimd.tensor_copy(w_bf[:, o, :, :, :], w_raw[:, o, :, :, :].rearrange("p s t m -> p s m t"))
+
+        spread_weights()
+        for c in range(CHUNKS):
+            cast_chunk(0, 0, c)
+        for c in range(CHUNKS):
+            cast_chunk(0, 1, c)
+        for u in range(2):
+            for i in range(2):
+                gather(i, u)
+        for c in range(CHUNKS):
+            cast_chunk(1, 0, c)
+        summed = 1
+        for i in range(UNITS):
+            if i == 0:
+                weigh_first()
+            else:
+                weigh(i)
+            if i < CHUNKS:
+                cast_chunk(1, 1, i)
+            if i == SUM_LAG + 2:
+                place_first()
+            if i + 2 < UNITS:
+                for u in range(2):
+                    gather(i + 2, u)
+            if i < TAPS:
+                cast_w(i)
+            while summed <= i - (SUM_LAG if i < LAST - 1 else 1):
+                sum_unit(summed)
+                if summed == 1:
+                    round_first()
+                summed = summed + 1
+        sum_unit(LAST)
+
+        w_codes = prod_pool.tile([P, TAPS, PASSES, CHANNELS], U32, name="prod", align_bytes=64)
+        for taps in (slice(0, 2), slice(2, 3)):
+            nc.vector.quantize_mx(
+                out=w_codes[:, taps, :, :].rearrange("p o s m -> p (o s m)").bitcast(FP8X4),
+                scales=w_scales[:, taps, :, :].rearrange("p o s m -> p (o s m)"),
+                in_=w_bf[:, taps, :, :, :].rearrange("p o s m t -> p (o s m t)"),
+            )
+        e_codes = {}
+
+        def quantize_e(lo, hi, pool, name):
+            codes = pool.tile([P, hi - lo, P], U32, name=name, align_bytes=64)
+            for i in range(lo, hi):
+                e_codes[i] = codes[:, i - lo, :]
+            nc.vector.quantize_mx(
+                out=codes[:].rearrange("p n g -> p (n g)").bitcast(FP8X4),
+                scales=e_scales[:, lo:hi, :].rearrange("p n g -> p (n g)"),
+                in_=e_bf[:, lo:hi, :, :].rearrange("p n g t -> p (n g t)"),
+            )
+
+        accs = {}
+
+        def multiply(i):
+            s, k = divmod(i, BLOCKS)
+            o, b = divmod(k, 2)
+            if i < 2:
+                accs[b] = psum.tile([P, P], F32, name=held_bank())
+            nc.tensor.matmul_mx(
+                out=accs[b][:],
+                lhsT=w_codes[:, o, s, :].bitcast(FP8X4),
+                lhsT_scale=w_scales[:, o, s, :],
+                rhs=e_codes[i].bitcast(FP8X4),
+                rhs_scale=e_scales[:, i, :],
+                start=(i < 2),
+                stop=(i >= UNITS - 2),
+            )
 
         def store(b):
             result = code_pool.tile([P, P], F32, name=f"result{b}")
-            nc.vector.tensor_copy(result[:], quantized["acc", b][:])
+            nc.vector.tensor_copy(result[:], accs[b][:])
             nc.sync.dma_start(out[:, b * P : (b + 1) * P], result[:])
 
-        for step in TAIL.split():
-            if step == "w":
-                quantize_w()
-            elif step == "a":
-                quantize_e(0, 8, prod_pool, "prod")
-            elif step == "b":
-                quantize_e(8, 10, code_pool, "codes4")
-            elif step == "c":
-                quantize_e(10, 11, code_pool, "codes5")
-            elif step == "d":
-                quantize_e(11, 12, code_pool, "codes6")
-            elif step == "f":
-                finish(finished)
-                finished = finished + 1
-            elif step == "x":
-                for n in range(6):
-                    multiply(n, 0)
-                store(0)
-            elif step == "y":
-                for n in range(5):
-                    multiply(n, 1)
-            else:
-                multiply(5, 1)
-                store(1)
+        quantize_e(0, 8, prod_pool, "prod")
+        quantize_e(8, 10, code_pool, "codes8")
+        quantize_e(10, 11, code_pool, "codes10")
+        for i in range(1, LAST, 2):
+            multiply(i)
+        for i in range(0, LAST, 2):
+            multiply(i)
+        store(0)
+        quantize_e(LAST, UNITS, code_pool, "codes11")
+        multiply(LAST)
+        store(1)

@@ -28,9 +28,8 @@ LIST_COLUMNS = ENTRIES // 16
 CHUNKS = 4
 CHUNK = COLUMNS // CHUNKS
 CORNER = 4 * P
-HELPED = 3
+HELPED = 2
 SUM_LAG = 2
-SUM_BANKS = 2
 
 
 def tile_attend_deform_kernel(tc, xT, w, part, offs, out):
@@ -50,8 +49,8 @@ def tile_attend_deform_kernel(tc, xT, w, part, offs, out):
         def staging_name(s, u, c):
             return f"staged{s}{u}{c}"
 
-        def load_window(s, u):
-            for c in range(CHUNKS):
+        def load_window(s, u, chunks=range(CHUNKS)):
+            for c in chunks:
                 raw = keep.tile([P, 2, CHUNK], F32, name=staging_name(s, u, c), align_bytes=64)
                 nc.sync.dma_start(raw[:], x_view[s, u, :, :, c * CHUNK : (c + 1) * CHUNK])
                 staged[s, u, c] = raw
@@ -72,12 +71,12 @@ def tile_attend_deform_kernel(tc, xT, w, part, offs, out):
         nc.scalar.dma_start(weights[:], part[0:1, :].rearrange("one (k g j) -> g (one k) j", g=P, j=CORNERS))
         load_window(0, 1)
         load_window(1, 0)
-        load_window(1, 1)
+        load_window(1, 1, range(CHUNKS // 2))
         w_raw = keep.tile([P, TAPS, PASSES, 4, CHANNELS], F32, name="w_raw")
-        w_view = w.rearrange("o (s p t) m -> o s p t m", s=PASSES, t=4)
+        w_view = w.rearrange("o (s p t) m -> o p s t m", s=PASSES, t=4)
         for o in range(TAPS):
-            for s in range(PASSES):
-                nc.sync.dma_start(w_raw[:, o, s, :, :], w_view[o, s])
+            nc.sync.dma_start(w_raw[:, o, :, :, :], w_view[o])
+        load_window(1, 1, range(CHUNKS // 2, CHUNKS))
 
         identity = keep.tile([P, P], F32, name="identity")
         make_identity(nc, identity[:])
@@ -104,7 +103,7 @@ def tile_attend_deform_kernel(tc, xT, w, part, offs, out):
             )
             words[i, u] = got
 
-        banks = [f"bank{n}" for n in range(8 - SUM_BANKS)]
+        banks = [f"bank{n}" for n in range(8)]
 
         def next_bank():
             name = banks[0]
@@ -176,13 +175,13 @@ def tile_attend_deform_kernel(tc, xT, w, part, offs, out):
 
         def weigh(i):
             k = i % BLOCKS
-            helped = i >= UNITS - HELPED
+            own = CORNERS if i < UNITS - HELPED else 4
             if i <= 2:
                 prod = keep.tile([P, CORNERS, 2, 2, P], F32, name=staging_name(1, 1, i - 1), align_bytes=64)
             else:
                 prod = prod_pool.tile([P, CORNERS, 2, 2, P], F32, name="prod", align_bytes=64)
             flat = prod[:].rearrange("g j u e p -> g (j u e p)")
-            left = list(range(4 if helped else CORNERS))
+            left = list(range(own))
             addends[i] = (prod, left)
 
             def add_corners(onto, taken, n):
@@ -205,7 +204,7 @@ def tile_attend_deform_kernel(tc, xT, w, part, offs, out):
                             else:
                                 weigh_and_add(prod[:, jj, u, :, :], src, scale)
                 return
-            for q in (0, 2, 1, 3) if helped else range(4):
+            for q in (0, 2, 1, 3) if own == 4 else range(4):
                 bank = psum.tile([P, 2, 2, P], F32, name=next_bank())
                 for u in (1, 0):
                     for h in range(2):
@@ -214,22 +213,21 @@ def tile_attend_deform_kernel(tc, xT, w, part, offs, out):
                     j = 2 * q + h
                     src = bank[:, h, :, :].bitcast(BF16).rearrange("g u (p e) -> g u e p", e=2)
                     scale = weights[:, k, j : j + 1]
-                    if helped and q >= 2:
+                    if j >= own:
                         for u in range(2):
-                            weigh_and_add(prod[:, j - 4, u, :, :], src[:, u, :, :], scale)
+                            weigh_and_add(prod[:, j % own, u, :, :], src[:, u, :, :], scale)
                     else:
                         nc.scalar.activation(prod[:, j, :, :, :], src, COPY, scale=scale)
-                if helped:
-                    if q == 2:
-                        add_corners(0, 1, 1)
-                elif q == 1 and i >= 2:
+                if own == 4 and q == 2:
+                    add_corners(0, 1, 1)
+                elif own == CORNERS and q == 1 and i >= 2:
                     add_corners(0, 2, 2)
-                elif q == 2 and i >= 3:
-                    add_corners(4, 5, 1)
+                elif own == CORNERS and q == 3 and i >= 2:
+                    add_corners(4, 6, 2)
 
         def sum_unit(i):
             prod, left = addends[i]
-            turned = psum.tile([P, 4, P], F32, name=f"sum{i % SUM_BANKS}")
+            turned = psum.tile([P, 4, P], F32, name=next_bank())
             if i == LAST:
                 steps = [(2 * u + e, j) for u in range(2) for j in left for e in range(2)]
                 flags = [(n == 0, n == len(steps) - 1) for n in range(len(steps))]
@@ -256,7 +254,6 @@ def tile_attend_deform_kernel(tc, xT, w, part, offs, out):
                 gather(i, u)
         for c in range(CHUNKS):
             cast_chunk(1, 0, c)
-        summed = 1
         for i in range(UNITS):
             if i == 0:
                 weigh_first()
@@ -271,12 +268,12 @@ def tile_attend_deform_kernel(tc, xT, w, part, offs, out):
                     gather(i + 2, u)
             if i < TAPS:
                 cast_w(i)
-            while summed <= i - (SUM_LAG if i < LAST - 1 else 1):
-                sum_unit(summed)
-                if summed == 1:
-                    round_first()
-                summed = summed + 1
-        sum_unit(LAST)
+            if i > SUM_LAG:
+                sum_unit(i - SUM_LAG)
+            if i == SUM_LAG + 1:
+                round_first()
+        for i in range(UNITS - SUM_LAG, UNITS):
+            sum_unit(i)
 
         w_codes = prod_pool.tile([P, TAPS, PASSES, CHANNELS], U32, name="prod", align_bytes=64)
         for taps in (slice(0, 2), slice(2, 3)):

@@ -20,8 +20,8 @@ ADD = mybir.AluOpType.add
 
 P = 128
 PASSES = FEATURES // 512
-BLOCKS = TAPS * POINTS // P
-UNITS = PASSES * BLOCKS
+BATCHES = TAPS * POINTS // P
+UNITS = PASSES * BATCHES
 LAST = UNITS - 1
 ENTRIES = P * CORNERS
 LIST_COLUMNS = ENTRIES // 16
@@ -41,35 +41,44 @@ def tile_attend_deform_kernel(tc, xT, w, part, offs, out):
         code_pool = ctx.enter_context(tc.tile_pool(name="codes", bufs=1))
         psum = ctx.enter_context(tc.psum_pool(name="banks", bufs=1))
 
-        offsets = lists.tile([P, BLOCKS * LIST_COLUMNS], U16, name="offsets")
-        x_view = xT.rearrange("(s p u e) c -> s u p e c", s=PASSES, p=P, u=2, e=2)
+        offsets = lists.tile([P, BATCHES * LIST_COLUMNS], U16, name="offsets")
+        x_view = xT.rearrange("(s p u r) c -> s u p r c", s=PASSES, p=P, u=2, r=2)
         staged = {}
         tables = {}
 
         def staging_name(s, u, c):
             return f"staged{s}{u}{c}"
 
+        def runs(s, u):
+            width = CHUNK // 2 if (s, u) == (0, 1) else CHUNK
+            return [slice(col, col + width) for col in range(0, CHUNK, width)]
+
         def load_window(s, u, chunks=range(CHUNKS)):
             for c in chunks:
                 raw = keep.tile([P, 2, CHUNK], F32, name=staging_name(s, u, c), align_bytes=64)
-                nc.sync.dma_start(raw[:], x_view[s, u, :, :, c * CHUNK : (c + 1) * CHUNK])
+                source = x_view[s, u, :, :, c * CHUNK : (c + 1) * CHUNK]
+                for run in runs(s, u):
+                    nc.sync.dma_start(raw[:, :, run], source[:, :, run])
                 staged[s, u, c] = raw
 
         def cast_chunk(s, u, c):
             if c == 0:
                 tables[s, u] = keep.tile([P, COLUMNS, 2], BF16, name=f"table{s}{u}", align_bytes=64)
             dst = tables[s, u][:, c * CHUNK : (c + 1) * CHUNK, :]
-            src = staged[s, u, c][:].rearrange("p e c -> p c e")
-            if (s, u) == (0, 0):
-                nc.vector.tensor_copy(dst, src)
-            else:
-                nc.scalar.activation(dst, src, COPY)
+            src = staged[s, u, c][:].rearrange("p r c -> p c r")
+            for run in runs(s, u):
+                if (s, u) == (0, 0):
+                    nc.vector.tensor_copy(dst[:, run, :], src[:, run, :])
+                else:
+                    nc.scalar.activation(dst[:, run, :], src[:, run, :], COPY)
 
         load_window(0, 0)
         nc.sync.dma_start(offsets[:], offs)
-        weights = keep.tile([P, BLOCKS, CORNERS], F32, name="weights")
-        nc.scalar.dma_start(weights[:], part[0:1, :].rearrange("one (k g j) -> g (one k) j", g=P, j=CORNERS))
+        weights = keep.tile([P, BATCHES, CORNERS], F32, name="weights")
+        part_view = part[0:1, :].rearrange("one (k g j) -> g (one k) j", g=P, j=CORNERS)
+        nc.scalar.dma_start(weights[:, 0:1, :], part_view[:, 0:1, :])
         load_window(0, 1)
+        nc.sync.dma_start(weights[:, 1:, :], part_view[:, 1:, :])
         load_window(1, 0)
         load_window(1, 1, range(CHUNKS // 2))
         w_raw = keep.tile([P, TAPS, PASSES, 4, CHANNELS], F32, name="w_raw")
@@ -89,14 +98,14 @@ def tile_attend_deform_kernel(tc, xT, w, part, offs, out):
                 name = f"words{i}{u}"
             elif i == 2:
                 name = staging_name(0, 1, CHUNKS - 1 - u)
-            elif i == BLOCKS:
+            elif i == BATCHES:
                 name = staging_name(1, 1, CHUNKS - 2 + u)
             else:
-                name = word_names[i - (2 if i < BLOCKS else 3), u]
+                name = word_names[i - (2 if i < BATCHES else 3), u]
             word_names[i, u] = name
-            s, k = divmod(i, BLOCKS)
+            s, k = divmod(i, BATCHES)
             got = keep.tile([P, ENTRIES], U32, name=name, align_bytes=64)
-            window = tables[s, u][:].rearrange("p c e -> p (c e)").bitcast(U32)
+            window = tables[s, u][:].rearrange("p c r -> p (c r)").bitcast(U32)
             nc.vector.tensor_copy(
                 got[:].rearrange("p (q g h) -> p g q h", q=4, h=2),
                 window.indirect(offsets[:, k * LIST_COLUMNS : (k + 1) * LIST_COLUMNS]),
@@ -137,23 +146,23 @@ def tile_attend_deform_kernel(tc, xT, w, part, offs, out):
             first["bank"] = held_bank()
             first["sums"] = psum.tile([P, 2, 2, P], F32, name=first["bank"])
             for u in range(2):
-                values = words[0, u][:].bitcast(BF16).rearrange("p (q g h e) -> p e q h g", q=4, h=2, e=2)
-                for e in range(2):
-                    products = keep.tile([P, CORNERS, P], F32, name=f"first_products{e}")
+                values = words[0, u][:].bitcast(BF16).rearrange("p (q g h r) -> p r q h g", q=4, h=2, r=2)
+                for r in range(2):
+                    products = keep.tile([P, CORNERS, P], F32, name=f"first_products{r}")
                     nc.gpsimd.tensor_tensor(
                         products[:].rearrange("p (q h) g -> p q h g", h=2),
-                        values[:, e],
+                        values[:, r],
                         first["spread"][:].rearrange("p (q h) g -> p q h g", h=2),
                         MULT,
                     )
                     for j in range(CORNERS):
-                        add_turned(first["sums"][:, u, e, :], products[:, j, :], j == 0, j == CORNERS - 1)
+                        add_turned(first["sums"][:, u, r, :], products[:, j, :], j == 0, j == CORNERS - 1)
 
         def round_first():
             rounded = keep.tile([P, 2, P, 2], BF16, name=staging_name(1, 1, 0), align_bytes=64)
-            nc.scalar.activation(rounded[:], first["sums"][:].rearrange("g u e p -> g u p e"), COPY)
+            nc.scalar.activation(rounded[:], first["sums"][:].rearrange("g u r p -> g u p r"), COPY)
             first["back"] = psum.tile([P, 2, P], F32, name=first["bank"])
-            pairs = rounded[:].rearrange("g u p e -> g u (p e)").bitcast(F32)
+            pairs = rounded[:].rearrange("g u p r -> g u (p r)").bitcast(F32)
             for u in range(2):
                 nc.tensor.transpose(first["back"][:, u, :], pairs[:, u, :], identity[:])
 
@@ -174,13 +183,13 @@ def tile_attend_deform_kernel(tc, xT, w, part, offs, out):
             nc.vector.scalar_tensor_tensor(dst, src, scale, dst, op0=MULT, op1=ADD)
 
         def weigh(i):
-            k = i % BLOCKS
+            k = i % BATCHES
             own = CORNERS if i < UNITS - HELPED else 4
             if i <= 2:
                 prod = keep.tile([P, CORNERS, 2, 2, P], F32, name=staging_name(1, 1, i - 1), align_bytes=64)
             else:
                 prod = prod_pool.tile([P, CORNERS, 2, 2, P], F32, name="prod", align_bytes=64)
-            flat = prod[:].rearrange("g j u e p -> g (j u e p)")
+            flat = prod[:].rearrange("g j u r p -> g (j u r p)")
             left = list(range(own))
             addends[i] = (prod, left)
 
@@ -197,7 +206,7 @@ def tile_attend_deform_kernel(tc, xT, w, part, offs, out):
                         for jj in range(4):
                             lift(bank[:, jj, :], i, u, 4 * half + jj)
                         for jj in range(4):
-                            src = bank[:, jj, :].bitcast(BF16).rearrange("g (p e) -> g e p", e=2)
+                            src = bank[:, jj, :].bitcast(BF16).rearrange("g (p r) -> g r p", r=2)
                             scale = weights[:, k, 4 * half + jj : 4 * half + jj + 1]
                             if half == 0:
                                 nc.scalar.activation(prod[:, jj, u, :, :], src, COPY, scale=scale)
@@ -211,15 +220,15 @@ def tile_attend_deform_kernel(tc, xT, w, part, offs, out):
                         lift(bank[:, h, u, :], i, u, 2 * q + h)
                 for h in range(2):
                     j = 2 * q + h
-                    src = bank[:, h, :, :].bitcast(BF16).rearrange("g u (p e) -> g u e p", e=2)
+                    src = bank[:, h, :, :].bitcast(BF16).rearrange("g u (p r) -> g u r p", r=2)
                     scale = weights[:, k, j : j + 1]
                     if j >= own:
                         for u in range(2):
                             weigh_and_add(prod[:, j % own, u, :, :], src[:, u, :, :], scale)
                     else:
                         nc.scalar.activation(prod[:, j, :, :, :], src, COPY, scale=scale)
-                if own == 4 and q == 2:
-                    add_corners(0, 1, 1)
+                if own == 4 and q >= 2:
+                    add_corners(2 * q - 4, 2 * q - 3, 1)
                 elif own == CORNERS and q == 1 and i >= 2:
                     add_corners(0, 2, 2)
                 elif own == CORNERS and q == 3 and i >= 2:
@@ -229,7 +238,7 @@ def tile_attend_deform_kernel(tc, xT, w, part, offs, out):
             prod, left = addends[i]
             turned = psum.tile([P, 4, P], F32, name=next_bank())
             if i == LAST:
-                steps = [(2 * u + e, j) for u in range(2) for j in left for e in range(2)]
+                steps = [(2 * u + r, j) for u in range(2) for j in left for r in range(2)]
                 flags = [(n == 0, n == len(steps) - 1) for n in range(len(steps))]
             else:
                 steps = [(t, j) for t in range(4) for j in left]
@@ -297,7 +306,7 @@ def tile_attend_deform_kernel(tc, xT, w, part, offs, out):
         accs = {}
 
         def multiply(i):
-            s, k = divmod(i, BLOCKS)
+            s, k = divmod(i, BATCHES)
             o, b = divmod(k, 2)
             if i < 2:
                 accs[b] = psum.tile([P, P], F32, name=held_bank())

@@ -49,28 +49,24 @@ def tile_attend_deform_kernel(tc, xT, w, part, offs, out):
         def staging_name(s, u, c):
             return f"staged{s}{u}{c}"
 
-        def runs(s, u):
-            width = CHUNK // 2 if (s, u) == (0, 1) else CHUNK
-            return [slice(col, col + width) for col in range(0, CHUNK, width)]
-
         def load_window(s, u, chunks=range(CHUNKS)):
             for c in chunks:
-                raw = keep.tile([P, 2, CHUNK], F32, name=staging_name(s, u, c), align_bytes=64)
-                source = x_view[s, u, :, :, c * CHUNK : (c + 1) * CHUNK]
-                for run in runs(s, u):
-                    nc.sync.dma_start(raw[:, :, run], source[:, :, run])
+                if c == 0:
+                    tables[s, u] = keep.tile([P, COLUMNS], F32, name=f"table{s}{u}", align_bytes=64)
+                if c % 1 == 0:
+                    run = slice(c * CHUNK, (c + 1) * CHUNK)
+                    nc.sync.dma_start(tables[s, u][:, run], x_view[s, u, :, 1, run])
+                raw = keep.tile([P, CHUNK], F32, name=staging_name(s, u, c), align_bytes=64)
+                nc.sync.dma_start(raw[:], x_view[s, u, :, 0, c * CHUNK : (c + 1) * CHUNK])
                 staged[s, u, c] = raw
 
         def cast_chunk(s, u, c):
-            if c == 0:
-                tables[s, u] = keep.tile([P, COLUMNS, 2], BF16, name=f"table{s}{u}", align_bytes=64)
-            dst = tables[s, u][:, c * CHUNK : (c + 1) * CHUNK, :]
-            src = staged[s, u, c][:].rearrange("p r c -> p c r")
-            for run in runs(s, u):
-                if (s, u) == (0, 0):
-                    nc.vector.tensor_copy(dst[:, run, :], src[:, run, :])
-                else:
-                    nc.scalar.activation(dst[:, run, :], src[:, run, :], COPY)
+            halves = tables[s, u][:].bitcast(BF16).rearrange("p (c r) -> p c r", r=2)
+            dst = halves[:, c * CHUNK : (c + 1) * CHUNK, 0]
+            if (s, u) == (0, 0) and c > 0:
+                nc.vector.tensor_copy(dst, staged[s, u, c][:])
+            else:
+                nc.scalar.activation(dst, staged[s, u, c][:], COPY)
 
         load_window(0, 0)
         nc.sync.dma_start(offsets[:], offs)
@@ -80,12 +76,12 @@ def tile_attend_deform_kernel(tc, xT, w, part, offs, out):
         load_window(0, 1)
         nc.sync.dma_start(weights[:, 1:, :], part_view[:, 1:, :])
         load_window(1, 0)
-        load_window(1, 1, range(CHUNKS // 2))
+        load_window(1, 1, range(2))
         w_raw = keep.tile([P, TAPS, PASSES, 4, CHANNELS], F32, name="w_raw")
         w_view = w.rearrange("o (s p t) m -> o p s t m", s=PASSES, t=4)
         for o in range(TAPS):
             nc.sync.dma_start(w_raw[:, o, :, :, :], w_view[o])
-        load_window(1, 1, range(CHUNKS // 2, CHUNKS))
+        load_window(1, 1, range(2, CHUNKS))
 
         identity = keep.tile([P, P], F32, name="identity")
         make_identity(nc, identity[:])
@@ -98,6 +94,8 @@ def tile_attend_deform_kernel(tc, xT, w, part, offs, out):
                 name = f"words{i}{u}"
             elif i == 2:
                 name = staging_name(0, 1, CHUNKS - 1 - u)
+            elif (i, u) == (3, 0):
+                name = staging_name(1, 0, 0)
             elif i == BATCHES:
                 name = staging_name(1, 1, CHUNKS - 2 + u)
             else:
@@ -105,7 +103,7 @@ def tile_attend_deform_kernel(tc, xT, w, part, offs, out):
             word_names[i, u] = name
             s, k = divmod(i, BATCHES)
             got = keep.tile([P, ENTRIES], U32, name=name, align_bytes=64)
-            window = tables[s, u][:].rearrange("p c r -> p (c r)").bitcast(U32)
+            window = tables[s, u][:].bitcast(U32)
             nc.vector.tensor_copy(
                 got[:].rearrange("p (q g h) -> p g q h", q=4, h=2),
                 window.indirect(offsets[:, k * LIST_COLUMNS : (k + 1) * LIST_COLUMNS]),
@@ -159,7 +157,7 @@ def tile_attend_deform_kernel(tc, xT, w, part, offs, out):
                         add_turned(first["sums"][:, u, r, :], products[:, j, :], j == 0, j == CORNERS - 1)
 
         def round_first():
-            rounded = keep.tile([P, 2, P, 2], BF16, name=staging_name(1, 1, 0), align_bytes=64)
+            rounded = keep.tile([P, 2, P, 2], BF16, name="prod1", align_bytes=64)
             nc.scalar.activation(rounded[:], first["sums"][:].rearrange("g u r p -> g u p r"), COPY)
             first["back"] = psum.tile([P, 2, P], F32, name=first["bank"])
             pairs = rounded[:].rearrange("g u p r -> g u (p r)").bitcast(F32)
@@ -182,11 +180,13 @@ def tile_attend_deform_kernel(tc, xT, w, part, offs, out):
         def weigh_and_add(dst, src, scale):
             nc.vector.scalar_tensor_tensor(dst, src, scale, dst, op0=MULT, op1=ADD)
 
-        def weigh(i):
+        def weigh(i, windows=(0, 1)):
             k = i % BATCHES
             own = CORNERS if i < UNITS - HELPED else 4
-            if i <= 2:
-                prod = keep.tile([P, CORNERS, 2, 2, P], F32, name=staging_name(1, 1, i - 1), align_bytes=64)
+            if i == 1 and (1 in addends):
+                prod = addends[1][0]
+            elif i <= 2:
+                prod = keep.tile([P, CORNERS, 2, 2, P], F32, name="prod1" if i == 1 else staging_name(1, 1, 0), align_bytes=64)
             else:
                 prod = prod_pool.tile([P, CORNERS, 2, 2, P], F32, name="prod", align_bytes=64)
             flat = prod[:].rearrange("g j u r p -> g (j u r p)")
@@ -199,8 +199,8 @@ def tile_attend_deform_kernel(tc, xT, w, part, offs, out):
                 for j in range(taken, taken + n):
                     left.remove(j)
 
-            if i == LAST:
-                for u in range(2):
+            if i == LAST or (i == 1 and 1):
+                for u in windows:
                     for half in range(2):
                         bank = psum.tile([P, 4, P], F32, name=next_bank())
                         for jj in range(4):
@@ -208,10 +208,15 @@ def tile_attend_deform_kernel(tc, xT, w, part, offs, out):
                         for jj in range(4):
                             src = bank[:, jj, :].bitcast(BF16).rearrange("g (p r) -> g r p", r=2)
                             scale = weights[:, k, 4 * half + jj : 4 * half + jj + 1]
-                            if half == 0:
-                                nc.scalar.activation(prod[:, jj, u, :, :], src, COPY, scale=scale)
+                            if half == 0 or i < LAST:
+                                nc.scalar.activation(prod[:, 4 * half + jj, u, :, :], src, COPY, scale=scale)
                             else:
                                 weigh_and_add(prod[:, jj, u, :, :], src, scale)
+                if i == 1:
+                    for u in windows:
+                        nc.gpsimd.tensor_tensor(prod[:, 0:4, u, :, :], prod[:, 0:4, u, :, :], prod[:, 4:8, u, :, :], ADD)
+                    for j in range(4, 8):
+                        left.remove(j)
                 return
             for q in (0, 2, 1, 3) if own == 4 else range(4):
                 bank = psum.tile([P, 2, 2, P], F32, name=next_bank())
@@ -251,7 +256,8 @@ def tile_attend_deform_kernel(tc, xT, w, part, offs, out):
         w_bf = keep.tile([P, TAPS, PASSES, CHANNELS, 4], BF16, name="w_bf", align_bytes=64)
 
         def cast_w(o):
-            nc.gpsimd.tensor_copy(w_bf[:, o, :, :, :], w_raw[:, o, :, :, :].rearrange("p s t m -> p s m t"))
+            src = w_raw[:, o, :, :, :].rearrange("p s t m -> p s m t")
+            nc.gpsimd.tensor_scalar(w_bf[:, o, :, :, :], src, 1.0, 0.0, op0=MULT, op1=ADD)
 
         spread_weights()
         for c in range(CHUNKS):
@@ -261,22 +267,26 @@ def tile_attend_deform_kernel(tc, xT, w, part, offs, out):
         for u in range(2):
             for i in range(2):
                 gather(i, u)
+        weigh_first()
+        if 1:
+            weigh(1, (0,))
         for c in range(CHUNKS):
             cast_chunk(1, 0, c)
         for i in range(UNITS):
-            if i == 0:
-                weigh_first()
-            else:
+            if i == 1 and 1:
+                weigh(1, (1,))
+            elif i > 0:
                 weigh(i)
-            if i < CHUNKS:
-                cast_chunk(1, 1, i)
+            for c in range(CHUNKS):
+                if (1, 1, 2, 3)[c] == i:
+                    cast_chunk(1, 1, c)
             if i == SUM_LAG + 2:
                 place_first()
             if i + 2 < UNITS:
                 for u in range(2):
                     gather(i + 2, u)
-            if i < TAPS:
-                cast_w(i)
+            if 1 <= i <= TAPS:
+                cast_w(i - 1)
             if i > SUM_LAG:
                 sum_unit(i - SUM_LAG)
             if i == SUM_LAG + 1:

@@ -182,7 +182,7 @@ def tile_attend_deform_kernel(tc, xT, w, part, offs, out):
 
         def weigh(i, windows=(0, 1)):
             k = i % BATCHES
-            own = CORNERS if i < UNITS - HELPED else 4
+            own = CORNERS
             if i == 1 and (1 in addends):
                 prod = addends[1][0]
             elif i <= 2:
@@ -218,7 +218,7 @@ def tile_attend_deform_kernel(tc, xT, w, part, offs, out):
                     for j in range(4, 8):
                         left.remove(j)
                 return
-            for q in (0, 2, 1, 3) if own == 4 else range(4):
+            for q in range(4):
                 bank = psum.tile([P, 2, 2, P], F32, name=next_bank())
                 for u in (1, 0):
                     for h in range(2):
@@ -227,21 +227,19 @@ def tile_attend_deform_kernel(tc, xT, w, part, offs, out):
                     j = 2 * q + h
                     src = bank[:, h, :, :].bitcast(BF16).rearrange("g u (p r) -> g u r p", r=2)
                     scale = weights[:, k, j : j + 1]
-                    if j >= own:
-                        for u in range(2):
-                            weigh_and_add(prod[:, j % own, u, :, :], src[:, u, :, :], scale)
-                    else:
-                        nc.scalar.activation(prod[:, j, :, :, :], src, COPY, scale=scale)
-                if own == 4 and q >= 2:
-                    add_corners(2 * q - 4, 2 * q - 3, 1)
-                elif own == CORNERS and q == 1 and i >= 2:
+                    nc.scalar.activation(prod[:, j, :, :, :], src, COPY, scale=scale)
+                if q == -1 and 4 <= i:
+                    sum_unit(i - SUM_LAG)
+                if q == 1:
                     add_corners(0, 2, 2)
-                elif own == CORNERS and q == 3 and i >= 2:
+                    if i in ():
+                        add_corners(0, 1, 1)
+                elif q == 3:
                     add_corners(4, 6, 2)
 
-        def sum_unit(i):
+        def sum_unit(i, name=None):
             prod, left = addends[i]
-            turned = psum.tile([P, 4, P], F32, name=next_bank())
+            turned = psum.tile([P, 4, P], F32, name=name or next_bank())
             if i == LAST:
                 steps = [(2 * u + r, j) for u in range(2) for j in left for r in range(2)]
                 flags = [(n == 0, n == len(steps) - 1) for n in range(len(steps))]
@@ -272,7 +270,7 @@ def tile_attend_deform_kernel(tc, xT, w, part, offs, out):
             weigh(1, (0,))
         for c in range(CHUNKS):
             cast_chunk(1, 0, c)
-        for i in range(UNITS):
+        for i in range(LAST - 1):
             if i == 1 and 1:
                 weigh(1, (1,))
             elif i > 0:
@@ -291,10 +289,69 @@ def tile_attend_deform_kernel(tc, xT, w, part, offs, out):
                 sum_unit(i - SUM_LAG)
             if i == SUM_LAG + 1:
                 round_first()
-        for i in range(UNITS - SUM_LAG, UNITS):
-            sum_unit(i)
+        def again(name):
+            banks.remove(name)
+            banks.append(name)
+            return name
 
-        w_codes = prod_pool.tile([P, TAPS, PASSES, CHANNELS], U32, name="prod", align_bytes=64)
+        def chain_bank(q):
+            i = LAST - 1
+            prod = addends[i][0]
+            bank = psum.tile([P, 2, 2, P], F32, name=next_bank())
+            for u in (1, 0):
+                for h in range(2):
+                    lift(bank[:, h, u, :], i, u, 2 * q + h)
+            for h in range(2):
+                j = 2 * q + h
+                scale = weights[:, i % BATCHES, j : j + 1]
+                for u in range(2):
+                    src = bank[:, h, u, :].bitcast(BF16).rearrange("g (p r) -> g r p", r=2)
+                    if j == 0:
+                        nc.vector.tensor_scalar(prod[:, 0, u, :, :], src, scale, None, op0=MULT)
+                    else:
+                        weigh_and_add(prod[:, 0, u, :, :], src, scale)
+
+        def last_bank(u, half, name):
+            prod = addends[LAST][0]
+            bank = psum.tile([P, 4, P], F32, name=name)
+            for jj in range(4):
+                lift(bank[:, jj, :], LAST, u, 4 * half + jj)
+            for jj in range(4):
+                src = bank[:, jj, :].bitcast(BF16).rearrange("g (p r) -> g r p", r=2)
+                scale = weights[:, LAST % BATCHES, 4 * half + jj : 4 * half + jj + 1]
+                if half == 0:
+                    nc.scalar.activation(prod[:, jj, u, :, :], src, COPY, scale=scale)
+                else:
+                    weigh_and_add(prod[:, jj, u, :, :], src, scale)
+            return name
+
+        chained = keep.tile([P, 1, 2, 2, P], F32, name="chained", align_bytes=64)
+        addends[LAST - 1] = (chained, [0])
+        closing = prod_pool.tile([P, CORNERS, 2, 2, P], F32, name="prod", align_bytes=64)
+        addends[LAST] = (closing, list(range(4)))
+        used = {}
+        used["q0"] = banks[0]
+        chain_bank(0)
+        used["q1"] = banks[0]
+        chain_bank(1)
+        used["q2"] = banks[0]
+        chain_bank(2)
+        used["s8"] = next_bank()
+        sum_unit(8, used["s8"])
+        used["a"] = last_bank(0, 0, next_bank())
+        used["q3"] = banks[0]
+        chain_bank(3)
+        used["c"] = last_bank(1, 0, next_bank())
+        used["b"] = last_bank(0, 1, next_bank())
+        used["d"] = last_bank(1, 1, again(used["a"]))
+        used["s9"] = next_bank()
+        sum_unit(9, used["s9"])
+        used["s10"] = again(used["c"])
+        sum_unit(10, used["s10"])
+        used["s11"] = next_bank()
+        sum_unit(11, used["s11"])
+
+        w_codes = keep.tile([P, TAPS, PASSES, CHANNELS], U32, name=word_names[LAST, 1], align_bytes=64)
         for taps in (slice(0, 2), slice(2, 3)):
             nc.vector.quantize_mx(
                 out=w_codes[:, taps, :, :].rearrange("p o s m -> p (o s m)").bitcast(FP8X4),
@@ -335,7 +392,7 @@ def tile_attend_deform_kernel(tc, xT, w, part, offs, out):
             nc.vector.tensor_copy(result[:], accs[b][:])
             nc.sync.dma_start(out[:, b * P : (b + 1) * P], result[:])
 
-        quantize_e(0, 8, prod_pool, "prod")
+        quantize_e(0, 8, keep, word_names[LAST, 0])
         quantize_e(8, 10, code_pool, "codes8")
         quantize_e(10, 11, code_pool, "codes10")
         for i in range(1, LAST, 2):

@@ -37,7 +37,6 @@ def tile_attend_deform_kernel(tc, xT, w, part, offs, out):
     with ExitStack() as ctx:
         lists = ctx.enter_context(tc.tile_pool(name="lists", bufs=1))
         keep = ctx.enter_context(tc.tile_pool(name="keep", bufs=1))
-        prod_pool = ctx.enter_context(tc.tile_pool(name="prod", bufs=SUM_LAG + 1))
         code_pool = ctx.enter_context(tc.tile_pool(name="codes", bufs=1))
         psum = ctx.enter_context(tc.psum_pool(name="banks", bufs=1))
 
@@ -53,8 +52,9 @@ def tile_attend_deform_kernel(tc, xT, w, part, offs, out):
             for c in chunks:
                 if c == 0:
                     tables[s, u] = keep.tile([P, COLUMNS], F32, name=f"table{s}{u}", align_bytes=64)
-                if c % 1 == 0:
-                    run = slice(c * CHUNK, (c + 1) * CHUNK)
+                wide = (1, 2, 2, 2)[2 * s + u]
+                if c % wide == 0:
+                    run = slice(c * CHUNK, (c + wide) * CHUNK)
                     nc.sync.dma_start(tables[s, u][:, run], x_view[s, u, :, 1, run])
                 raw = keep.tile([P, CHUNK], F32, name=staging_name(s, u, c), align_bytes=64)
                 nc.sync.dma_start(raw[:], x_view[s, u, :, 0, c * CHUNK : (c + 1) * CHUNK])
@@ -90,16 +90,14 @@ def tile_attend_deform_kernel(tc, xT, w, part, offs, out):
         word_names = {}
 
         def gather(i, u):
-            if i < 2:
-                name = f"words{i}{u}"
-            elif i == 2:
-                name = staging_name(0, 1, CHUNKS - 1 - u)
-            elif (i, u) == (3, 0):
+            if (i, u) == (3, 0):
+                name = staging_name(0, 1, CHUNKS - 1)
+            elif (i, u) == (4, 0):
                 name = staging_name(1, 0, 0)
-            elif i == BATCHES:
-                name = staging_name(1, 1, CHUNKS - 2 + u)
+            elif i < 4:
+                name = f"words{i}{u}"
             else:
-                name = word_names[i - (2 if i < BATCHES else 3), u]
+                name = word_names[i - 3, u]
             word_names[i, u] = name
             s, k = divmod(i, BATCHES)
             got = keep.tile([P, ENTRIES], U32, name=name, align_bytes=64)
@@ -157,7 +155,7 @@ def tile_attend_deform_kernel(tc, xT, w, part, offs, out):
                         add_turned(first["sums"][:, u, r, :], products[:, j, :], j == 0, j == CORNERS - 1)
 
         def round_first():
-            rounded = keep.tile([P, 2, P, 2], BF16, name="prod1", align_bytes=64)
+            rounded = keep.tile([P, 2, P, 2], BF16, name=staging_name(1, 1, 0), align_bytes=64)
             nc.scalar.activation(rounded[:], first["sums"][:].rearrange("g u r p -> g u p r"), COPY)
             first["back"] = psum.tile([P, 2, P], F32, name=first["bank"])
             pairs = rounded[:].rearrange("g u p r -> g u (p r)").bitcast(F32)
@@ -172,6 +170,7 @@ def tile_attend_deform_kernel(tc, xT, w, part, offs, out):
             banks.append(first["bank"])
 
         addends = {}
+        halves = {}
 
         def lift(dst, i, u, j):
             planes = words[i, u][:].bitcast(F32).rearrange("p (q g h) -> p q g h", q=4, h=2)
@@ -183,12 +182,14 @@ def tile_attend_deform_kernel(tc, xT, w, part, offs, out):
         def weigh(i, windows=(0, 1)):
             k = i % BATCHES
             own = CORNERS
-            if i == 1 and (1 in addends):
-                prod = addends[1][0]
+            if i == 1:
+                u = windows[0]
+                halves[u] = keep.tile([P, CORNERS, 1, 2, P], F32, name=("prod1", staging_name(1, 1, 0))[u], align_bytes=64)
+                prod = halves[u]
             elif i <= 2:
-                prod = keep.tile([P, CORNERS, 2, 2, P], F32, name="prod1" if i == 1 else staging_name(1, 1, 0), align_bytes=64)
+                prod = keep.tile([P, CORNERS, 2, 2, P], F32, name=staging_name(1, 1, 1), align_bytes=64)
             else:
-                prod = prod_pool.tile([P, CORNERS, 2, 2, P], F32, name="prod", align_bytes=64)
+                prod = keep.tile([P, CORNERS, 2, 2, P], F32, name=(staging_name(1, 1, 2), "prod_a", "prod_b")[i % 3], align_bytes=64)
             flat = prod[:].rearrange("g j u r p -> g (j u r p)")
             left = list(range(own))
             addends[i] = (prod, left)
@@ -209,12 +210,12 @@ def tile_attend_deform_kernel(tc, xT, w, part, offs, out):
                             src = bank[:, jj, :].bitcast(BF16).rearrange("g (p r) -> g r p", r=2)
                             scale = weights[:, k, 4 * half + jj : 4 * half + jj + 1]
                             if half == 0 or i < LAST:
-                                nc.scalar.activation(prod[:, 4 * half + jj, u, :, :], src, COPY, scale=scale)
+                                nc.scalar.activation(prod[:, 4 * half + jj, 0, :, :], src, COPY, scale=scale)
                             else:
                                 weigh_and_add(prod[:, jj, u, :, :], src, scale)
                 if i == 1:
                     for u in windows:
-                        nc.gpsimd.tensor_tensor(prod[:, 0:4, u, :, :], prod[:, 0:4, u, :, :], prod[:, 4:8, u, :, :], ADD)
+                        nc.gpsimd.tensor_tensor(prod[:, 0:4, 0, :, :], prod[:, 0:4, 0, :, :], prod[:, 4:8, 0, :, :], ADD)
                     for j in range(4, 8):
                         left.remove(j)
                 return
@@ -247,7 +248,8 @@ def tile_attend_deform_kernel(tc, xT, w, part, offs, out):
                 steps = [(t, j) for t in range(4) for j in left]
                 flags = [(j == left[0], j == left[-1]) for t, j in steps]
             for (t, j), (start, stop) in zip(steps, flags):
-                add_turned(turned[:, t, :], prod[:, j, t // 2, t % 2, :], start, stop)
+                src = halves[t // 2][:, j, 0, t % 2, :] if i == 1 else prod[:, j, t // 2, t % 2, :]
+                add_turned(turned[:, t, :], src, start, stop)
             nc.scalar.activation(e_bf[:, i, :, :], turned[:].rearrange("p t g -> p g t"), COPY)
 
         w_scales = keep.tile([P, TAPS, PASSES, CHANNELS], U8, name="w_scales", align_bytes=64)
@@ -263,7 +265,7 @@ def tile_attend_deform_kernel(tc, xT, w, part, offs, out):
         for c in range(CHUNKS):
             cast_chunk(0, 1, c)
         for u in range(2):
-            for i in range(2):
+            for i in range(3):
                 gather(i, u)
         weigh_first()
         if 1:
@@ -276,11 +278,11 @@ def tile_attend_deform_kernel(tc, xT, w, part, offs, out):
             elif i > 0:
                 weigh(i)
             for c in range(CHUNKS):
-                if (1, 1, 2, 3)[c] == i:
+                if (0, 0, 2, 2)[c] == i:
                     cast_chunk(1, 1, c)
             if i == SUM_LAG + 2:
                 place_first()
-            if i + 2 < UNITS:
+            if 2 < i + 2 < UNITS:
                 for u in range(2):
                     gather(i + 2, u)
             if 1 <= i <= TAPS:
@@ -308,8 +310,27 @@ def tile_attend_deform_kernel(tc, xT, w, part, offs, out):
                     src = bank[:, h, u, :].bitcast(BF16).rearrange("g (p r) -> g r p", r=2)
                     if j == 0:
                         nc.vector.tensor_scalar(prod[:, 0, u, :, :], src, scale, None, op0=MULT)
-                    else:
+                    elif j < CORNERS - 1:
                         weigh_and_add(prod[:, 0, u, :, :], src, scale)
+                    else:
+                        nc.vector.scalar_tensor_tensor(
+                            chain_rounded[:, u, :, :],
+                            src.rearrange("g r p -> g p r"),
+                            scale,
+                            prod[:, 0, u, :, :].rearrange("g r p -> g p r"),
+                            op0=MULT,
+                            op1=ADD,
+                        )
+
+        def turn_chain(name):
+            back = psum.tile([P, 2, P], F32, name=name)
+            pairs = chain_rounded[:].rearrange("g u p r -> g u (p r)").bitcast(F32)
+            for u in range(2):
+                nc.tensor.transpose(back[:, u, :], pairs[:, u, :], identity[:])
+            nc.scalar.copy(
+                e_bf[:, LAST - 1, :, :].rearrange("p g t -> p (g t)").bitcast(F32).rearrange("p (g u) -> p g u", u=2),
+                back[:].rearrange("p u g -> p g u"),
+            )
 
         def last_bank(u, half, name):
             prod = addends[LAST][0]
@@ -327,8 +348,9 @@ def tile_attend_deform_kernel(tc, xT, w, part, offs, out):
 
         chained = keep.tile([P, 1, 2, 2, P], F32, name="chained", align_bytes=64)
         addends[LAST - 1] = (chained, [0])
-        closing = prod_pool.tile([P, CORNERS, 2, 2, P], F32, name="prod", align_bytes=64)
+        closing = keep.tile([P, CORNERS, 2, 2, P], F32, name="prod_a", align_bytes=64)
         addends[LAST] = (closing, list(range(4)))
+        chain_rounded = keep.tile([P, 2, P, 2], BF16, name="chain_rounded", align_bytes=64)
         used = {}
         used["q0"] = banks[0]
         chain_bank(0)
@@ -347,7 +369,7 @@ def tile_attend_deform_kernel(tc, xT, w, part, offs, out):
         used["s9"] = next_bank()
         sum_unit(9, used["s9"])
         used["s10"] = again(used["c"])
-        sum_unit(10, used["s10"])
+        turn_chain(used["s10"])
         used["s11"] = next_bank()
         sum_unit(11, used["s11"])
 

@@ -23,12 +23,14 @@ PASSES = FEATURES // 512
 BATCHES = TAPS * POINTS // P
 UNITS = PASSES * BATCHES
 LAST = UNITS - 1
+CHAINED = LAST - 1
 ENTRIES = P * CORNERS
 LIST_COLUMNS = ENTRIES // 16
 CHUNKS = 4
 CHUNK = COLUMNS // CHUNKS
-CORNER = 4 * P
-HELPED = 2
+HALF = CORNERS // 2
+EARLY = 3
+WORD_SETS = 3
 SUM_LAG = 2
 
 
@@ -37,7 +39,6 @@ def tile_attend_deform_kernel(tc, xT, w, part, offs, out):
     with ExitStack() as ctx:
         lists = ctx.enter_context(tc.tile_pool(name="lists", bufs=1))
         keep = ctx.enter_context(tc.tile_pool(name="keep", bufs=1))
-        code_pool = ctx.enter_context(tc.tile_pool(name="codes", bufs=1))
         psum = ctx.enter_context(tc.psum_pool(name="banks", bufs=1))
 
         offsets = lists.tile([P, BATCHES * LIST_COLUMNS], U16, name="offsets")
@@ -49,12 +50,12 @@ def tile_attend_deform_kernel(tc, xT, w, part, offs, out):
             return f"staged{s}{u}{c}"
 
         def load_window(s, u, chunks=range(CHUNKS)):
+            span = 1 if s == 0 else 2
             for c in chunks:
                 if c == 0:
                     tables[s, u] = keep.tile([P, COLUMNS], F32, name=f"table{s}{u}", align_bytes=64)
-                wide = (1, 2, 2, 2)[2 * s + u]
-                if c % wide == 0:
-                    run = slice(c * CHUNK, (c + wide) * CHUNK)
+                if c % span == 0:
+                    run = slice(c * CHUNK, (c + span) * CHUNK)
                     nc.sync.dma_start(tables[s, u][:, run], x_view[s, u, :, 1, run])
                 raw = keep.tile([P, CHUNK], F32, name=staging_name(s, u, c), align_bytes=64)
                 nc.sync.dma_start(raw[:], x_view[s, u, :, 0, c * CHUNK : (c + 1) * CHUNK])
@@ -76,12 +77,12 @@ def tile_attend_deform_kernel(tc, xT, w, part, offs, out):
         load_window(0, 1)
         nc.sync.dma_start(weights[:, 1:, :], part_view[:, 1:, :])
         load_window(1, 0)
-        load_window(1, 1, range(2))
+        load_window(1, 1, range(CHUNKS // 2))
         w_raw = keep.tile([P, TAPS, PASSES, 4, CHANNELS], F32, name="w_raw")
         w_view = w.rearrange("o (s p t) m -> o p s t m", s=PASSES, t=4)
         for o in range(TAPS):
             nc.sync.dma_start(w_raw[:, o, :, :, :], w_view[o])
-        load_window(1, 1, range(2, CHUNKS))
+        load_window(1, 1, range(CHUNKS // 2, CHUNKS))
 
         identity = keep.tile([P, P], F32, name="identity")
         make_identity(nc, identity[:])
@@ -90,34 +91,33 @@ def tile_attend_deform_kernel(tc, xT, w, part, offs, out):
         word_names = {}
 
         def gather(i, u):
-            if (i, u) == (3, 0):
+            if (i, u) == (EARLY, 0):
                 name = staging_name(0, 1, CHUNKS - 1)
-            elif (i, u) == (4, 0):
+            elif (i, u) == (EARLY + 1, 0):
                 name = staging_name(1, 0, 0)
-            elif i < 4:
+            elif i <= EARLY:
                 name = f"words{i}{u}"
             else:
-                name = word_names[i - 3, u]
+                name = word_names[i - WORD_SETS, u]
             word_names[i, u] = name
             s, k = divmod(i, BATCHES)
             got = keep.tile([P, ENTRIES], U32, name=name, align_bytes=64)
-            window = tables[s, u][:].bitcast(U32)
             nc.vector.tensor_copy(
                 got[:].rearrange("p (q g h) -> p g q h", q=4, h=2),
-                window.indirect(offsets[:, k * LIST_COLUMNS : (k + 1) * LIST_COLUMNS]),
+                tables[s, u][:].bitcast(U32).indirect(offsets[:, k * LIST_COLUMNS : (k + 1) * LIST_COLUMNS]),
             )
             words[i, u] = got
 
         banks = [f"bank{n}" for n in range(8)]
 
-        def next_bank():
-            name = banks[0]
+        def take_bank(name=None):
+            name = name or banks[0]
             banks.remove(name)
             banks.append(name)
             return name
 
         def held_bank():
-            name = next_bank()
+            name = banks[0]
             banks.remove(name)
             return name
 
@@ -127,16 +127,29 @@ def tile_attend_deform_kernel(tc, xT, w, part, offs, out):
         e_bf = keep.tile([P, UNITS, P, 4], BF16, name="e_bf", align_bytes=64)
         e_scales = keep.tile([P, UNITS, P], U8, name="e_scales", align_bytes=64)
 
+        def turn_back(rounded, bank_name):
+            back = psum.tile([P, 2, P], F32, name=bank_name)
+            pairs = rounded[:].rearrange("g u p r -> g u (p r)").bitcast(F32)
+            for u in range(2):
+                nc.tensor.transpose(back[:, u, :], pairs[:, u, :], identity[:])
+            return back
+
+        def place(i, back):
+            nc.scalar.copy(
+                e_bf[:, i, :, :].rearrange("p g t -> p (g t)").bitcast(F32).rearrange("p (g u) -> p g u", u=2),
+                back[:].rearrange("p u g -> p g u"),
+            )
+
         first = {}
 
         def spread_weights():
             first["spread"] = keep.tile([P, CORNERS, P], F32, name="spread")
             for half in range(2):
-                bank = psum.tile([P, 4, P], F32, name=next_bank())
-                for jj in range(4):
-                    j = 4 * half + jj
+                bank = psum.tile([P, HALF, P], F32, name=take_bank())
+                for jj in range(HALF):
+                    j = HALF * half + jj
                     nc.tensor.transpose(bank[:, jj, :], weights[:, 0, j : j + 1].to_broadcast([P, P]), identity[:])
-                nc.scalar.copy(first["spread"][:, 4 * half : 4 * half + 4, :], bank[:])
+                nc.scalar.copy(first["spread"][:, HALF * half : HALF * (half + 1), :], bank[:])
 
         def weigh_first():
             first["bank"] = held_bank()
@@ -157,221 +170,153 @@ def tile_attend_deform_kernel(tc, xT, w, part, offs, out):
         def round_first():
             rounded = keep.tile([P, 2, P, 2], BF16, name=staging_name(1, 1, 0), align_bytes=64)
             nc.scalar.activation(rounded[:], first["sums"][:].rearrange("g u r p -> g u p r"), COPY)
-            first["back"] = psum.tile([P, 2, P], F32, name=first["bank"])
-            pairs = rounded[:].rearrange("g u p r -> g u (p r)").bitcast(F32)
-            for u in range(2):
-                nc.tensor.transpose(first["back"][:, u, :], pairs[:, u, :], identity[:])
+            first["back"] = turn_back(rounded, first["bank"])
 
         def place_first():
-            nc.scalar.copy(
-                e_bf[:, 0, :, :].rearrange("p g t -> p (g t)").bitcast(F32).rearrange("p (g u) -> p g u", u=2),
-                first["back"][:].rearrange("p u g -> p g u"),
-            )
+            place(0, first["back"])
             banks.append(first["bank"])
 
         addends = {}
-        halves = {}
 
         def lift(dst, i, u, j):
             planes = words[i, u][:].bitcast(F32).rearrange("p (q g h) -> p q g h", q=4, h=2)
             nc.tensor.transpose(dst, planes[:, j // 2, :, j % 2], identity[:])
 
+        def weight(i, j):
+            return weights[:, i % BATCHES, j : j + 1]
+
+        def lift_half(i, u, half, bank_name):
+            bank = psum.tile([P, HALF, P], F32, name=bank_name)
+            for jj in range(HALF):
+                lift(bank[:, jj, :], i, u, HALF * half + jj)
+            return [bank[:, jj, :].bitcast(BF16).rearrange("g (p r) -> g r p", r=2) for jj in range(HALF)]
+
+        def lift_pair(i, q):
+            bank = psum.tile([P, 2, 2, P], F32, name=take_bank())
+            for u in (1, 0):
+                for h in range(2):
+                    lift(bank[:, h, u, :], i, u, 2 * q + h)
+            return [bank[:, h, :, :].bitcast(BF16).rearrange("g u (p r) -> g u r p", r=2) for h in range(2)]
+
         def weigh_and_add(dst, src, scale):
             nc.vector.scalar_tensor_tensor(dst, src, scale, dst, op0=MULT, op1=ADD)
 
-        def weigh(i, windows=(0, 1)):
-            k = i % BATCHES
-            own = CORNERS
-            if i == 1:
-                u = windows[0]
-                halves[u] = keep.tile([P, CORNERS, 1, 2, P], F32, name=("prod1", staging_name(1, 1, 0))[u], align_bytes=64)
-                prod = halves[u]
-            elif i <= 2:
-                prod = keep.tile([P, CORNERS, 2, 2, P], F32, name=staging_name(1, 1, 1), align_bytes=64)
-            else:
-                prod = keep.tile([P, CORNERS, 2, 2, P], F32, name=(staging_name(1, 1, 2), "prod_a", "prod_b")[i % 3], align_bytes=64)
-            flat = prod[:].rearrange("g j u r p -> g (j u r p)")
-            left = list(range(own))
-            addends[i] = (prod, left)
+        def weigh_second(u):
+            prod = keep.tile([P, CORNERS, 2, P], F32, name=("prod1", staging_name(1, 1, 0))[u], align_bytes=64)
+            for half in range(2):
+                for jj, src in enumerate(lift_half(1, u, half, take_bank())):
+                    j = HALF * half + jj
+                    nc.scalar.activation(prod[:, j, :, :], src, COPY, scale=weight(1, j))
+            if u == 1:
+                nc.gpsimd.tensor_tensor(prod[:, :HALF, :, :], prod[:, :HALF, :, :], prod[:, HALF:, :, :], ADD)
+            addends.setdefault(1, {})[u] = (prod, range(HALF if u == 1 else CORNERS))
 
-            def add_corners(onto, taken, n):
-                dst = flat[:, CORNER * onto : CORNER * (onto + n)]
-                nc.gpsimd.tensor_tensor(dst, dst, flat[:, CORNER * taken : CORNER * (taken + n)], ADD)
-                for j in range(taken, taken + n):
-                    left.remove(j)
-
-            if i == LAST or (i == 1 and 1):
-                for u in windows:
-                    for half in range(2):
-                        bank = psum.tile([P, 4, P], F32, name=next_bank())
-                        for jj in range(4):
-                            lift(bank[:, jj, :], i, u, 4 * half + jj)
-                        for jj in range(4):
-                            src = bank[:, jj, :].bitcast(BF16).rearrange("g (p r) -> g r p", r=2)
-                            scale = weights[:, k, 4 * half + jj : 4 * half + jj + 1]
-                            if half == 0 or i < LAST:
-                                nc.scalar.activation(prod[:, 4 * half + jj, 0, :, :], src, COPY, scale=scale)
-                            else:
-                                weigh_and_add(prod[:, jj, u, :, :], src, scale)
-                if i == 1:
-                    for u in windows:
-                        nc.gpsimd.tensor_tensor(prod[:, 0:4, 0, :, :], prod[:, 0:4, 0, :, :], prod[:, 4:8, 0, :, :], ADD)
-                    for j in range(4, 8):
-                        left.remove(j)
-                return
+        def weigh(i):
+            name = staging_name(1, 1, 1) if i == 2 else (staging_name(1, 1, 2), "prod_a", "prod_b")[i % (SUM_LAG + 1)]
+            prod = keep.tile([P, CORNERS, 2, 2, P], F32, name=name, align_bytes=64)
             for q in range(4):
-                bank = psum.tile([P, 2, 2, P], F32, name=next_bank())
-                for u in (1, 0):
-                    for h in range(2):
-                        lift(bank[:, h, u, :], i, u, 2 * q + h)
-                for h in range(2):
-                    j = 2 * q + h
-                    src = bank[:, h, :, :].bitcast(BF16).rearrange("g u (p r) -> g u r p", r=2)
-                    scale = weights[:, k, j : j + 1]
-                    nc.scalar.activation(prod[:, j, :, :, :], src, COPY, scale=scale)
-                if q == -1 and 4 <= i:
-                    sum_unit(i - SUM_LAG)
-                if q == 1:
-                    add_corners(0, 2, 2)
-                    if i in ():
-                        add_corners(0, 1, 1)
-                elif q == 3:
-                    add_corners(4, 6, 2)
+                for h, src in enumerate(lift_pair(i, q)):
+                    nc.scalar.activation(prod[:, 2 * q + h, :, :, :], src, COPY, scale=weight(i, 2 * q + h))
+                if q % 2 == 1:
+                    onto = prod[:, 2 * q - 2 : 2 * q, :, :, :].rearrange("g j u r p -> g (j u r p)")
+                    taken = prod[:, 2 * q : 2 * q + 2, :, :, :].rearrange("g j u r p -> g (j u r p)")
+                    nc.gpsimd.tensor_tensor(onto, onto, taken, ADD)
+            addends[i] = {u: (prod[:, :, u, :, :], (0, 1, 4, 5)) for u in range(2)}
 
-        def sum_unit(i, name=None):
-            prod, left = addends[i]
-            turned = psum.tile([P, 4, P], F32, name=name or next_bank())
+        def sum_unit(i, bank_name=None):
+            turned = psum.tile([P, 4, P], F32, name=take_bank(bank_name))
             if i == LAST:
-                steps = [(2 * u + r, j) for u in range(2) for j in left for r in range(2)]
+                steps = [(u, r, j) for u, (prod, left) in addends[i].items() for j in left for r in range(2)]
                 flags = [(n == 0, n == len(steps) - 1) for n in range(len(steps))]
             else:
-                steps = [(t, j) for t in range(4) for j in left]
-                flags = [(j == left[0], j == left[-1]) for t, j in steps]
-            for (t, j), (start, stop) in zip(steps, flags):
-                src = halves[t // 2][:, j, 0, t % 2, :] if i == 1 else prod[:, j, t // 2, t % 2, :]
-                add_turned(turned[:, t, :], src, start, stop)
+                steps = [(u, r, j) for u, (prod, left) in addends[i].items() for r in range(2) for j in left]
+                flags = [(j == addends[i][u][1][0], j == addends[i][u][1][-1]) for u, r, j in steps]
+            for (u, r, j), (start, stop) in zip(steps, flags):
+                add_turned(turned[:, 2 * u + r, :], addends[i][u][0][:, j, r, :], start, stop)
             nc.scalar.activation(e_bf[:, i, :, :], turned[:].rearrange("p t g -> p g t"), COPY)
 
         w_scales = keep.tile([P, TAPS, PASSES, CHANNELS], U8, name="w_scales", align_bytes=64)
         w_bf = keep.tile([P, TAPS, PASSES, CHANNELS, 4], BF16, name="w_bf", align_bytes=64)
 
-        def cast_w(o):
+        def round_w(o):
             src = w_raw[:, o, :, :, :].rearrange("p s t m -> p s m t")
             nc.gpsimd.tensor_scalar(w_bf[:, o, :, :, :], src, 1.0, 0.0, op0=MULT, op1=ADD)
 
         spread_weights()
-        for c in range(CHUNKS):
-            cast_chunk(0, 0, c)
-        for c in range(CHUNKS):
-            cast_chunk(0, 1, c)
         for u in range(2):
-            for i in range(3):
+            for c in range(CHUNKS):
+                cast_chunk(0, u, c)
+        for u in range(2):
+            for i in range(EARLY):
                 gather(i, u)
         weigh_first()
-        if 1:
-            weigh(1, (0,))
+        weigh_second(0)
         for c in range(CHUNKS):
             cast_chunk(1, 0, c)
-        for i in range(LAST - 1):
-            if i == 1 and 1:
-                weigh(1, (1,))
-            elif i > 0:
+        for c in range(CHUNKS // 2):
+            cast_chunk(1, 1, c)
+        for i in range(1, CHAINED):
+            if i == 1:
+                weigh_second(1)
+            else:
                 weigh(i)
-            for c in range(CHUNKS):
-                if (0, 0, 2, 2)[c] == i:
+            if i == 2:
+                for c in range(CHUNKS // 2, CHUNKS):
                     cast_chunk(1, 1, c)
             if i == SUM_LAG + 2:
                 place_first()
-            if 2 < i + 2 < UNITS:
-                for u in range(2):
-                    gather(i + 2, u)
-            if 1 <= i <= TAPS:
-                cast_w(i - 1)
+            for u in range(2):
+                gather(i + 2, u)
+            if i <= TAPS:
+                round_w(i - 1)
             if i > SUM_LAG:
                 sum_unit(i - SUM_LAG)
             if i == SUM_LAG + 1:
                 round_first()
-        def again(name):
-            banks.remove(name)
-            banks.append(name)
-            return name
 
-        def chain_bank(q):
-            i = LAST - 1
-            prod = addends[i][0]
-            bank = psum.tile([P, 2, 2, P], F32, name=next_bank())
-            for u in (1, 0):
-                for h in range(2):
-                    lift(bank[:, h, u, :], i, u, 2 * q + h)
-            for h in range(2):
+        chain = keep.tile([P, 2, 2, P], F32, name="chain", align_bytes=64)
+        chain_rounded = keep.tile([P, 2, P, 2], BF16, name="chain_rounded", align_bytes=64)
+        closing = keep.tile([P, HALF, 2, 2, P], F32, name="prod_a", align_bytes=64)
+        addends[LAST] = {u: (closing[:, :, u, :, :], range(HALF)) for u in range(2)}
+
+        def chain_pair(q):
+            for h, src in enumerate(lift_pair(CHAINED, q)):
                 j = 2 * q + h
-                scale = weights[:, i % BATCHES, j : j + 1]
                 for u in range(2):
-                    src = bank[:, h, u, :].bitcast(BF16).rearrange("g (p r) -> g r p", r=2)
                     if j == 0:
-                        nc.vector.tensor_scalar(prod[:, 0, u, :, :], src, scale, None, op0=MULT)
+                        nc.vector.tensor_scalar(chain[:, u, :, :], src[:, u, :, :], weight(CHAINED, j), None, op0=MULT)
                     elif j < CORNERS - 1:
-                        weigh_and_add(prod[:, 0, u, :, :], src, scale)
+                        weigh_and_add(chain[:, u, :, :], src[:, u, :, :], weight(CHAINED, j))
                     else:
                         nc.vector.scalar_tensor_tensor(
                             chain_rounded[:, u, :, :],
-                            src.rearrange("g r p -> g p r"),
-                            scale,
-                            prod[:, 0, u, :, :].rearrange("g r p -> g p r"),
+                            src[:, u, :, :].rearrange("g r p -> g p r"),
+                            weight(CHAINED, j),
+                            chain[:, u, :, :].rearrange("g r p -> g p r"),
                             op0=MULT,
                             op1=ADD,
                         )
 
-        def turn_chain(name):
-            back = psum.tile([P, 2, P], F32, name=name)
-            pairs = chain_rounded[:].rearrange("g u p r -> g u (p r)").bitcast(F32)
-            for u in range(2):
-                nc.tensor.transpose(back[:, u, :], pairs[:, u, :], identity[:])
-            nc.scalar.copy(
-                e_bf[:, LAST - 1, :, :].rearrange("p g t -> p (g t)").bitcast(F32).rearrange("p (g u) -> p g u", u=2),
-                back[:].rearrange("p u g -> p g u"),
-            )
-
-        def last_bank(u, half, name):
-            prod = addends[LAST][0]
-            bank = psum.tile([P, 4, P], F32, name=name)
-            for jj in range(4):
-                lift(bank[:, jj, :], LAST, u, 4 * half + jj)
-            for jj in range(4):
-                src = bank[:, jj, :].bitcast(BF16).rearrange("g (p r) -> g r p", r=2)
-                scale = weights[:, LAST % BATCHES, 4 * half + jj : 4 * half + jj + 1]
+        def close_half(u, half, bank_name=None):
+            bank_name = take_bank(bank_name)
+            for jj, src in enumerate(lift_half(LAST, u, half, bank_name)):
                 if half == 0:
-                    nc.scalar.activation(prod[:, jj, u, :, :], src, COPY, scale=scale)
+                    nc.scalar.activation(closing[:, jj, u, :, :], src, COPY, scale=weight(LAST, jj))
                 else:
-                    weigh_and_add(prod[:, jj, u, :, :], src, scale)
-            return name
+                    weigh_and_add(closing[:, jj, u, :, :], src, weight(LAST, HALF + jj))
+            return bank_name
 
-        chained = keep.tile([P, 1, 2, 2, P], F32, name="chained", align_bytes=64)
-        addends[LAST - 1] = (chained, [0])
-        closing = keep.tile([P, CORNERS, 2, 2, P], F32, name="prod_a", align_bytes=64)
-        addends[LAST] = (closing, list(range(4)))
-        chain_rounded = keep.tile([P, 2, P, 2], BF16, name="chain_rounded", align_bytes=64)
-        used = {}
-        used["q0"] = banks[0]
-        chain_bank(0)
-        used["q1"] = banks[0]
-        chain_bank(1)
-        used["q2"] = banks[0]
-        chain_bank(2)
-        used["s8"] = next_bank()
-        sum_unit(8, used["s8"])
-        used["a"] = last_bank(0, 0, next_bank())
-        used["q3"] = banks[0]
-        chain_bank(3)
-        used["c"] = last_bank(1, 0, next_bank())
-        used["b"] = last_bank(0, 1, next_bank())
-        used["d"] = last_bank(1, 1, again(used["a"]))
-        used["s9"] = next_bank()
-        sum_unit(9, used["s9"])
-        used["s10"] = again(used["c"])
-        turn_chain(used["s10"])
-        used["s11"] = next_bank()
-        sum_unit(11, used["s11"])
+        for q in range(3):
+            chain_pair(q)
+        sum_unit(CHAINED - 2)
+        scalar_bank = [close_half(0, 0)]
+        chain_pair(3)
+        scalar_bank.append(close_half(1, 0))
+        close_half(0, 1)
+        close_half(1, 1, scalar_bank[0])
+        sum_unit(CHAINED - 1)
+        place(CHAINED, turn_back(chain_rounded, take_bank(scalar_bank[1])))
+        sum_unit(LAST)
 
         w_codes = keep.tile([P, TAPS, PASSES, CHANNELS], U32, name=word_names[LAST, 1], align_bytes=64)
         for taps in (slice(0, 2), slice(2, 3)):
@@ -382,8 +327,8 @@ def tile_attend_deform_kernel(tc, xT, w, part, offs, out):
             )
         e_codes = {}
 
-        def quantize_e(lo, hi, pool, name):
-            codes = pool.tile([P, hi - lo, P], U32, name=name, align_bytes=64)
+        def quantize_e(lo, hi, name):
+            codes = keep.tile([P, hi - lo, P], U32, name=name, align_bytes=64)
             for i in range(lo, hi):
                 e_codes[i] = codes[:, i - lo, :]
             nc.vector.quantize_mx(
@@ -410,18 +355,18 @@ def tile_attend_deform_kernel(tc, xT, w, part, offs, out):
             )
 
         def store(b):
-            result = code_pool.tile([P, P], F32, name=f"result{b}")
+            result = keep.tile([P, P], F32, name=f"result{b}")
             nc.vector.tensor_copy(result[:], accs[b][:])
             nc.sync.dma_start(out[:, b * P : (b + 1) * P], result[:])
 
-        quantize_e(0, 8, keep, word_names[LAST, 0])
-        quantize_e(8, 10, code_pool, "codes8")
-        quantize_e(10, 11, code_pool, "codes10")
+        quantize_e(0, 8, word_names[LAST, 0])
+        quantize_e(8, 10, "codes8")
+        quantize_e(10, 11, "codes10")
         for i in range(1, LAST, 2):
             multiply(i)
         for i in range(0, LAST, 2):
             multiply(i)
         store(0)
-        quantize_e(LAST, UNITS, code_pool, "codes11")
+        quantize_e(LAST, UNITS, "codes11")
         multiply(LAST)
         store(1)

@@ -223,10 +223,14 @@ def tile_attend_deform_kernel(tc, xT, w, part, offs, out):
                     nc.gpsimd.tensor_tensor(onto, onto, taken, ADD)
             addends[i] = {u: (prod[:, :, u, :, :], (0, 1, 4, 5)) for u in range(2)}
 
-        def sum_unit(i, bank_name=None):
-            turned = psum.tile([P, 4, P], F32, name=take_bank(bank_name))
-            if i == LAST:
-                steps = [(u, r, j) for u, (prod, left) in addends[i].items() for j in left for r in range(2)]
+        def sum_unit(i):
+            bank_name = take_bank()
+            turned = psum.tile([P, 4, P], F32, name=bank_name)
+            if i >= CHAINED - 1:
+                if i == LAST:
+                    steps = [(u, r, j) for u, (prod, left) in addends[i].items() for j in left for r in range(2)]
+                else:
+                    steps = [(u, r, j) for j in addends[i][0][1] for u in range(2) for r in range(2)]
                 flags = [(n == 0, n == len(steps) - 1) for n in range(len(steps))]
             else:
                 steps = [(u, r, j) for u, (prod, left) in addends[i].items() for r in range(2) for j in left]
@@ -234,6 +238,7 @@ def tile_attend_deform_kernel(tc, xT, w, part, offs, out):
             for (u, r, j), (start, stop) in zip(steps, flags):
                 add_turned(turned[:, 2 * u + r, :], addends[i][u][0][:, j, r, :], start, stop)
             nc.scalar.activation(e_bf[:, i, :, :], turned[:].rearrange("p t g -> p g t"), COPY)
+            return bank_name
 
         w_scales = keep.tile([P, TAPS, PASSES, CHANNELS], U8, name="w_scales", align_bytes=64)
         w_bf = keep.tile([P, TAPS, PASSES, CHANNELS, 4], BF16, name="w_bf", align_bytes=64)
@@ -276,8 +281,8 @@ def tile_attend_deform_kernel(tc, xT, w, part, offs, out):
 
         chain = keep.tile([P, 2, 2, P], F32, name="chain", align_bytes=64)
         chain_rounded = keep.tile([P, 2, P, 2], BF16, name="chain_rounded", align_bytes=64)
-        closing = keep.tile([P, HALF, 2, 2, P], F32, name="prod_a", align_bytes=64)
-        addends[LAST] = {u: (closing[:, :, u, :, :], range(HALF)) for u in range(2)}
+        closing = keep.tile([P, CORNERS, 2, 2, P], F32, name="prod_a", align_bytes=64)
+        addends[LAST] = {1: (closing[:, :, 1, :, :], (0, 1, 4, 5, 6, 7)), 0: (closing[:, :, 0, :, :], range(HALF))}
 
         def chain_pair(q):
             for h, src in enumerate(lift_pair(CHAINED, q)):
@@ -300,39 +305,39 @@ def tile_attend_deform_kernel(tc, xT, w, part, offs, out):
         def close_half(u, half, bank_name=None):
             bank_name = take_bank(bank_name)
             for jj, src in enumerate(lift_half(LAST, u, half, bank_name)):
-                if half == 0:
-                    nc.scalar.activation(closing[:, jj, u, :, :], src, COPY, scale=weight(LAST, jj))
+                j = HALF * half + jj
+                if (u, half) == (0, 1):
+                    weigh_and_add(closing[:, jj, u, :, :], src, weight(LAST, j))
                 else:
-                    weigh_and_add(closing[:, jj, u, :, :], src, weight(LAST, HALF + jj))
+                    nc.scalar.activation(closing[:, j, u, :, :], src, COPY, scale=weight(LAST, j))
+            if (u, half) == (1, 0):
+                nc.gpsimd.tensor_tensor(closing[:, 0:2, u, :, :], closing[:, 0:2, u, :, :], closing[:, 2:4, u, :, :], ADD)
             return bank_name
 
         for q in range(3):
             chain_pair(q)
-        sum_unit(CHAINED - 2)
-        scalar_bank = [close_half(0, 0)]
+        summed_bank = sum_unit(CHAINED - 2)
+        first_bank = close_half(1, 0)
         chain_pair(3)
-        scalar_bank.append(close_half(1, 0))
-        close_half(0, 1)
-        close_half(1, 1, scalar_bank[0])
+        second_bank = close_half(0, 0)
+        close_half(1, 1, summed_bank)
+        close_half(0, 1, first_bank)
         sum_unit(CHAINED - 1)
-        place(CHAINED, turn_back(chain_rounded, take_bank(scalar_bank[1])))
+        place(CHAINED, turn_back(chain_rounded, take_bank(second_bank)))
         sum_unit(LAST)
 
-        w_codes = keep.tile([P, TAPS, PASSES, CHANNELS], U32, name=word_names[LAST, 1], align_bytes=64)
+        w_codes = keep.tile([P, TAPS, PASSES, CHANNELS], U32, name=word_names[LAST, 0], align_bytes=64)
         for taps in (slice(0, 2), slice(2, 3)):
             nc.vector.quantize_mx(
                 out=w_codes[:, taps, :, :].rearrange("p o s m -> p (o s m)").bitcast(FP8X4),
                 scales=w_scales[:, taps, :, :].rearrange("p o s m -> p (o s m)"),
                 in_=w_bf[:, taps, :, :, :].rearrange("p o s m t -> p (o s m t)"),
             )
-        e_codes = {}
+        e_codes = keep.tile([P, UNITS, P], U32, name="chain_rounded", align_bytes=64)
 
-        def quantize_e(lo, hi, name):
-            codes = keep.tile([P, hi - lo, P], U32, name=name, align_bytes=64)
-            for i in range(lo, hi):
-                e_codes[i] = codes[:, i - lo, :]
+        def quantize_e(lo, hi):
             nc.vector.quantize_mx(
-                out=codes[:].rearrange("p n g -> p (n g)").bitcast(FP8X4),
+                out=e_codes[:, lo:hi, :].rearrange("p n g -> p (n g)").bitcast(FP8X4),
                 scales=e_scales[:, lo:hi, :].rearrange("p n g -> p (n g)"),
                 in_=e_bf[:, lo:hi, :, :].rearrange("p n g t -> p (n g t)"),
             )
@@ -348,7 +353,7 @@ def tile_attend_deform_kernel(tc, xT, w, part, offs, out):
                 out=accs[b][:],
                 lhsT=w_codes[:, o, s, :].bitcast(FP8X4),
                 lhsT_scale=w_scales[:, o, s, :],
-                rhs=e_codes[i].bitcast(FP8X4),
+                rhs=e_codes[:, i, :].bitcast(FP8X4),
                 rhs_scale=e_scales[:, i, :],
                 start=(i < 2),
                 stop=(i >= UNITS - 2),
@@ -356,17 +361,17 @@ def tile_attend_deform_kernel(tc, xT, w, part, offs, out):
 
         def store(b):
             result = keep.tile([P, P], F32, name=f"result{b}")
-            nc.vector.tensor_copy(result[:], accs[b][:])
+            if b == 0:
+                nc.scalar.copy(result[:], accs[b][:])
+            else:
+                nc.vector.tensor_copy(result[:], accs[b][:])
             nc.sync.dma_start(out[:, b * P : (b + 1) * P], result[:])
 
-        quantize_e(0, 8, word_names[LAST, 0])
-        quantize_e(8, 10, "codes8")
-        quantize_e(10, 11, "codes10")
-        for i in range(1, LAST, 2):
-            multiply(i)
-        for i in range(0, LAST, 2):
-            multiply(i)
+        for lo, hi in ((0, 4), (4, 8), (8, 10), (10, 11)):
+            quantize_e(lo, hi)
+            for i in range(lo, hi):
+                multiply(i)
         store(0)
-        quantize_e(LAST, UNITS, "codes11")
+        quantize_e(LAST, UNITS)
         multiply(LAST)
         store(1)

@@ -28,9 +28,11 @@ ENTRIES = P * CORNERS
 LIST_COLUMNS = ENTRIES // 16
 CHUNKS = 4
 CHUNK = COLUMNS // CHUNKS
+SHARE = 5 * CHUNK // 8
 HALF = CORNERS // 2
 EARLY = 3
 WORD_SETS = 3
+PLAIN = ((1, 0), (1, 1), (2, 0))
 SUM_LAG = 2
 
 
@@ -64,7 +66,10 @@ def tile_attend_deform_kernel(tc, xT, w, part, offs, out):
         def cast_chunk(s, u, c):
             halves = tables[s, u][:].bitcast(BF16).rearrange("p (c r) -> p c r", r=2)
             dst = halves[:, c * CHUNK : (c + 1) * CHUNK, 0]
-            if (s, u) == (0, 0) and c > 0:
+            if (s, u, c) == (0, 0, CHUNKS - 1):
+                nc.vector.tensor_copy(dst[:, :SHARE], staged[s, u, c][:, :SHARE])
+                nc.scalar.activation(dst[:, SHARE:], staged[s, u, c][:, SHARE:], COPY)
+            elif (s, u) == (0, 0) and c > 0:
                 nc.vector.tensor_copy(dst, staged[s, u, c][:])
             else:
                 nc.scalar.activation(dst, staged[s, u, c][:], COPY)
@@ -103,7 +108,7 @@ def tile_attend_deform_kernel(tc, xT, w, part, offs, out):
             s, k = divmod(i, BATCHES)
             got = keep.tile([P, ENTRIES], U32, name=name, align_bytes=64)
             nc.vector.tensor_copy(
-                got[:].rearrange("p (q g h) -> p g q h", q=4, h=2),
+                got[:] if (i, u) in PLAIN else got[:].rearrange("p (q g h) -> p g q h", q=4, h=2),
                 tables[s, u][:].bitcast(U32).indirect(offsets[:, k * LIST_COLUMNS : (k + 1) * LIST_COLUMNS]),
             )
             words[i, u] = got
@@ -179,7 +184,8 @@ def tile_attend_deform_kernel(tc, xT, w, part, offs, out):
         addends = {}
 
         def lift(dst, i, u, j):
-            planes = words[i, u][:].bitcast(F32).rearrange("p (q g h) -> p q g h", q=4, h=2)
+            order = "p (g q h) -> p q g h" if (i, u) in PLAIN else "p (q g h) -> p q g h"
+            planes = words[i, u][:].bitcast(F32).rearrange(order, q=4, h=2)
             nc.tensor.transpose(dst, planes[:, j // 2, :, j % 2], identity[:])
 
         def weight(i, j):

@@ -23,7 +23,6 @@ PASSES = FEATURES // 512
 BATCHES = TAPS * POINTS // P
 UNITS = PASSES * BATCHES
 LAST = UNITS - 1
-CHAINED = LAST - 1
 ENTRIES = P * CORNERS
 LIST_COLUMNS = ENTRIES // 16
 CHUNKS = 4
@@ -31,9 +30,16 @@ CHUNK = COLUMNS // CHUNKS
 SHARE = 5 * CHUNK // 8
 HALF = CORNERS // 2
 EARLY = 3
-WORD_SETS = 3
-PLAIN = ((1, 0), (1, 1), (2, 0))
+SPREAD = 2
+PLAIN = ()
 SUM_LAG = 2
+SKIP = ()
+HELP = 2
+CHAINED = LAST - 1
+TAIL = CHAINED
+PRODS = ("prod_c", "prod_a", "prod_b")
+GROUPED = 3
+GADDS = 2
 
 
 def tile_attend_deform_kernel(tc, xT, w, part, offs, out):
@@ -51,7 +57,7 @@ def tile_attend_deform_kernel(tc, xT, w, part, offs, out):
         def staging_name(s, u, c):
             return f"staged{s}{u}{c}"
 
-        def load_window(s, u, chunks=range(CHUNKS)):
+        def load_window(s, u, chunks=range(CHUNKS), name=None):
             span = 1 if s == 0 else 2
             for c in chunks:
                 if c == 0:
@@ -59,7 +65,7 @@ def tile_attend_deform_kernel(tc, xT, w, part, offs, out):
                 if c % span == 0:
                     run = slice(c * CHUNK, (c + span) * CHUNK)
                     nc.sync.dma_start(tables[s, u][:, run], x_view[s, u, :, 1, run])
-                raw = keep.tile([P, CHUNK], F32, name=staging_name(s, u, c), align_bytes=64)
+                raw = keep.tile([P, CHUNK], F32, name=name or staging_name(s, u, c), align_bytes=64)
                 nc.sync.dma_start(raw[:], x_view[s, u, :, 0, c * CHUNK : (c + 1) * CHUNK])
                 staged[s, u, c] = raw
 
@@ -78,16 +84,19 @@ def tile_attend_deform_kernel(tc, xT, w, part, offs, out):
         nc.sync.dma_start(offsets[:], offs)
         weights = keep.tile([P, BATCHES, CORNERS], F32, name="weights")
         part_view = part[0:1, :].rearrange("one (k g j) -> g (one k) j", g=P, j=CORNERS)
-        nc.scalar.dma_start(weights[:, 0:1, :], part_view[:, 0:1, :])
-        load_window(0, 1)
-        nc.sync.dma_start(weights[:, 1:, :], part_view[:, 1:, :])
-        load_window(1, 0)
-        load_window(1, 1, range(CHUNKS // 2))
-        w_raw = keep.tile([P, TAPS, PASSES, 4, CHANNELS], F32, name="w_raw")
+        nc.scalar.dma_start(weights[:, :SPREAD, :], part_view[:, :SPREAD, :])
+        w_raw = {}
         w_view = w.rearrange("o (s p t) m -> o p s t m", s=PASSES, t=4)
+        load_window(0, 1)
+        nc.sync.dma_start(weights[:, SPREAD : SPREAD + 1, :], part_view[:, SPREAD : SPREAD + 1, :])
+        load_window(1, 0)
+        load_window(1, 1)
         for o in range(TAPS):
-            nc.sync.dma_start(w_raw[:, o, :, :, :], w_view[o])
-        load_window(1, 1, range(CHUNKS // 2, CHUNKS))
+            if o == TAPS - 1:
+                nc.sync.dma_start(weights[:, SPREAD + 1 :, :], part_view[:, SPREAD + 1 :, :])
+            for s in range(PASSES):
+                w_raw[o, s] = keep.tile([P, 4, CHANNELS], F32, name=f"w_raw{o}{s}", align_bytes=64)
+                nc.sync.dma_start(w_raw[o, s][:], w_view[o, :, s])
 
         identity = keep.tile([P, P], F32, name="identity")
         make_identity(nc, identity[:])
@@ -95,15 +104,7 @@ def tile_attend_deform_kernel(tc, xT, w, part, offs, out):
         words = {}
         word_names = {}
 
-        def gather(i, u):
-            if (i, u) == (EARLY, 0):
-                name = staging_name(0, 1, CHUNKS - 1)
-            elif (i, u) == (EARLY + 1, 0):
-                name = staging_name(1, 0, 0)
-            elif i <= EARLY:
-                name = f"words{i}{u}"
-            else:
-                name = word_names[i - WORD_SETS, u]
+        def gather(i, u, name):
             word_names[i, u] = name
             s, k = divmod(i, BATCHES)
             got = keep.tile([P, ENTRIES], U32, name=name, align_bytes=64)
@@ -129,57 +130,69 @@ def tile_attend_deform_kernel(tc, xT, w, part, offs, out):
         def add_turned(dst, src, start, stop):
             nc.tensor.matmul(dst, src, identity[:], start=start, stop=stop, is_transpose=True)
 
-        e_bf = keep.tile([P, UNITS, P, 4], BF16, name="e_bf", align_bytes=64)
+        e_tiles = {}
+
+        def e_bf(lo, hi=None):
+            n = min(lo // 4, 1)
+            if n not in e_tiles:
+                name = "e_bf" if n else "w_raw00"
+                e_tiles[n] = keep.tile([P, UNITS - 4 if n else 4, P, 4], BF16, name=name, align_bytes=64)
+            if hi is None:
+                return e_tiles[n][:, lo - 4 * n, :, :]
+            return e_tiles[n][:, lo - 4 * n : hi - 4 * n, :, :]
+
         e_scales = keep.tile([P, UNITS, P], U8, name="e_scales", align_bytes=64)
 
-        def turn_back(rounded, bank_name):
-            back = psum.tile([P, 2, P], F32, name=bank_name)
-            pairs = rounded[:].rearrange("g u p r -> g u (p r)").bitcast(F32)
-            for u in range(2):
-                nc.tensor.transpose(back[:, u, :], pairs[:, u, :], identity[:])
-            return back
+        spread = {}
+        sum_banks = {}
+        sums = {}
+        backs = {}
 
-        def place(i, back):
-            nc.scalar.copy(
-                e_bf[:, i, :, :].rearrange("p g t -> p (g t)").bitcast(F32).rearrange("p (g u) -> p g u", u=2),
-                back[:].rearrange("p u g -> p g u"),
-            )
-
-        first = {}
-
-        def spread_weights():
-            first["spread"] = keep.tile([P, CORNERS, P], F32, name="spread")
+        def spread_weights(i, name):
+            spread[i] = keep.tile([P, CORNERS, P], F32, name=name, align_bytes=64)
             for half in range(2):
                 bank = psum.tile([P, HALF, P], F32, name=take_bank())
                 for jj in range(HALF):
                     j = HALF * half + jj
-                    nc.tensor.transpose(bank[:, jj, :], weights[:, 0, j : j + 1].to_broadcast([P, P]), identity[:])
-                nc.scalar.copy(first["spread"][:, HALF * half : HALF * (half + 1), :], bank[:])
+                    nc.tensor.transpose(bank[:, jj, :], weights[:, i, j : j + 1].to_broadcast([P, P]), identity[:])
+                nc.scalar.copy(spread[i][:, HALF * half : HALF * (half + 1), :], bank[:])
 
-        def weigh_first():
-            first["bank"] = held_bank()
-            first["sums"] = psum.tile([P, 2, 2, P], F32, name=first["bank"])
+        products = {}
+
+        def weigh_gathered(i, u, r, name):
+            values = words[i, u][:].bitcast(BF16).rearrange("p (q g h r) -> p r q h g", q=4, h=2, r=2)
+            products[i, u, r] = keep.tile([P, CORNERS, P], F32, name=name, align_bytes=64)
+            nc.gpsimd.tensor_tensor(
+                products[i, u, r][:].rearrange("p (q h) g -> p q h g", h=2),
+                values[:, r],
+                spread[i][:].rearrange("p (q h) g -> p q h g", h=2),
+                MULT,
+            )
+
+        def sum_gathered(i, u, r):
+            if i not in sums:
+                sum_banks[i] = held_bank()
+                sums[i] = psum.tile([P, 2, 2, P], F32, name=sum_banks[i])
+            for j in range(CORNERS):
+                add_turned(sums[i][:, u, r, :], products[i, u, r][:, j, :], j == 0, j == CORNERS - 1)
+
+        def round_gathered(i, name):
+            rounded = keep.tile([P, 2, P, 2], BF16, name=name, align_bytes=64)
+            nc.scalar.activation(rounded[:], sums[i][:].rearrange("g u r p -> g u p r"), COPY)
+            turn_back(i, rounded)
+
+        def turn_back(i, rounded):
+            backs[i] = psum.tile([P, 2, P], F32, name=sum_banks[i])
+            pairs = rounded[:].rearrange("g u p r -> g u (p r)").bitcast(F32)
             for u in range(2):
-                values = words[0, u][:].bitcast(BF16).rearrange("p (q g h r) -> p r q h g", q=4, h=2, r=2)
-                for r in range(2):
-                    products = keep.tile([P, CORNERS, P], F32, name=f"first_products{r}")
-                    nc.gpsimd.tensor_tensor(
-                        products[:].rearrange("p (q h) g -> p q h g", h=2),
-                        values[:, r],
-                        first["spread"][:].rearrange("p (q h) g -> p q h g", h=2),
-                        MULT,
-                    )
-                    for j in range(CORNERS):
-                        add_turned(first["sums"][:, u, r, :], products[:, j, :], j == 0, j == CORNERS - 1)
+                nc.tensor.transpose(backs[i][:, u, :], pairs[:, u, :], identity[:])
 
-        def round_first():
-            rounded = keep.tile([P, 2, P, 2], BF16, name=staging_name(1, 1, 0), align_bytes=64)
-            nc.scalar.activation(rounded[:], first["sums"][:].rearrange("g u r p -> g u p r"), COPY)
-            first["back"] = turn_back(rounded, first["bank"])
-
-        def place_first():
-            place(0, first["back"])
-            banks.append(first["bank"])
+        def place(i):
+            nc.scalar.copy(
+                e_bf(i).rearrange("p g t -> p (g t)").bitcast(F32).rearrange("p (g u) -> p g u", u=2),
+                backs[i][:].rearrange("p u g -> p g u"),
+            )
+            banks.append(sum_banks[i])
 
         addends = {}
 
@@ -207,96 +220,135 @@ def tile_attend_deform_kernel(tc, xT, w, part, offs, out):
         def weigh_and_add(dst, src, scale):
             nc.vector.scalar_tensor_tensor(dst, src, scale, dst, op0=MULT, op1=ADD)
 
-        def weigh_second(u):
-            prod = keep.tile([P, CORNERS, 2, P], F32, name=("prod1", staging_name(1, 1, 0))[u], align_bytes=64)
-            for half in range(2):
-                for jj, src in enumerate(lift_half(1, u, half, take_bank())):
-                    j = HALF * half + jj
-                    nc.scalar.activation(prod[:, j, :, :], src, COPY, scale=weight(1, j))
-            if u == 1:
-                nc.gpsimd.tensor_tensor(prod[:, :HALF, :, :], prod[:, :HALF, :, :], prod[:, HALF:, :, :], ADD)
-            addends.setdefault(1, {})[u] = (prod, range(HALF if u == 1 else CORNERS))
+        lifted = {}
+
+        def lift_window(i, u):
+            lifted[i, u] = [src for half in range(2) for src in lift_half(i, u, half, take_bank())]
+
+        def weigh_window(i, u, name):
+            products[i, u] = keep.tile([P, CORNERS, 2, P], F32, name=name, align_bytes=64)
+            for j, src in enumerate(lifted[i, u]):
+                nc.scalar.activation(products[i, u][:, j, :, :], src, COPY, scale=weight(i, j))
+
+        def sum_window(i, u):
+            if u == 0:
+                sum_banks[i] = held_bank()
+                sums[i] = psum.tile([P, 4, P], F32, name=sum_banks[i])
+            for r in range(2):
+                for j in range(CORNERS):
+                    add_turned(sums[i][:, 2 * u + r, :], products[i, u][:, j, r, :], j == 0, j == CORNERS - 1)
+
+        def lift_unit(i):
+            lifted[i] = [lift_pair(i, q) for q in range(4)]
 
         def weigh(i):
-            name = staging_name(1, 1, 1) if i == 2 else (staging_name(1, 1, 2), "prod_a", "prod_b")[i % (SUM_LAG + 1)]
+            name = PRODS[i % 3]
             prod = keep.tile([P, CORNERS, 2, 2, P], F32, name=name, align_bytes=64)
             for q in range(4):
-                for h, src in enumerate(lift_pair(i, q)):
+                for h, src in enumerate(lifted[i][q] if i in lifted else lift_pair(i, q)):
                     nc.scalar.activation(prod[:, 2 * q + h, :, :, :], src, COPY, scale=weight(i, 2 * q + h))
                 if q % 2 == 1:
                     onto = prod[:, 2 * q - 2 : 2 * q, :, :, :].rearrange("g j u r p -> g (j u r p)")
                     taken = prod[:, 2 * q : 2 * q + 2, :, :, :].rearrange("g j u r p -> g (j u r p)")
                     nc.gpsimd.tensor_tensor(onto, onto, taken, ADD)
-            addends[i] = {u: (prod[:, :, u, :, :], (0, 1, 4, 5)) for u in range(2)}
+            addends[i] = {u: prod[:, :, u, :, :] for u in range(2)}
 
-        def sum_unit(i):
-            bank_name = take_bank()
-            turned = psum.tile([P, 4, P], F32, name=bank_name)
-            if i >= CHAINED - 1:
-                if i == LAST:
-                    steps = [(u, r, j) for u, (prod, left) in addends[i].items() for j in left for r in range(2)]
-                else:
-                    steps = [(u, r, j) for j in addends[i][0][1] for u in range(2) for r in range(2)]
-                flags = [(n == 0, n == len(steps) - 1) for n in range(len(steps))]
-            else:
-                steps = [(u, r, j) for u, (prod, left) in addends[i].items() for r in range(2) for j in left]
-                flags = [(j == addends[i][u][1][0], j == addends[i][u][1][-1]) for u, r, j in steps]
-            for (u, r, j), (start, stop) in zip(steps, flags):
-                add_turned(turned[:, 2 * u + r, :], addends[i][u][0][:, j, r, :], start, stop)
-            nc.scalar.activation(e_bf[:, i, :, :], turned[:].rearrange("p t g -> p g t"), COPY)
-            return bank_name
+        def add_up(i, steps, first, last):
+            if first:
+                sum_banks[i] = held_bank()
+                sums[i] = psum.tile([P, 4, P], F32, name=sum_banks[i])
+            for n, (u, r, j) in enumerate(steps):
+                add_turned(sums[i][:, 2 * u + r, :], addends[i][u][:, j, r, :], first and n == 0, last and n == len(steps) - 1)
+            if last:
+                nc.scalar.activation(e_bf(i), sums[i][:].rearrange("p t g -> p g t"), COPY)
+                banks.append(sum_banks[i])
+                return sum_banks[i]
+
+        def sum_half(i, half):
+            steps = [(u, r, HALF * half + h) for h in range(2) for u in range(2) for r in range(2)]
+            return add_up(i, steps, half == 0, half == 1)
 
         w_scales = keep.tile([P, TAPS, PASSES, CHANNELS], U8, name="w_scales", align_bytes=64)
         w_bf = keep.tile([P, TAPS, PASSES, CHANNELS, 4], BF16, name="w_bf", align_bytes=64)
 
         def round_w(o):
-            src = w_raw[:, o, :, :, :].rearrange("p s t m -> p s m t")
-            nc.gpsimd.tensor_scalar(w_bf[:, o, :, :, :], src, 1.0, 0.0, op0=MULT, op1=ADD)
+            for s in range(PASSES):
+                src = w_raw[o, s][:].rearrange("p t m -> p m t")
+                if o < TAPS - 1:
+                    nc.scalar.activation(w_bf[:, o, s], src, COPY)
+                else:
+                    nc.gpsimd.tensor_scalar(w_bf[:, o, s], src, 1.0, 0.0, op0=MULT, op1=ADD)
 
-        spread_weights()
-        for u in range(2):
-            for c in range(CHUNKS):
-                cast_chunk(0, u, c)
-        for u in range(2):
-            for i in range(EARLY):
-                gather(i, u)
-        weigh_first()
-        weigh_second(0)
+        spread_weights(0, "spread")
         for c in range(CHUNKS):
+            cast_chunk(0, 0, c)
+        spread_weights(1, staging_name(0, 0, CHUNKS - 1))
+        for c in range(CHUNKS):
+            cast_chunk(0, 1, c)
+        for i, u in ((0, 0), (2, 0), (1, 0), (2, 1), (0, 1), (1, 1)):
+            gather(i, u, f"words{i}{u}")
+        lift_window(2, 0)
+        for r in range(2):
+            weigh_gathered(0, 0, r, f"first{r}")
+            sum_gathered(0, 0, r)
+        weigh_window(2, 0, "prod2")
+        lift_window(2, 1)
+        for c in range(3):
             cast_chunk(1, 0, c)
-        for c in range(CHUNKS // 2):
+        sum_window(2, 0)
+        weigh_gathered(1, 0, 0, staging_name(0, 1, 3))
+        sum_gathered(1, 0, 0)
+        gather(3, 0, staging_name(0, 1, 3))
+        weigh_gathered(1, 0, 1, staging_name(1, 0, 0))
+        sum_gathered(1, 0, 1)
+        weigh_window(2, 1, staging_name(1, 0, 2))
+        cast_chunk(1, 0, 3)
+        sum_window(2, 1)
+        weigh_gathered(0, 1, 0, staging_name(1, 0, 1))
+        sum_gathered(0, 1, 0)
+        weigh_gathered(0, 1, 1, staging_name(1, 0, 3))
+        sum_gathered(0, 1, 1)
+        for c in range(CHUNKS):
             cast_chunk(1, 1, c)
-        for i in range(1, CHAINED):
-            if i == 1:
-                weigh_second(1)
-            else:
-                weigh(i)
-            if i == 2:
-                for c in range(CHUNKS // 2, CHUNKS):
-                    cast_chunk(1, 1, c)
-            if i == SUM_LAG + 2:
-                place_first()
-            for u in range(2):
-                gather(i + 2, u)
-            if i <= TAPS:
-                round_w(i - 1)
-            if i > SUM_LAG:
-                sum_unit(i - SUM_LAG)
-            if i == SUM_LAG + 1:
-                round_first()
+        gather(3, 1, staging_name(1, 1, 0))
+        lift_unit(3)
+        for r in range(2):
+            weigh_gathered(1, 1, r, staging_name(1, 1, 1 + r))
+            sum_gathered(1, 1, r)
+        for o in range(TAPS):
+            round_w(o)
+        nc.scalar.activation(e_bf(2), sums[2][:].rearrange("p t g -> p g t"), COPY)
+        banks.append(sum_banks[2])
+        names = [staging_name(1, 1, 3), "w_raw01", "w_raw11", "w_raw20"]
+        for u in range(2):
+            gather(4, u, names.pop(0))
+        for i in range(3, TAIL):
+            weigh(i)
+            if 0 <= i - 4 < SPREAD:
+                place(i - 4)
+            if i - 3 < SPREAD:
+                round_gathered(i - 3, "w_raw21")
+            if i + 2 <= LAST:
+                for u in range(2):
+                    gather(i + 2, u, names.pop(0) if names else word_names[i, u])
+            if i - 2 >= 3:
+                sum_half(i - 2, 1)
+            if i - 1 >= 3:
+                sum_half(i - 1, 0)
 
         chain = keep.tile([P, 2, 2, P], F32, name="chain", align_bytes=64)
         chain_rounded = keep.tile([P, 2, P, 2], BF16, name="chain_rounded", align_bytes=64)
-        closing = keep.tile([P, CORNERS, 2, 2, P], F32, name="prod_a", align_bytes=64)
-        addends[LAST] = {1: (closing[:, :, 1, :, :], (0, 1, 4, 5, 6, 7)), 0: (closing[:, :, 0, :, :], range(HALF))}
-
-        def chain_pair(q):
-            for h, src in enumerate(lift_pair(CHAINED, q)):
+        closing = keep.tile([P, CORNERS, 2, 2, P], F32, name=PRODS[LAST % 3], align_bytes=64)
+        addends[LAST] = {u: closing[:, :, u, :, :] for u in range(2)}
+        lift_unit(CHAINED)
+        for q in range(4):
+            for h, src in enumerate(lifted[CHAINED][q]):
                 j = 2 * q + h
+                if j == 0:
+                    nc.scalar.activation(chain[:], src, COPY, scale=weight(CHAINED, j))
+                    continue
                 for u in range(2):
-                    if j == 0:
-                        nc.vector.tensor_scalar(chain[:, u, :, :], src[:, u, :, :], weight(CHAINED, j), None, op0=MULT)
-                    elif j < CORNERS - 1:
+                    if j < CORNERS - 1:
                         weigh_and_add(chain[:, u, :, :], src[:, u, :, :], weight(CHAINED, j))
                     else:
                         nc.vector.scalar_tensor_tensor(
@@ -312,25 +364,29 @@ def tile_attend_deform_kernel(tc, xT, w, part, offs, out):
             bank_name = take_bank(bank_name)
             for jj, src in enumerate(lift_half(LAST, u, half, bank_name)):
                 j = HALF * half + jj
-                if (u, half) == (0, 1):
-                    weigh_and_add(closing[:, jj, u, :, :], src, weight(LAST, j))
+                if u == 0 and j >= CORNERS - HELP:
+                    weigh_and_add(closing[:, j - HALF, u, :, :], src, weight(LAST, j))
                 else:
                     nc.scalar.activation(closing[:, j, u, :, :], src, COPY, scale=weight(LAST, j))
-            if (u, half) == (1, 0):
-                nc.gpsimd.tensor_tensor(closing[:, 0:2, u, :, :], closing[:, 0:2, u, :, :], closing[:, 2:4, u, :, :], ADD)
+            if u == 1 and half < GADDS:
+                onto = closing[:, HALF * half : HALF * half + 2, u, :, :]
+                nc.gpsimd.tensor_tensor(onto, onto, closing[:, HALF * half + 2 : HALF * half + 4, u, :, :], ADD)
             return bank_name
 
-        for q in range(3):
-            chain_pair(q)
-        summed_bank = sum_unit(CHAINED - 2)
         first_bank = close_half(1, 0)
-        chain_pair(3)
-        second_bank = close_half(0, 0)
-        close_half(1, 1, summed_bank)
-        close_half(0, 1, first_bank)
-        sum_unit(CHAINED - 1)
-        place(CHAINED, turn_back(chain_rounded, take_bank(second_bank)))
-        sum_unit(LAST)
+        second_bank = sum_half(CHAINED - 2, 1)
+        close_half(1, 1)
+        sum_half(CHAINED - 1, 0)
+        close_half(0, 0, first_bank)
+        close_half(0, 1, second_bank)
+        sum_half(CHAINED - 1, 1)
+        early = [(1, j) for j in ((0, 1) if GADDS == 2 else (4, 5, 6, 7, 0, 1))] + [(0, j) for j in range(HALF - HELP)]
+        late = [(0, j) for j in range(HALF, CORNERS - HELP)] + [(1, j) for j in ((4, 5) if GADDS == 2 else ())] + [(0, j) for j in range(HALF - HELP, HALF)]
+        add_up(LAST, [(u, r, j) for u, j in early for r in range(2)], True, False)
+        sum_banks[CHAINED] = held_bank()
+        turn_back(CHAINED, chain_rounded)
+        place(CHAINED)
+        add_up(LAST, [(u, r, j) for u, j in late for r in range(2)], False, True)
 
         w_codes = keep.tile([P, TAPS, PASSES, CHANNELS], U32, name=word_names[LAST, 0], align_bytes=64)
         for taps in (slice(0, 2), slice(2, 3)):
@@ -345,7 +401,7 @@ def tile_attend_deform_kernel(tc, xT, w, part, offs, out):
             nc.vector.quantize_mx(
                 out=e_codes[:, lo:hi, :].rearrange("p n g -> p (n g)").bitcast(FP8X4),
                 scales=e_scales[:, lo:hi, :].rearrange("p n g -> p (n g)"),
-                in_=e_bf[:, lo:hi, :, :].rearrange("p n g t -> p (n g t)"),
+                in_=e_bf(lo, hi).rearrange("p n g t -> p (n g t)"),
             )
 
         accs = {}

@@ -31,15 +31,17 @@ SHARE = 5 * CHUNK // 8
 HALF = CORNERS // 2
 EARLY = 3
 SPREAD = 2
-PLAIN = ()
+PLAIN = ((2, 0),)
 SUM_LAG = 2
 SKIP = ()
-HELP = 2
+HELP = 4
 CHAINED = LAST - 1
 TAIL = CHAINED
 PRODS = ("prod_c", "prod_a", "prod_b")
 GROUPED = 3
 GADDS = 2
+START = "V"
+OWN = False
 
 
 def tile_attend_deform_kernel(tc, xT, w, part, offs, out):
@@ -84,7 +86,8 @@ def tile_attend_deform_kernel(tc, xT, w, part, offs, out):
         nc.sync.dma_start(offsets[:], offs)
         weights = keep.tile([P, BATCHES, CORNERS], F32, name="weights")
         part_view = part[0:1, :].rearrange("one (k g j) -> g (one k) j", g=P, j=CORNERS)
-        nc.scalar.dma_start(weights[:, :SPREAD, :], part_view[:, :SPREAD, :])
+        nc.scalar.dma_start(weights[:, 0:1, :], part_view[:, 0:1, :])
+        nc.sync.dma_start(weights[:, 1:SPREAD, :], part_view[:, 1:SPREAD, :])
         w_raw = {}
         w_view = w.rearrange("o (s p t) m -> o p s t m", s=PASSES, t=4)
         load_window(0, 1)
@@ -247,7 +250,7 @@ def tile_attend_deform_kernel(tc, xT, w, part, offs, out):
             for q in range(4):
                 for h, src in enumerate(lifted[i][q] if i in lifted else lift_pair(i, q)):
                     nc.scalar.activation(prod[:, 2 * q + h, :, :, :], src, COPY, scale=weight(i, 2 * q + h))
-                if q % 2 == 1:
+                if q % 2 == 1 and (i, q // 2) not in SKIP:
                     onto = prod[:, 2 * q - 2 : 2 * q, :, :, :].rearrange("g j u r p -> g (j u r p)")
                     taken = prod[:, 2 * q : 2 * q + 2, :, :, :].rearrange("g j u r p -> g (j u r p)")
                     nc.gpsimd.tensor_tensor(onto, onto, taken, ADD)
@@ -265,7 +268,7 @@ def tile_attend_deform_kernel(tc, xT, w, part, offs, out):
                 return sum_banks[i]
 
         def sum_half(i, half):
-            steps = [(u, r, HALF * half + h) for h in range(2) for u in range(2) for r in range(2)]
+            steps = [(u, r, HALF * half + h) for h in range(HALF if (i, half) in SKIP else 2) for u in range(2) for r in range(2)]
             return add_up(i, steps, half == 0, half == 1)
 
         w_scales = keep.tile([P, TAPS, PASSES, CHANNELS], U8, name="w_scales", align_bytes=64)
@@ -295,9 +298,9 @@ def tile_attend_deform_kernel(tc, xT, w, part, offs, out):
         lift_window(2, 1)
         for c in range(3):
             cast_chunk(1, 0, c)
-        sum_window(2, 0)
         weigh_gathered(1, 0, 0, staging_name(0, 1, 3))
         sum_gathered(1, 0, 0)
+        sum_window(2, 0)
         gather(3, 0, staging_name(0, 1, 3))
         weigh_gathered(1, 0, 1, staging_name(1, 0, 0))
         sum_gathered(1, 0, 1)
@@ -319,7 +322,7 @@ def tile_attend_deform_kernel(tc, xT, w, part, offs, out):
             round_w(o)
         nc.scalar.activation(e_bf(2), sums[2][:].rearrange("p t g -> p g t"), COPY)
         banks.append(sum_banks[2])
-        names = [staging_name(1, 1, 3), "w_raw01", "w_raw11", "w_raw20"]
+        names = [staging_name(1, 1, 3), "w_raw01", "w_raw10", "w_raw11"]
         for u in range(2):
             gather(4, u, names.pop(0))
         for i in range(3, TAIL):
@@ -327,7 +330,7 @@ def tile_attend_deform_kernel(tc, xT, w, part, offs, out):
             if 0 <= i - 4 < SPREAD:
                 place(i - 4)
             if i - 3 < SPREAD:
-                round_gathered(i - 3, "w_raw21")
+                round_gathered(i - 3, "w_raw20")
             if i + 2 <= LAST:
                 for u in range(2):
                     gather(i + 2, u, names.pop(0) if names else word_names[i, u])
@@ -344,11 +347,13 @@ def tile_attend_deform_kernel(tc, xT, w, part, offs, out):
         for q in range(4):
             for h, src in enumerate(lifted[CHAINED][q]):
                 j = 2 * q + h
-                if j == 0:
+                if j == 0 and START == "S":
                     nc.scalar.activation(chain[:], src, COPY, scale=weight(CHAINED, j))
                     continue
                 for u in range(2):
-                    if j < CORNERS - 1:
+                    if j == 0:
+                        nc.vector.tensor_scalar(chain[:, u, :, :], src[:, u, :, :], weight(CHAINED, j), None, op0=MULT)
+                    elif j < CORNERS - 1:
                         weigh_and_add(chain[:, u, :, :], src[:, u, :, :], weight(CHAINED, j))
                     else:
                         nc.vector.scalar_tensor_tensor(
@@ -365,7 +370,12 @@ def tile_attend_deform_kernel(tc, xT, w, part, offs, out):
             for jj, src in enumerate(lift_half(LAST, u, half, bank_name)):
                 j = HALF * half + jj
                 if u == 0 and j >= CORNERS - HELP:
-                    weigh_and_add(closing[:, j - HALF, u, :, :], src, weight(LAST, j))
+                    if not OWN:
+                        weigh_and_add(closing[:, j - HALF, u, :, :], src, weight(LAST, j))
+                    elif j < CORNERS - HELP + 2:
+                        nc.vector.tensor_scalar(closing[:, j, u, :, :], src, weight(LAST, j), None, op0=MULT)
+                    else:
+                        weigh_and_add(closing[:, CORNERS - HELP + (j - CORNERS + HELP) % 2, u, :, :], src, weight(LAST, j))
                 else:
                     nc.scalar.activation(closing[:, j, u, :, :], src, COPY, scale=weight(LAST, j))
             if u == 1 and half < GADDS:
@@ -380,8 +390,13 @@ def tile_attend_deform_kernel(tc, xT, w, part, offs, out):
         close_half(0, 0, first_bank)
         close_half(0, 1, second_bank)
         sum_half(CHAINED - 1, 1)
-        early = [(1, j) for j in ((0, 1) if GADDS == 2 else (4, 5, 6, 7, 0, 1))] + [(0, j) for j in range(HALF - HELP)]
-        late = [(0, j) for j in range(HALF, CORNERS - HELP)] + [(1, j) for j in ((4, 5) if GADDS == 2 else ())] + [(0, j) for j in range(HALF - HELP, HALF)]
+        early = [(1, j) for j in ((0, 1) if GADDS == 2 else (4, 5, 6, 7, 0, 1))]
+        late = [(1, j) for j in ((4, 5) if GADDS == 2 else ())]
+        if OWN:
+            late = late + [(0, j) for j in range(CORNERS - HELP + 2)]
+        else:
+            early = early + [(0, j) for j in range(HALF - HELP)]
+            late = [(0, j) for j in range(HALF, CORNERS - HELP)] + late + [(0, j) for j in range(HALF - HELP, HALF)]
         add_up(LAST, [(u, r, j) for u, j in early for r in range(2)], True, False)
         sum_banks[CHAINED] = held_bank()
         turn_back(CHAINED, chain_rounded)
@@ -389,12 +404,14 @@ def tile_attend_deform_kernel(tc, xT, w, part, offs, out):
         add_up(LAST, [(u, r, j) for u, j in late for r in range(2)], False, True)
 
         w_codes = keep.tile([P, TAPS, PASSES, CHANNELS], U32, name=word_names[LAST, 0], align_bytes=64)
-        for taps in (slice(0, 2), slice(2, 3)):
+
+        def quantize_w(taps):
             nc.vector.quantize_mx(
                 out=w_codes[:, taps, :, :].rearrange("p o s m -> p (o s m)").bitcast(FP8X4),
                 scales=w_scales[:, taps, :, :].rearrange("p o s m -> p (o s m)"),
                 in_=w_bf[:, taps, :, :, :].rearrange("p o s m t -> p (o s m t)"),
             )
+
         e_codes = keep.tile([P, UNITS, P], U32, name="chain_rounded", align_bytes=64)
 
         def quantize_e(lo, hi):
@@ -430,6 +447,8 @@ def tile_attend_deform_kernel(tc, xT, w, part, offs, out):
             nc.sync.dma_start(out[:, b * P : (b + 1) * P], result[:])
 
         for lo, hi in ((0, 4), (4, 8), (8, 10), (10, 11)):
+            if lo < BATCHES:
+                quantize_w(slice(lo // 2, min(hi // 2, TAPS)))
             quantize_e(lo, hi)
             for i in range(lo, hi):
                 multiply(i)

@@ -34,7 +34,7 @@ SPREAD = 2
 PLAIN = ((2, 0),)
 SUM_LAG = 2
 SKIP = ()
-HELP = 4
+HELP = 2
 CHAINED = LAST - 1
 TAIL = CHAINED
 PRODS = ("prod_c", "prod_a", "prod_b")
@@ -42,6 +42,7 @@ GROUPED = 3
 GADDS = 2
 START = "V"
 OWN = False
+THIRD = (8,)
 
 
 def tile_attend_deform_kernel(tc, xT, w, part, offs, out):
@@ -207,11 +208,14 @@ def tile_attend_deform_kernel(tc, xT, w, part, offs, out):
         def weight(i, j):
             return weights[:, i % BATCHES, j : j + 1]
 
+        def lift_some(i, u, corners, bank_name):
+            bank = psum.tile([P, len(corners), P], F32, name=bank_name)
+            for jj, j in enumerate(corners):
+                lift(bank[:, jj, :], i, u, j)
+            return [bank[:, jj, :].bitcast(BF16).rearrange("g (p r) -> g r p", r=2) for jj in range(len(corners))]
+
         def lift_half(i, u, half, bank_name):
-            bank = psum.tile([P, HALF, P], F32, name=bank_name)
-            for jj in range(HALF):
-                lift(bank[:, jj, :], i, u, HALF * half + jj)
-            return [bank[:, jj, :].bitcast(BF16).rearrange("g (p r) -> g r p", r=2) for jj in range(HALF)]
+            return lift_some(i, u, range(HALF * half, HALF * (half + 1)), bank_name)
 
         def lift_pair(i, q):
             bank = psum.tile([P, 2, 2, P], F32, name=take_bank())
@@ -322,15 +326,16 @@ def tile_attend_deform_kernel(tc, xT, w, part, offs, out):
             round_w(o)
         nc.scalar.activation(e_bf(2), sums[2][:].rearrange("p t g -> p g t"), COPY)
         banks.append(sum_banks[2])
-        names = [staging_name(1, 1, 3), "w_raw01", "w_raw10", "w_raw11"]
+        round_gathered(0, "w_raw11")
+        names = [staging_name(1, 1, 3), "w_raw01", "w_raw10", "w_raw20"]
         for u in range(2):
             gather(4, u, names.pop(0))
         for i in range(3, TAIL):
             weigh(i)
-            if 0 <= i - 4 < SPREAD:
-                place(i - 4)
             if i - 3 < SPREAD:
-                round_gathered(i - 3, "w_raw20")
+                place(i - 3)
+            if i == 3:
+                round_gathered(1, "w_raw11")
             if i + 2 <= LAST:
                 for u in range(2):
                     gather(i + 2, u, names.pop(0) if names else word_names[i, u])
@@ -388,15 +393,21 @@ def tile_attend_deform_kernel(tc, xT, w, part, offs, out):
         close_half(1, 1)
         sum_half(CHAINED - 1, 0)
         close_half(0, 0, first_bank)
-        close_half(0, 1, second_bank)
+        own = range(HALF, CORNERS - HELP)
+        if HELP < HALF:
+            for j, src in zip(own, lift_some(LAST, 0, own, take_bank(second_bank))):
+                nc.scalar.activation(closing[:, j, 0, :, :], src, COPY, scale=weight(LAST, j))
+        helped = range(CORNERS - HELP, CORNERS)
+        for j, src in zip(helped, lift_some(LAST, 0, helped, take_bank(None if HELP < HALF else second_bank))):
+            weigh_and_add(closing[:, j - CORNERS + HELP, 0, :, :], src, weight(LAST, j))
         sum_half(CHAINED - 1, 1)
         early = [(1, j) for j in ((0, 1) if GADDS == 2 else (4, 5, 6, 7, 0, 1))]
         late = [(1, j) for j in ((4, 5) if GADDS == 2 else ())]
         if OWN:
             late = late + [(0, j) for j in range(CORNERS - HELP + 2)]
         else:
-            early = early + [(0, j) for j in range(HALF - HELP)]
-            late = [(0, j) for j in range(HALF, CORNERS - HELP)] + late + [(0, j) for j in range(HALF - HELP, HALF)]
+            early = early + [(0, j) for j in range(HELP, HALF)]
+            late = [(0, j) for j in range(HALF, CORNERS - HELP)] + late + [(0, j) for j in range(HELP)]
         add_up(LAST, [(u, r, j) for u, j in early for r in range(2)], True, False)
         sum_banks[CHAINED] = held_bank()
         turn_back(CHAINED, chain_rounded)

@@ -29,20 +29,14 @@ CHUNKS = 4
 CHUNK = COLUMNS // CHUNKS
 SHARE = 5 * CHUNK // 8
 HALF = CORNERS // 2
-EARLY = 3
 SPREAD = 2
-PLAIN = ((2, 0),)
-SUM_LAG = 2
-SKIP = ()
-HELP = 2
+SOLO = SPREAD
+STREAM = SOLO + 1
 CHAINED = LAST - 1
-TAIL = CHAINED
-PRODS = ("prod_c", "prod_a", "prod_b")
-GROUPED = 3
-GADDS = 2
-START = "V"
-OWN = False
-THIRD = (8,)
+PLAIN = (SOLO, 0)
+PRODUCTS = ("prod_c", "prod_a", "prod_b")
+HELP = 2
+FIRST_E = 4
 
 
 def tile_attend_deform_kernel(tc, xT, w, part, offs, out):
@@ -60,17 +54,18 @@ def tile_attend_deform_kernel(tc, xT, w, part, offs, out):
         def staging_name(s, u, c):
             return f"staged{s}{u}{c}"
 
-        def load_window(s, u, chunks=range(CHUNKS), name=None):
+        def w_name(o, s):
+            return f"w_raw{o}{s}"
+
+        def load_window(s, u):
             span = 1 if s == 0 else 2
-            for c in chunks:
-                if c == 0:
-                    tables[s, u] = keep.tile([P, COLUMNS], F32, name=f"table{s}{u}", align_bytes=64)
+            tables[s, u] = keep.tile([P, COLUMNS], F32, name=f"table{s}{u}", align_bytes=64)
+            for c in range(CHUNKS):
                 if c % span == 0:
                     run = slice(c * CHUNK, (c + span) * CHUNK)
                     nc.sync.dma_start(tables[s, u][:, run], x_view[s, u, :, 1, run])
-                raw = keep.tile([P, CHUNK], F32, name=name or staging_name(s, u, c), align_bytes=64)
-                nc.sync.dma_start(raw[:], x_view[s, u, :, 0, c * CHUNK : (c + 1) * CHUNK])
-                staged[s, u, c] = raw
+                staged[s, u, c] = keep.tile([P, CHUNK], F32, name=staging_name(s, u, c), align_bytes=64)
+                nc.sync.dma_start(staged[s, u, c][:], x_view[s, u, :, 0, c * CHUNK : (c + 1) * CHUNK])
 
         def cast_chunk(s, u, c):
             halves = tables[s, u][:].bitcast(BF16).rearrange("p (c r) -> p c r", r=2)
@@ -89,17 +84,17 @@ def tile_attend_deform_kernel(tc, xT, w, part, offs, out):
         part_view = part[0:1, :].rearrange("one (k g j) -> g (one k) j", g=P, j=CORNERS)
         nc.scalar.dma_start(weights[:, 0:1, :], part_view[:, 0:1, :])
         nc.sync.dma_start(weights[:, 1:SPREAD, :], part_view[:, 1:SPREAD, :])
-        w_raw = {}
-        w_view = w.rearrange("o (s p t) m -> o p s t m", s=PASSES, t=4)
         load_window(0, 1)
-        nc.sync.dma_start(weights[:, SPREAD : SPREAD + 1, :], part_view[:, SPREAD : SPREAD + 1, :])
+        nc.sync.dma_start(weights[:, SOLO:STREAM, :], part_view[:, SOLO:STREAM, :])
         load_window(1, 0)
         load_window(1, 1)
+        w_raw = {}
+        w_view = w.rearrange("o (s p t) m -> o p s t m", s=PASSES, t=4)
         for o in range(TAPS):
             if o == TAPS - 1:
-                nc.sync.dma_start(weights[:, SPREAD + 1 :, :], part_view[:, SPREAD + 1 :, :])
+                nc.sync.dma_start(weights[:, STREAM:, :], part_view[:, STREAM:, :])
             for s in range(PASSES):
-                w_raw[o, s] = keep.tile([P, 4, CHANNELS], F32, name=f"w_raw{o}{s}", align_bytes=64)
+                w_raw[o, s] = keep.tile([P, 4, CHANNELS], F32, name=w_name(o, s), align_bytes=64)
                 nc.sync.dma_start(w_raw[o, s][:], w_view[o, :, s])
 
         identity = keep.tile([P, P], F32, name="identity")
@@ -111,12 +106,11 @@ def tile_attend_deform_kernel(tc, xT, w, part, offs, out):
         def gather(i, u, name):
             word_names[i, u] = name
             s, k = divmod(i, BATCHES)
-            got = keep.tile([P, ENTRIES], U32, name=name, align_bytes=64)
+            words[i, u] = keep.tile([P, ENTRIES], U32, name=name, align_bytes=64)
             nc.vector.tensor_copy(
-                got[:] if (i, u) in PLAIN else got[:].rearrange("p (q g h) -> p g q h", q=4, h=2),
+                words[i, u][:] if (i, u) == PLAIN else words[i, u][:].rearrange("p (q g h) -> p g q h", q=4, h=2),
                 tables[s, u][:].bitcast(U32).indirect(offsets[:, k * LIST_COLUMNS : (k + 1) * LIST_COLUMNS]),
             )
-            words[i, u] = got
 
         banks = [f"bank{n}" for n in range(8)]
 
@@ -126,7 +120,7 @@ def tile_attend_deform_kernel(tc, xT, w, part, offs, out):
             banks.append(name)
             return name
 
-        def held_bank():
+        def hold_bank():
             name = banks[0]
             banks.remove(name)
             return name
@@ -136,20 +130,24 @@ def tile_attend_deform_kernel(tc, xT, w, part, offs, out):
 
         e_tiles = {}
 
-        def e_bf(lo, hi=None):
-            n = min(lo // 4, 1)
-            if n not in e_tiles:
-                name = "e_bf" if n else "w_raw00"
-                e_tiles[n] = keep.tile([P, UNITS - 4 if n else 4, P, 4], BF16, name=name, align_bytes=64)
-            if hi is None:
-                return e_tiles[n][:, lo - 4 * n, :, :]
-            return e_tiles[n][:, lo - 4 * n : hi - 4 * n, :, :]
+        def e_bf(lo, hi):
+            first = lo < FIRST_E
+            if first not in e_tiles:
+                name, units = (w_name(0, 0), FIRST_E) if first else ("e_bf", UNITS - FIRST_E)
+                e_tiles[first] = keep.tile([P, units, P, 4], BF16, name=name, align_bytes=64)
+            base = 0 if first else FIRST_E
+            return e_tiles[first][:, lo - base : hi - base, :, :]
 
         e_scales = keep.tile([P, UNITS, P], U8, name="e_scales", align_bytes=64)
-
-        spread = {}
         sum_banks = {}
         sums = {}
+
+        def round_sum(i):
+            nc.scalar.activation(e_bf(i, i + 1)[:, 0], sums[i][:].rearrange("p t g -> p g t"), COPY)
+            banks.append(sum_banks[i])
+
+        spread = {}
+        products = {}
         backs = {}
 
         def spread_weights(i, name):
@@ -161,29 +159,20 @@ def tile_attend_deform_kernel(tc, xT, w, part, offs, out):
                     nc.tensor.transpose(bank[:, jj, :], weights[:, i, j : j + 1].to_broadcast([P, P]), identity[:])
                 nc.scalar.copy(spread[i][:, HALF * half : HALF * (half + 1), :], bank[:])
 
-        products = {}
-
         def weigh_gathered(i, u, r, name):
             values = words[i, u][:].bitcast(BF16).rearrange("p (q g h r) -> p r q h g", q=4, h=2, r=2)
-            products[i, u, r] = keep.tile([P, CORNERS, P], F32, name=name, align_bytes=64)
+            planes = keep.tile([P, CORNERS, P], F32, name=name, align_bytes=64)
             nc.gpsimd.tensor_tensor(
-                products[i, u, r][:].rearrange("p (q h) g -> p q h g", h=2),
+                planes[:].rearrange("p (q h) g -> p q h g", h=2),
                 values[:, r],
                 spread[i][:].rearrange("p (q h) g -> p q h g", h=2),
                 MULT,
             )
-
-        def sum_gathered(i, u, r):
             if i not in sums:
-                sum_banks[i] = held_bank()
+                sum_banks[i] = hold_bank()
                 sums[i] = psum.tile([P, 2, 2, P], F32, name=sum_banks[i])
             for j in range(CORNERS):
-                add_turned(sums[i][:, u, r, :], products[i, u, r][:, j, :], j == 0, j == CORNERS - 1)
-
-        def round_gathered(i, name):
-            rounded = keep.tile([P, 2, P, 2], BF16, name=name, align_bytes=64)
-            nc.scalar.activation(rounded[:], sums[i][:].rearrange("g u r p -> g u p r"), COPY)
-            turn_back(i, rounded)
+                add_turned(sums[i][:, u, r, :], planes[:, j, :], j == 0, j == CORNERS - 1)
 
         def turn_back(i, rounded):
             backs[i] = psum.tile([P, 2, P], F32, name=sum_banks[i])
@@ -191,31 +180,34 @@ def tile_attend_deform_kernel(tc, xT, w, part, offs, out):
             for u in range(2):
                 nc.tensor.transpose(backs[i][:, u, :], pairs[:, u, :], identity[:])
 
+        def round_gathered(i, name):
+            rounded = keep.tile([P, 2, P, 2], BF16, name=name, align_bytes=64)
+            nc.scalar.activation(rounded[:], sums[i][:].rearrange("g u r p -> g u p r"), COPY)
+            turn_back(i, rounded)
+
         def place(i):
             nc.scalar.copy(
-                e_bf(i).rearrange("p g t -> p (g t)").bitcast(F32).rearrange("p (g u) -> p g u", u=2),
+                e_bf(i, i + 1)[:, 0].rearrange("p g t -> p (g t)").bitcast(F32).rearrange("p (g u) -> p g u", u=2),
                 backs[i][:].rearrange("p u g -> p g u"),
             )
             banks.append(sum_banks[i])
 
-        addends = {}
-
         def lift(dst, i, u, j):
-            order = "p (g q h) -> p q g h" if (i, u) in PLAIN else "p (q g h) -> p q g h"
+            order = "p (g q h) -> p q g h" if (i, u) == PLAIN else "p (q g h) -> p q g h"
             planes = words[i, u][:].bitcast(F32).rearrange(order, q=4, h=2)
             nc.tensor.transpose(dst, planes[:, j // 2, :, j % 2], identity[:])
 
         def weight(i, j):
             return weights[:, i % BATCHES, j : j + 1]
 
-        def lift_some(i, u, corners, bank_name):
+        def lift_corners(i, u, corners, bank_name):
             bank = psum.tile([P, len(corners), P], F32, name=bank_name)
             for jj, j in enumerate(corners):
                 lift(bank[:, jj, :], i, u, j)
-            return [bank[:, jj, :].bitcast(BF16).rearrange("g (p r) -> g r p", r=2) for jj in range(len(corners))]
+            return [(j, bank[:, jj, :].bitcast(BF16).rearrange("g (p r) -> g r p", r=2)) for jj, j in enumerate(corners)]
 
-        def lift_half(i, u, half, bank_name):
-            return lift_some(i, u, range(HALF * half, HALF * (half + 1)), bank_name)
+        def half_of(half):
+            return range(HALF * half, HALF * (half + 1))
 
         def lift_pair(i, q):
             bank = psum.tile([P, 2, 2, P], F32, name=take_bank())
@@ -229,51 +221,50 @@ def tile_attend_deform_kernel(tc, xT, w, part, offs, out):
 
         lifted = {}
 
-        def lift_window(i, u):
-            lifted[i, u] = [src for half in range(2) for src in lift_half(i, u, half, take_bank())]
+        def lift_window(u):
+            lifted[SOLO, u] = [pair for half in range(2) for pair in lift_corners(SOLO, u, half_of(half), take_bank())]
 
-        def weigh_window(i, u, name):
-            products[i, u] = keep.tile([P, CORNERS, 2, P], F32, name=name, align_bytes=64)
-            for j, src in enumerate(lifted[i, u]):
-                nc.scalar.activation(products[i, u][:, j, :, :], src, COPY, scale=weight(i, j))
+        def weigh_window(u, name):
+            products[SOLO, u] = keep.tile([P, CORNERS, 2, P], F32, name=name, align_bytes=64)
+            for j, src in lifted[SOLO, u]:
+                nc.scalar.activation(products[SOLO, u][:, j, :, :], src, COPY, scale=weight(SOLO, j))
 
-        def sum_window(i, u):
+        def sum_window(u):
             if u == 0:
-                sum_banks[i] = held_bank()
-                sums[i] = psum.tile([P, 4, P], F32, name=sum_banks[i])
+                sum_banks[SOLO] = hold_bank()
+                sums[SOLO] = psum.tile([P, 4, P], F32, name=sum_banks[SOLO])
             for r in range(2):
                 for j in range(CORNERS):
-                    add_turned(sums[i][:, 2 * u + r, :], products[i, u][:, j, r, :], j == 0, j == CORNERS - 1)
+                    add_turned(sums[SOLO][:, 2 * u + r, :], products[SOLO, u][:, j, r, :], j == 0, j == CORNERS - 1)
 
         def lift_unit(i):
             lifted[i] = [lift_pair(i, q) for q in range(4)]
 
         def weigh(i):
-            name = PRODS[i % 3]
-            prod = keep.tile([P, CORNERS, 2, 2, P], F32, name=name, align_bytes=64)
+            prod = keep.tile([P, CORNERS, 2, 2, P], F32, name=PRODUCTS[i % len(PRODUCTS)], align_bytes=64)
             for q in range(4):
                 for h, src in enumerate(lifted[i][q] if i in lifted else lift_pair(i, q)):
                     nc.scalar.activation(prod[:, 2 * q + h, :, :, :], src, COPY, scale=weight(i, 2 * q + h))
-                if q % 2 == 1 and (i, q // 2) not in SKIP:
+                if q % 2 == 1:
                     onto = prod[:, 2 * q - 2 : 2 * q, :, :, :].rearrange("g j u r p -> g (j u r p)")
                     taken = prod[:, 2 * q : 2 * q + 2, :, :, :].rearrange("g j u r p -> g (j u r p)")
                     nc.gpsimd.tensor_tensor(onto, onto, taken, ADD)
-            addends[i] = {u: prod[:, :, u, :, :] for u in range(2)}
+            products[i] = prod
 
-        def add_up(i, steps, first, last):
+        def add_up(i, addends, first, last):
             if first:
-                sum_banks[i] = held_bank()
+                sum_banks[i] = hold_bank()
                 sums[i] = psum.tile([P, 4, P], F32, name=sum_banks[i])
-            for n, (u, r, j) in enumerate(steps):
-                add_turned(sums[i][:, 2 * u + r, :], addends[i][u][:, j, r, :], first and n == 0, last and n == len(steps) - 1)
+            steps = [(u, j, r) for u, j in addends for r in range(2)]
+            for n, (u, j, r) in enumerate(steps):
+                add_turned(
+                    sums[i][:, 2 * u + r, :], products[i][:, j, u, r, :], first and n == 0, last and n == len(steps) - 1
+                )
             if last:
-                nc.scalar.activation(e_bf(i), sums[i][:].rearrange("p t g -> p g t"), COPY)
-                banks.append(sum_banks[i])
-                return sum_banks[i]
+                round_sum(i)
 
         def sum_half(i, half):
-            steps = [(u, r, HALF * half + h) for h in range(HALF if (i, half) in SKIP else 2) for u in range(2) for r in range(2)]
-            return add_up(i, steps, half == 0, half == 1)
+            add_up(i, [(u, HALF * half + h) for h in range(2) for u in range(2)], half == 0, half == 1)
 
         w_scales = keep.tile([P, TAPS, PASSES, CHANNELS], U8, name="w_scales", align_bytes=64)
         w_bf = keep.tile([P, TAPS, PASSES, CHANNELS, 4], BF16, name="w_bf", align_bytes=64)
@@ -281,7 +272,7 @@ def tile_attend_deform_kernel(tc, xT, w, part, offs, out):
         def round_w(o):
             for s in range(PASSES):
                 src = w_raw[o, s][:].rearrange("p t m -> p m t")
-                if o < TAPS - 1:
+                if PASSES * o + s < TAPS * PASSES // 2:
                     nc.scalar.activation(w_bf[:, o, s], src, COPY)
                 else:
                     nc.gpsimd.tensor_scalar(w_bf[:, o, s], src, 1.0, 0.0, op0=MULT, op1=ADD)
@@ -292,69 +283,59 @@ def tile_attend_deform_kernel(tc, xT, w, part, offs, out):
         spread_weights(1, staging_name(0, 0, CHUNKS - 1))
         for c in range(CHUNKS):
             cast_chunk(0, 1, c)
-        for i, u in ((0, 0), (2, 0), (1, 0), (2, 1), (0, 1), (1, 1)):
+        for i, u in ((0, 0), (SOLO, 0), (1, 0), (SOLO, 1), (0, 1), (1, 1)):
             gather(i, u, f"words{i}{u}")
-        lift_window(2, 0)
+        lift_window(0)
         for r in range(2):
             weigh_gathered(0, 0, r, f"first{r}")
-            sum_gathered(0, 0, r)
-        weigh_window(2, 0, "prod2")
-        lift_window(2, 1)
-        for c in range(3):
+        weigh_window(0, "solo")
+        lift_window(1)
+        for c in range(CHUNKS - 1):
             cast_chunk(1, 0, c)
         weigh_gathered(1, 0, 0, staging_name(0, 1, 3))
-        sum_gathered(1, 0, 0)
-        sum_window(2, 0)
-        gather(3, 0, staging_name(0, 1, 3))
+        sum_window(0)
+        gather(STREAM, 0, staging_name(0, 1, 3))
         weigh_gathered(1, 0, 1, staging_name(1, 0, 0))
-        sum_gathered(1, 0, 1)
-        weigh_window(2, 1, staging_name(1, 0, 2))
-        cast_chunk(1, 0, 3)
-        sum_window(2, 1)
+        weigh_window(1, staging_name(1, 0, 2))
+        cast_chunk(1, 0, CHUNKS - 1)
+        sum_window(1)
         weigh_gathered(0, 1, 0, staging_name(1, 0, 1))
-        sum_gathered(0, 1, 0)
         weigh_gathered(0, 1, 1, staging_name(1, 0, 3))
-        sum_gathered(0, 1, 1)
         for c in range(CHUNKS):
             cast_chunk(1, 1, c)
-        gather(3, 1, staging_name(1, 1, 0))
-        lift_unit(3)
+        gather(STREAM, 1, staging_name(1, 1, 0))
+        lift_unit(STREAM)
         for r in range(2):
             weigh_gathered(1, 1, r, staging_name(1, 1, 1 + r))
-            sum_gathered(1, 1, r)
         for o in range(TAPS):
             round_w(o)
-        nc.scalar.activation(e_bf(2), sums[2][:].rearrange("p t g -> p g t"), COPY)
-        banks.append(sum_banks[2])
-        round_gathered(0, "w_raw11")
-        names = [staging_name(1, 1, 3), "w_raw01", "w_raw10", "w_raw20"]
+        round_sum(SOLO)
+        round_gathered(0, w_name(1, 0))
+        freed = [staging_name(1, 1, 3), w_name(0, 1), w_name(1, 1), w_name(2, 0)]
         for u in range(2):
-            gather(4, u, names.pop(0))
-        for i in range(3, TAIL):
+            gather(STREAM + 1, u, freed.pop(0))
+
+        for i in range(STREAM, CHAINED):
             weigh(i)
-            if i - 3 < SPREAD:
-                place(i - 3)
-            if i == 3:
-                round_gathered(1, "w_raw11")
-            if i + 2 <= LAST:
-                for u in range(2):
-                    gather(i + 2, u, names.pop(0) if names else word_names[i, u])
-            if i - 2 >= 3:
+            if i - STREAM < SPREAD:
+                place(i - STREAM)
+            if i == STREAM:
+                round_gathered(1, w_name(1, 0))
+            for u in range(2):
+                gather(i + 2, u, freed.pop(0) if freed else word_names[i, u])
+            if i - 2 >= STREAM:
                 sum_half(i - 2, 1)
-            if i - 1 >= 3:
+            if i - 1 >= STREAM:
                 sum_half(i - 1, 0)
 
         chain = keep.tile([P, 2, 2, P], F32, name="chain", align_bytes=64)
         chain_rounded = keep.tile([P, 2, P, 2], BF16, name="chain_rounded", align_bytes=64)
-        closing = keep.tile([P, CORNERS, 2, 2, P], F32, name=PRODS[LAST % 3], align_bytes=64)
-        addends[LAST] = {u: closing[:, :, u, :, :] for u in range(2)}
+        closing = keep.tile([P, CORNERS, 2, 2, P], F32, name=PRODUCTS[LAST % len(PRODUCTS)], align_bytes=64)
+        products[LAST] = closing
         lift_unit(CHAINED)
         for q in range(4):
             for h, src in enumerate(lifted[CHAINED][q]):
                 j = 2 * q + h
-                if j == 0 and START == "S":
-                    nc.scalar.activation(chain[:], src, COPY, scale=weight(CHAINED, j))
-                    continue
                 for u in range(2):
                     if j == 0:
                         nc.vector.tensor_scalar(chain[:, u, :, :], src[:, u, :, :], weight(CHAINED, j), None, op0=MULT)
@@ -370,49 +351,32 @@ def tile_attend_deform_kernel(tc, xT, w, part, offs, out):
                             op1=ADD,
                         )
 
-        def close_half(u, half, bank_name=None):
-            bank_name = take_bank(bank_name)
-            for jj, src in enumerate(lift_half(LAST, u, half, bank_name)):
-                j = HALF * half + jj
-                if u == 0 and j >= CORNERS - HELP:
-                    if not OWN:
-                        weigh_and_add(closing[:, j - HALF, u, :, :], src, weight(LAST, j))
-                    elif j < CORNERS - HELP + 2:
-                        nc.vector.tensor_scalar(closing[:, j, u, :, :], src, weight(LAST, j), None, op0=MULT)
-                    else:
-                        weigh_and_add(closing[:, CORNERS - HELP + (j - CORNERS + HELP) % 2, u, :, :], src, weight(LAST, j))
-                else:
-                    nc.scalar.activation(closing[:, j, u, :, :], src, COPY, scale=weight(LAST, j))
-            if u == 1 and half < GADDS:
-                onto = closing[:, HALF * half : HALF * half + 2, u, :, :]
-                nc.gpsimd.tensor_tensor(onto, onto, closing[:, HALF * half + 2 : HALF * half + 4, u, :, :], ADD)
+        def close(u, corners, bank_name):
+            for j, src in lift_corners(LAST, u, corners, bank_name):
+                nc.scalar.activation(closing[:, j, u, :, :], src, COPY, scale=weight(LAST, j))
+
+        def close_halved(half):
+            bank_name = take_bank()
+            close(1, half_of(half), bank_name)
+            onto = closing[:, HALF * half : HALF * half + 2, 1, :, :]
+            nc.gpsimd.tensor_tensor(onto, onto, closing[:, HALF * half + 2 : HALF * half + 4, 1, :, :], ADD)
             return bank_name
 
-        first_bank = close_half(1, 0)
-        second_bank = sum_half(CHAINED - 2, 1)
-        close_half(1, 1)
+        first_bank = close_halved(0)
+        sum_half(CHAINED - 2, 1)
+        close_halved(1)
         sum_half(CHAINED - 1, 0)
-        close_half(0, 0, first_bank)
-        own = range(HALF, CORNERS - HELP)
-        if HELP < HALF:
-            for j, src in zip(own, lift_some(LAST, 0, own, take_bank(second_bank))):
-                nc.scalar.activation(closing[:, j, 0, :, :], src, COPY, scale=weight(LAST, j))
-        helped = range(CORNERS - HELP, CORNERS)
-        for j, src in zip(helped, lift_some(LAST, 0, helped, take_bank(None if HELP < HALF else second_bank))):
+        close(0, half_of(0), take_bank(first_bank))
+        close(0, range(HALF, CORNERS - HELP), take_bank(sum_banks[CHAINED - 2]))
+        for j, src in lift_corners(LAST, 0, range(CORNERS - HELP, CORNERS), take_bank()):
             weigh_and_add(closing[:, j - CORNERS + HELP, 0, :, :], src, weight(LAST, j))
         sum_half(CHAINED - 1, 1)
-        early = [(1, j) for j in ((0, 1) if GADDS == 2 else (4, 5, 6, 7, 0, 1))]
-        late = [(1, j) for j in ((4, 5) if GADDS == 2 else ())]
-        if OWN:
-            late = late + [(0, j) for j in range(CORNERS - HELP + 2)]
-        else:
-            early = early + [(0, j) for j in range(HELP, HALF)]
-            late = [(0, j) for j in range(HALF, CORNERS - HELP)] + late + [(0, j) for j in range(HELP)]
-        add_up(LAST, [(u, r, j) for u, j in early for r in range(2)], True, False)
-        sum_banks[CHAINED] = held_bank()
+        add_up(LAST, [(1, 0), (1, 1)] + [(0, j) for j in range(HELP, HALF)], True, False)
+        sum_banks[CHAINED] = hold_bank()
         turn_back(CHAINED, chain_rounded)
         place(CHAINED)
-        add_up(LAST, [(u, r, j) for u, j in late for r in range(2)], False, True)
+        late = [(0, j) for j in range(HALF, CORNERS - HELP)] + [(1, HALF), (1, HALF + 1)] + [(0, j) for j in range(HELP)]
+        add_up(LAST, late, False, True)
 
         w_codes = keep.tile([P, TAPS, PASSES, CHANNELS], U32, name=word_names[LAST, 0], align_bytes=64)
 
@@ -438,7 +402,7 @@ def tile_attend_deform_kernel(tc, xT, w, part, offs, out):
             s, k = divmod(i, BATCHES)
             o, b = divmod(k, 2)
             if i < 2:
-                accs[b] = psum.tile([P, P], F32, name=held_bank())
+                accs[b] = psum.tile([P, P], F32, name=hold_bank())
             nc.tensor.matmul_mx(
                 out=accs[b][:],
                 lhsT=w_codes[:, o, s, :].bitcast(FP8X4),
@@ -457,7 +421,7 @@ def tile_attend_deform_kernel(tc, xT, w, part, offs, out):
                 nc.vector.tensor_copy(result[:], accs[b][:])
             nc.sync.dma_start(out[:, b * P : (b + 1) * P], result[:])
 
-        for lo, hi in ((0, 4), (4, 8), (8, 10), (10, 11)):
+        for lo, hi in ((0, FIRST_E), (FIRST_E, 2 * FIRST_E), (2 * FIRST_E, CHAINED), (CHAINED, LAST)):
             if lo < BATCHES:
                 quantize_w(slice(lo // 2, min(hi // 2, TAPS)))
             quantize_e(lo, hi)

from contextlib import ExitStack

import concourse.mybir as mybir
from concourse.masks import make_identity

TAPS, POINTS, CORNERS, COLUMNS, FEATURES, CHANNELS = 3, 256, 8, 2048, 1024, 128

FLOPS = 2 * TAPS * FEATURES * POINTS * CHANNELS
BYTES = 4 * FEATURES * COLUMNS + 4 * TAPS * FEATURES * CHANNELS + 4 * TAPS * POINTS * CORNERS + 2 * 128 * 384 + 4 * CHANNELS * POINTS

F32 = mybir.dt.float32
BF16 = mybir.dt.bfloat16
U32 = mybir.dt.uint32
U16 = mybir.dt.uint16
U8 = mybir.dt.uint8
FP8X4 = mybir.dt.float8_e4m3fn_x4
COPY = mybir.ActivationFunctionType.Copy
MULT = mybir.AluOpType.mult
ADD = mybir.AluOpType.add

P = 128
PASSES = FEATURES // 512
BATCHES = TAPS * POINTS // P
UNITS = PASSES * BATCHES
LAST = UNITS - 1
ENTRIES = P * CORNERS
LIST_COLUMNS = ENTRIES // 16
CHUNKS = 4
CHUNK = COLUMNS // CHUNKS
SHARE = 5 * CHUNK // 8
HALF = CORNERS // 2
SPREAD = 2
SOLO = SPREAD
STREAM = SOLO + 1
CHAINED = LAST - 1
PLAIN = (SOLO, 0)
PRODUCTS = ("prod_c", "prod_a", "prod_b")
HELP = 2
FIRST_E = 4


def tile_attend_deform_kernel(tc, xT, w, part, offs, out):
    nc = tc.nc
    with ExitStack() as ctx:
        lists = ctx.enter_context(tc.tile_pool(name="lists", bufs=1))
        keep = ctx.enter_context(tc.tile_pool(name="keep", bufs=1))
        psum = ctx.enter_context(tc.psum_pool(name="banks", bufs=1))

        offsets = lists.tile([P, BATCHES * LIST_COLUMNS], U16, name="offsets")
        x_view = xT.rearrange("(s p u r) c -> s u p r c", s=PASSES, p=P, u=2, r=2)
        staged = {}
        tables = {}

        def staging_name(s, u, c):
            return f"staged{s}{u}{c}"

        def w_name(o, s):
            return f"w_raw{o}{s}"

        def load_window(s, u):
            span = 1 if s == 0 else 2
            tables[s, u] = keep.tile([P, COLUMNS], F32, name=f"table{s}{u}", align_bytes=64)
            for c in range(CHUNKS):
                if c % span == 0:
                    run = slice(c * CHUNK, (c + span) * CHUNK)
                    nc.sync.dma_start(tables[s, u][:, run], x_view[s, u, :, 1, run])
                staged[s, u, c] = keep.tile([P, CHUNK], F32, name=staging_name(s, u, c), align_bytes=64)
                nc.sync.dma_start(staged[s, u, c][:], x_view[s, u, :, 0, c * CHUNK : (c + 1) * CHUNK])

        def cast_chunk(s, u, c):
            halves = tables[s, u][:].bitcast(BF16).rearrange("p (c r) -> p c r", r=2)
            dst = halves[:, c * CHUNK : (c + 1) * CHUNK, 0]
            if (s, u, c) == (0, 0, CHUNKS - 1):
                nc.vector.tensor_copy(dst[:, :SHARE], staged[s, u, c][:, :SHARE])
                nc.scalar.activation(dst[:, SHARE:], staged[s, u, c][:, SHARE:], COPY)
            elif (s, u) == (0, 0) and c > 0:
                nc.vector.tensor_copy(dst, staged[s, u, c][:])
            else:
                nc.scalar.activation(dst, staged[s, u, c][:], COPY)

        load_window(0, 0)
        nc.sync.dma_start(offsets[:], offs)
        weights = keep.tile([P, BATCHES, CORNERS], F32, name="weights")
        part_view = part[0:1, :].rearrange("one (k g j) -> g (one k) j", g=P, j=CORNERS)
        nc.scalar.dma_start(weights[:, 0:1, :], part_view[:, 0:1, :])
        nc.sync.dma_start(weights[:, 1:SPREAD, :], part_view[:, 1:SPREAD, :])
        load_window(0, 1)
        nc.sync.dma_start(weights[:, SOLO:STREAM, :], part_view[:, SOLO:STREAM, :])
        load_window(1, 0)
        load_window(1, 1)
        w_raw = {}
        w_view = w.rearrange("o (s p t) m -> o p s t m", s=PASSES, t=4)
        for o in range(TAPS):
            if o == TAPS - 1:
                nc.sync.dma_start(weights[:, STREAM:, :], part_view[:, STREAM:, :])
            for s in range(PASSES):
                w_raw[o, s] = keep.tile([P, 4, CHANNELS], F32, name=w_name(o, s), align_bytes=64)
                nc.sync.dma_start(w_raw[o, s][:], w_view[o, :, s])

        identity = keep.tile([P, P], F32, name="identity")
        make_identity(nc, identity[:])

        words = {}
        word_names = {}

        def gather(i, u, name):
            word_names[i, u] = name
            s, k = divmod(i, BATCHES)
            words[i, u] = keep.tile([P, ENTRIES], U32, name=name, align_bytes=64)
            nc.vector.tensor_copy(
                words[i, u][:] if (i, u) == PLAIN else words[i, u][:].rearrange("p (q g h) -> p g q h", q=4, h=2),
                tables[s, u][:].bitcast(U32).indirect(offsets[:, k * LIST_COLUMNS : (k + 1) * LIST_COLUMNS]),
            )

        banks = [f"bank{n}" for n in range(8)]

        def take_bank(name=None):
            name = name or banks[0]
            banks.remove(name)
            banks.append(name)
            return name

        def hold_bank():
            name = banks[0]
            banks.remove(name)
            return name

        def add_turned(dst, src, start, stop):
            nc.tensor.matmul(dst, src, identity[:], start=start, stop=stop, is_transpose=True)

        e_tiles = {}

        def e_bf(lo, hi):
            first = lo < FIRST_E
            if first not in e_tiles:
                name, units = (w_name(0, 0), FIRST_E) if first else ("e_bf", UNITS - FIRST_E)
                e_tiles[first] = keep.tile([P, units, P, 4], BF16, name=name, align_bytes=64)
            base = 0 if first else FIRST_E
            return e_tiles[first][:, lo - base : hi - base, :, :]

        e_scales = keep.tile([P, UNITS, P], U8, name="e_scales", align_bytes=64)
        sum_banks = {}
        sums = {}

        def round_sum(i):
            nc.scalar.activation(e_bf(i, i + 1)[:, 0], sums[i][:].rearrange("p t g -> p g t"), COPY)
            banks.append(sum_banks[i])

        spread = {}
        products = {}
        backs = {}

        def spread_weights(i, name):
            spread[i] = keep.tile([P, CORNERS, P], F32, name=name, align_bytes=64)
            for half in range(2):
                bank = psum.tile([P, HALF, P], F32, name=take_bank())
                for jj in range(HALF):
                    j = HALF * half + jj
                    nc.tensor.transpose(bank[:, jj, :], weights[:, i, j : j + 1].to_broadcast([P, P]), identity[:])
                nc.scalar.copy(spread[i][:, HALF * half : HALF * (half + 1), :], bank[:])

        def weigh_gathered(i, u, r, name):
            values = words[i, u][:].bitcast(BF16).rearrange("p (q g h r) -> p r q h g", q=4, h=2, r=2)
            planes = keep.tile([P, CORNERS, P], F32, name=name, align_bytes=64)
            nc.gpsimd.tensor_tensor(
                planes[:].rearrange("p (q h) g -> p q h g", h=2),
                values[:, r],
                spread[i][:].rearrange("p (q h) g -> p q h g", h=2),
                MULT,
            )
            if i not in sums:
                sum_banks[i] = hold_bank()
                sums[i] = psum.tile([P, 2, 2, P], F32, name=sum_banks[i])
            for j in range(CORNERS):
                add_turned(sums[i][:, u, r, :], planes[:, j, :], j == 0, j == CORNERS - 1)

        def turn_back(i, rounded):
            backs[i] = psum.tile([P, 2, P], F32, name=sum_banks[i])
            pairs = rounded[:].rearrange("g u p r -> g u (p r)").bitcast(F32)
            for u in range(2):
                nc.tensor.transpose(backs[i][:, u, :], pairs[:, u, :], identity[:])

        def round_gathered(i, name):
            rounded = keep.tile([P, 2, P, 2], BF16, name=name, align_bytes=64)
            nc.scalar.activation(rounded[:], sums[i][:].rearrange("g u r p -> g u p r"), COPY)
            turn_back(i, rounded)

        def place(i):
            nc.scalar.copy(
                e_bf(i, i + 1)[:, 0].rearrange("p g t -> p (g t)").bitcast(F32).rearrange("p (g u) -> p g u", u=2),
                backs[i][:].rearrange("p u g -> p g u"),
            )
            banks.append(sum_banks[i])

        def lift(dst, i, u, j):
            order = "p (g q h) -> p q g h" if (i, u) == PLAIN else "p (q g h) -> p q g h"
            planes = words[i, u][:].bitcast(F32).rearrange(order, q=4, h=2)
            nc.tensor.transpose(dst, planes[:, j // 2, :, j % 2], identity[:])

        def weight(i, j):
            return weights[:, i % BATCHES, j : j + 1]

        def lift_corners(i, u, corners, bank_name):
            bank = psum.tile([P, len(corners), P], F32, name=bank_name)
            for jj, j in enumerate(corners):
                lift(bank[:, jj, :], i, u, j)
            return [(j, bank[:, jj, :].bitcast(BF16).rearrange("g (p r) -> g r p", r=2)) for jj, j in enumerate(corners)]

        def half_of(half):
            return range(HALF * half, HALF * (half + 1))

        def lift_pair(i, q):
            bank = psum.tile([P, 2, 2, P], F32, name=take_bank())
            for u in (1, 0):
                for h in range(2):
                    lift(bank[:, h, u, :], i, u, 2 * q + h)
            return [bank[:, h, :, :].bitcast(BF16).rearrange("g u (p r) -> g u r p", r=2) for h in range(2)]

        def weigh_and_add(dst, src, scale):
            nc.vector.scalar_tensor_tensor(dst, src, scale, dst, op0=MULT, op1=ADD)

        lifted = {}

        def lift_window(u):
            lifted[SOLO, u] = [pair for half in range(2) for pair in lift_corners(SOLO, u, half_of(half), take_bank())]

        def weigh_window(u, name):
            products[SOLO, u] = keep.tile([P, CORNERS, 2, P], F32, name=name, align_bytes=64)
            for j, src in lifted[SOLO, u]:
                nc.scalar.activation(products[SOLO, u][:, j, :, :], src, COPY, scale=weight(SOLO, j))

        def sum_window(u):
            if u == 0:
                sum_banks[SOLO] = hold_bank()
                sums[SOLO] = psum.tile([P, 4, P], F32, name=sum_banks[SOLO])
            for r in range(2):
                for j in range(CORNERS):
                    add_turned(sums[SOLO][:, 2 * u + r, :], products[SOLO, u][:, j, r, :], j == 0, j == CORNERS - 1)

        def lift_unit(i):
            lifted[i] = [lift_pair(i, q) for q in range(4)]

        def weigh(i):
            prod = keep.tile([P, CORNERS, 2, 2, P], F32, name=PRODUCTS[i % len(PRODUCTS)], align_bytes=64)
            for q in range(4):
                for h, src in enumerate(lifted[i][q] if i in lifted else lift_pair(i, q)):
                    nc.scalar.activation(prod[:, 2 * q + h, :, :, :], src, COPY, scale=weight(i, 2 * q + h))
                if q % 2 == 1:
                    onto = prod[:, 2 * q - 2 : 2 * q, :, :, :].rearrange("g j u r p -> g (j u r p)")
                    taken = prod[:, 2 * q : 2 * q + 2, :, :, :].rearrange("g j u r p -> g (j u r p)")
                    nc.gpsimd.tensor_tensor(onto, onto, taken, ADD)
            products[i] = prod

        def add_up(i, addends, first, last):
            if first:
                sum_banks[i] = hold_bank()
                sums[i] = psum.tile([P, 4, P], F32, name=sum_banks[i])
            steps = [(u, j, r) for u, j in addends for r in range(2)]
            for n, (u, j, r) in enumerate(steps):
                add_turned(
                    sums[i][:, 2 * u + r, :], products[i][:, j, u, r, :], first and n == 0, last and n == len(steps) - 1
                )
            if last:
                round_sum(i)

        def sum_half(i, half):
            add_up(i, [(u, HALF * half + h) for h in range(2) for u in range(2)], half == 0, half == 1)

        w_scales = keep.tile([P, TAPS, PASSES, CHANNELS], U8, name="w_scales", align_bytes=64)
        w_bf = keep.tile([P, TAPS, PASSES, CHANNELS, 4], BF16, name="w_bf", align_bytes=64)

        def round_w(o):
            for s in range(PASSES):
                src = w_raw[o, s][:].rearrange("p t m -> p m t")
                if PASSES * o + s < TAPS * PASSES // 2:
                    nc.scalar.activation(w_bf[:, o, s], src, COPY)
                else:
                    nc.gpsimd.tensor_scalar(w_bf[:, o, s], src, 1.0, 0.0, op0=MULT, op1=ADD)

        spread_weights(0, "spread")
        for c in range(CHUNKS):
            cast_chunk(0, 0, c)
        spread_weights(1, staging_name(0, 0, CHUNKS - 1))
        for c in range(CHUNKS):
            cast_chunk(0, 1, c)
        for i, u in ((0, 0), (SOLO, 0), (1, 0), (SOLO, 1), (0, 1), (1, 1)):
            gather(i, u, f"words{i}{u}")
        lift_window(0)
        for r in range(2):
            weigh_gathered(0, 0, r, f"first{r}")
        weigh_window(0, "solo")
        lift_window(1)
        for c in range(CHUNKS - 1):
            cast_chunk(1, 0, c)
        weigh_gathered(1, 0, 0, staging_name(0, 1, 3))
        sum_window(0)
        gather(STREAM, 0, staging_name(0, 1, 3))
        weigh_gathered(1, 0, 1, staging_name(1, 0, 0))
        weigh_window(1, staging_name(1, 0, 2))
        cast_chunk(1, 0, CHUNKS - 1)
        sum_window(1)
        weigh_gathered(0, 1, 0, staging_name(1, 0, 1))
        weigh_gathered(0, 1, 1, staging_name(1, 0, 3))
        for c in range(CHUNKS):
            cast_chunk(1, 1, c)
        gather(STREAM, 1, staging_name(1, 1, 0))
        lift_unit(STREAM)
        for r in range(2):
            weigh_gathered(1, 1, r, staging_name(1, 1, 1 + r))
        for o in range(TAPS):
            round_w(o)
        round_sum(SOLO)
        round_gathered(0, w_name(1, 0))
        freed = [staging_name(1, 1, 3), w_name(0, 1), w_name(1, 1), w_name(2, 0)]
        for u in range(2):
            gather(STREAM + 1, u, freed.pop(0))

        for i in range(STREAM, CHAINED):
            weigh(i)
            if i - STREAM < SPREAD:
                place(i - STREAM)
            if i == STREAM:
                round_gathered(1, w_name(1, 0))
            for u in range(2):
                gather(i + 2, u, freed.pop(0) if freed else word_names[i, u])
            if i - 2 >= STREAM:
                sum_half(i - 2, 1)
            if i - 1 >= STREAM:
                sum_half(i - 1, 0)

        chain = keep.tile([P, 2, 2, P], F32, name="chain", align_bytes=64)
        chain_rounded = keep.tile([P, 2, P, 2], BF16, name="chain_rounded", align_bytes=64)
        closing = keep.tile([P, CORNERS, 2, 2, P], F32, name=PRODUCTS[LAST % len(PRODUCTS)], align_bytes=64)
        products[LAST] = closing
        lift_unit(CHAINED)
        for q in range(4):
            for h, src in enumerate(lifted[CHAINED][q]):
                j = 2 * q + h
                for u in range(2):
                    if j == 0:
                        nc.vector.tensor_scalar(chain[:, u, :, :], src[:, u, :, :], weight(CHAINED, j), None, op0=MULT)
                    elif j < CORNERS - 1:
                        weigh_and_add(chain[:, u, :, :], src[:, u, :, :], weight(CHAINED, j))
                    else:
                        nc.vector.scalar_tensor_tensor(
                            chain_rounded[:, u, :, :],
                            src[:, u, :, :].rearrange("g r p -> g p r"),
                            weight(CHAINED, j),
                            chain[:, u, :, :].rearrange("g r p -> g p r"),
                            op0=MULT,
                            op1=ADD,
                        )

        def close(u, corners, bank_name):
            for j, src in lift_corners(LAST, u, corners, bank_name):
                nc.scalar.activation(closing[:, j, u, :, :], src, COPY, scale=weight(LAST, j))

        def close_halved(half):
            bank_name = take_bank()
            close(1, half_of(half), bank_name)
            onto = closing[:, HALF * half : HALF * half + 2, 1, :, :]
            nc.gpsimd.tensor_tensor(onto, onto, closing[:, HALF * half + 2 : HALF * half + 4, 1, :, :], ADD)
            return bank_name

        first_bank = close_halved(0)
        sum_half(CHAINED - 2, 1)
        close_halved(1)
        sum_half(CHAINED - 1, 0)
        close(0, half_of(0), take_bank(first_bank))
        close(0, range(HALF, CORNERS - HELP), take_bank(sum_banks[CHAINED - 2]))
        for j, src in lift_corners(LAST, 0, range(CORNERS - HELP, CORNERS), take_bank()):
            weigh_and_add(closing[:, j - CORNERS + HELP, 0, :, :], src, weight(LAST, j))
        sum_half(CHAINED - 1, 1)
        add_up(LAST, [(1, 0), (1, 1)] + [(0, j) for j in range(HELP, HALF)], True, False)
        sum_banks[CHAINED] = hold_bank()
        turn_back(CHAINED, chain_rounded)
        place(CHAINED)
        late = [(0, j) for j in range(HALF, CORNERS - HELP)] + [(1, HALF), (1, HALF + 1)] + [(0, j) for j in range(HELP)]
        add_up(LAST, late, False, True)

        w_codes = keep.tile([P, TAPS, PASSES, CHANNELS], U32, name=word_names[LAST, 0], align_bytes=64)

        def quantize_w(taps):
            nc.vector.quantize_mx(
                out=w_codes[:, taps, :, :].rearrange("p o s m -> p (o s m)").bitcast(FP8X4),
                scales=w_scales[:, taps, :, :].rearrange("p o s m -> p (o s m)"),
                in_=w_bf[:, taps, :, :, :].rearrange("p o s m t -> p (o s m t)"),
            )

        e_codes = keep.tile([P, UNITS, P], U32, name="chain_rounded", align_bytes=64)

        def quantize_e(lo, hi):
            nc.vector.quantize_mx(
                out=e_codes[:, lo:hi, :].rearrange("p n g -> p (n g)").bitcast(FP8X4),
                scales=e_scales[:, lo:hi, :].rearrange("p n g -> p (n g)"),
                in_=e_bf(lo, hi).rearrange("p n g t -> p (n g t)"),
            )

        accs = {}

        def multiply(i):
            s, k = divmod(i, BATCHES)
            o, b = divmod(k, 2)
            if i < 2:
                accs[b] = psum.tile([P, P], F32, name=hold_bank())
            nc.tensor.matmul_mx(
                out=accs[b][:],
                lhsT=w_codes[:, o, s, :].bitcast(FP8X4),
                lhsT_scale=w_scales[:, o, s, :],
                rhs=e_codes[:, i, :].bitcast(FP8X4),
                rhs_scale=e_scales[:, i, :],
                start=(i < 2),
                stop=(i >= UNITS - 2),
            )

        def store(b):
            result = keep.tile([P, P], F32, name=f"result{b}")
            if b == 0:
                nc.scalar.copy(result[:], accs[b][:])
            else:
                nc.vector.tensor_copy(result[:], accs[b][:])
            nc.sync.dma_start(out[:, b * P : (b + 1) * P], result[:])

        for lo, hi in ((0, FIRST_E), (FIRST_E, 2 * FIRST_E), (2 * FIRST_E, CHAINED), (CHAINED, LAST)):
            if lo < BATCHES:
                quantize_w(slice(lo // 2, min(hi // 2, TAPS)))
            quantize_e(lo, hi)
            for i in range(lo, hi):
                multiply(i)
        store(0)
        quantize_e(LAST, UNITS)
        multiply(LAST)
        store(1)
